import numpy as np
import ml_dtypes


def mxq(x, axis, fmt="e4m3"):
    dtype, down = {"e4m3": (ml_dtypes.float8_e4m3fn, 7), "e5m2": (ml_dtypes.float8_e5m2, 14)}[fmt]
    v = np.moveaxis(np.asarray(x, np.float32).astype(ml_dtypes.bfloat16).astype(np.float64), axis, -1)
    blocks = v.reshape(v.shape[:-1] + (-1, 32))
    amax = np.abs(blocks).max(-1, keepdims=True)
    byte = np.maximum(np.where(amax > 0, np.frexp(amax)[1] - 1 + 127, 0) - down, 1)
    scale = np.exp2(byte - 127.0)
    codes = (blocks / scale).astype(np.float32).astype(dtype).astype(np.float64)
    return np.moveaxis((codes * scale).reshape(v.shape), -1, axis)


WIDE = False


def mx_kscale(k):
    if not WIDE:
        return np.ones(k)
    levels = np.array([10, -10, 5, -5, 0])
    if k % 512:
        return np.exp2(np.random.permutation(np.resize(levels, k // 32))).repeat(32)
    a = np.empty((k // 512, 16))
    for p in range(k // 512):
        a[p, :8] = np.random.permutation(np.resize(levels, 8))
        for g in range(8):
            far = levels[np.abs(levels - a[p, g]) >= 10]
            a[p, g + 8] = far[np.random.randint(len(far))]
    return np.exp2(a.ravel()).repeat(32)


def f64(x):
    return np.asarray(x).astype(np.float64)


def striped(idx):
    return np.tile(idx.reshape(-1, 16).T, (8, 1)).astype(np.uint16)


def unstriped(offs):
    return offs[:16].T.reshape(-1).astype(np.int64)


E2M1 = np.array([0.0, 0.5, 1.0, 1.5, 2.0, 3.0, 4.0, 6.0, -0.0, -0.5, -1.0, -1.5, -2.0, -3.0, -4.0, -6.0])


def pack_weight(w, fmt):
    k, n = w.shape
    w = f64(np.asarray(w, np.float32).astype(ml_dtypes.bfloat16)).reshape(k // 32, 32, n)
    amax = np.abs(w).max(1)
    if fmt == "e4m3":
        byte = np.frexp(amax)[1] - 1 + 127 - 7
    else:
        mant, ex = np.frexp(amax / 6.0)
        byte = np.where(mant > 0.5, ex, ex - 1) + 127
    byte = np.clip(np.where(amax > 0, byte, 1), 1, 254)
    scaled = (w * np.exp2(127.0 - byte)[:, None, :]).reshape(k, n).astype(np.float32)
    by_word = np.ascontiguousarray(scaled.reshape(k // 512, 128, 4, n).transpose(0, 1, 3, 2))
    if fmt == "e4m3":
        words = by_word.astype(ml_dtypes.float8_e4m3fn).view(np.uint8)
    else:
        c = by_word.astype(ml_dtypes.float4_e2m1fn).view(np.uint8) & 0xF
        words = (c[..., 0::2] | (c[..., 1::2] << 4)).reshape(k // 512, 128, 2 * n)
    return np.ascontiguousarray(words), np.ascontiguousarray(byte.astype(np.uint8).reshape(k // 512, 16, n))


def unpack_weight(words, scales, fmt):
    g, _, n = scales.shape
    words = np.ascontiguousarray(words).reshape(g, 128, n, -1)
    if fmt == "e4m3":
        vals = words.view(ml_dtypes.float8_e4m3fn).astype(np.float64)
    else:
        nib = np.empty((g, 128, n, 4), np.uint8)
        nib[..., 0::2] = words & 0xF
        nib[..., 1::2] = words >> 4
        vals = E2M1[nib]
    vals = vals * np.repeat(np.exp2(scales.astype(np.float64) - 127.0), 8, axis=1)[..., None]
    return vals.transpose(0, 1, 3, 2).reshape(g * 512, n)


def relu(v):
    return np.maximum(v, 0.0)


K, T, E, B, H, N = 1024, 512, 6, 4, 512, 512


def setup_inputs():
    n = np.random.standard_normal
    s = mx_kscale(K)
    u = mx_kscale(H)
    slot_token = np.random.permutation(T)[:128 * B]
    block = np.sort(np.random.randint(E, size=B))
    x = pack_weight(n((K, T)) * s[:, None], "e4m3")
    wa = pack_weight(n((K, E * H)) / np.sqrt(K) / s[:, None] * np.tile(u, E), "e4m3")
    wb = pack_weight(n((H, E * N)) / np.sqrt(H) / u[:, None], "e4m3")
    return {
        "x_words": x[0],
        "x_scales": x[1],
        "w": (n((K, N)) / np.sqrt(K) / s[:, None]).astype(np.float32),
        "wa_words": wa[0],
        "wa_scales": wa[1],
        "wb_words": wb[0],
        "wb_scales": wb[1],
        "gate": (np.tile(np.random.uniform(0.2, 1.0, 128 * B), (128, 1))).astype(np.float32),
        "offs": striped(slot_token),
        "offs2": striped((block[:, None] * H + np.arange(H)).reshape(-1)),
        "offs3": striped((block[:, None] * N + np.arange(N)).reshape(-1)),
    }


def reference(x_words, x_scales, w, wa_words, wa_scales, wb_words, wb_scales, gate, offs, offs2, offs3):
    wq = mxq(f64(w), 0, "e4m3")
    idx, idx2, idx3 = unstriped(offs), unstriped(offs2), unstriped(offs3)
    x = unpack_weight(x_words, x_scales, "e4m3")
    out = wq.T @ x
    wa = unpack_weight(wa_words, wa_scales, "e4m3")[:, idx2]
    wb = unpack_weight(wb_words, wb_scales, "e4m3")[:, idx3]
    xq = x[:, idx]
    h = np.concatenate([wa[:, m * H:(m + 1) * H].T @ xq[:, 128 * m:128 * m + 128] for m in range(B)], axis=1)
    hq = mxq(relu(h), 0, "e4m3")
    y = np.concatenate([wb[:, m * N:(m + 1) * N].T @ hq[:, 128 * m:128 * m + 128] for m in range(B)], axis=1)
    out[:, idx] += f64(gate[:1]) * y
    return out

@@ -1,0 +1,211 @@
+from contextlib import ExitStack
+
+import concourse.mybir as mybir
+from concourse.masks import make_identity
+
+K, T, E, B, H, N = 1024, 512, 6, 4, 512, 512
+FLOPS = 2 * K * N * T + 2 * K * H * T + 2 * H * N * T
+
+F32 = mybir.dt.float32
+BF16 = mybir.dt.bfloat16
+I32 = mybir.dt.int32
+U32 = mybir.dt.uint32
+U16 = mybir.dt.uint16
+U8 = mybir.dt.uint8
+FP8X4 = mybir.dt.float8_e4m3fn_x4
+RELU = mybir.ActivationFunctionType.Relu
+MULT = mybir.AluOpType.mult
+ADD = mybir.AluOpType.add
+
+P = 128
+PASSES = K // 512
+SLOTS = 128
+HALVES = 2
+HALF_BLOCKS = B // HALVES
+HALF_SLOTS = HALF_BLOCKS * SLOTS
+TOKEN_WINDOW = 704
+CHUNKS = N // P
+
+
+def words_of(dram_pass):
+    return dram_pass.rearrange("p c d -> p (c d)").bitcast(I32)
+
+
+def load_scales(nc, tile, dram_scales, width):
+    passes = dram_scales.shape[0]
+    for q in range(4):
+        nc.sync.dma_start(
+            out=tile[32 * q : 32 * q + 4 * passes, 0:width].bitcast(I32),
+            in_=dram_scales[:, 4 * q : 4 * q + 4, :].bitcast(I32),
+        )
+
+
+def tile_moe_dyl_relu_kernel(
+    tc, x_words, x_scales, w, wa_words, wa_scales, wb_words, wb_scales, gate, offs, offs2, offs3, out
+):
+    nc = tc.nc
+    with ExitStack() as ctx:
+        lists = ctx.enter_context(tc.tile_pool(name="lists", bufs=1))
+        keep = ctx.enter_context(tc.tile_pool(name="keep", bufs=1))
+        base_psum = ctx.enter_context(tc.psum_pool(name="base_psum", bufs=1))
+        work_psum = ctx.enter_context(tc.psum_pool(name="work_psum", bufs=4))
+
+        token_list = lists.tile([P, T // 16], U16, name="token_list")
+        a_list = lists.tile([P, B * H // 16], U16, name="a_list")
+        b_list = lists.tile([P, B * N // 16], U16, name="b_list")
+
+        xw = [keep.tile([P, TOKEN_WINDOW], I32, name=f"xw{s}", align_bytes=64) for s in range(PASSES)]
+        xs = keep.tile([P, TOKEN_WINDOW], U8, name="xs", align_bytes=64)
+        aw = [keep.tile([P, E * H], I32, name=f"aw{s}", align_bytes=64) for s in range(PASSES)]
+        a_sc = keep.tile([P, E * H], U8, name="a_sc", align_bytes=64)
+        bw = keep.tile([P, E * N], I32, name="bw", align_bytes=64)
+        b_sc = keep.tile([P, E * N], U8, name="b_sc", align_bytes=64)
+        w_raw = [keep.tile([P, 4, N], F32, name=f"w_raw{s}") for s in range(PASSES)]
+        gate_sb = keep.tile([P, T], F32, name="gate_sb")
+        ident = keep.tile([P, P], F32, name="ident")
+
+        nc.vector.memset(xs[:].bitcast(I32), 0)
+        for s in range(PASSES):
+            nc.vector.memset(xw[s][:, T:TOKEN_WINDOW], 0)
+        nc.vector.memset(a_sc[:].bitcast(I32), 0)
+        nc.vector.memset(b_sc[:].bitcast(I32), 0)
+        make_identity(nc, ident[:])
+
+        nc.sync.dma_start(token_list[:], offs)
+        for s in range(PASSES):
+            nc.sync.dma_start(out=xw[s][:, 0:T], in_=words_of(x_words[s]))
+        load_scales(nc, xs, x_scales, T)
+        nc.sync.dma_start(out=aw[0][:], in_=words_of(wa_words[0]))
+        nc.sync.dma_start(a_list[:], offs2)
+        nc.sync.dma_start(out=aw[1][:], in_=words_of(wa_words[1]))
+        load_scales(nc, a_sc, wa_scales, E * H)
+        for s in range(PASSES):
+            nc.sync.dma_start(
+                out=w_raw[s][:], in_=w[512 * s : 512 * (s + 1), :].rearrange("(p j) n -> p j n", j=4)
+            )
+        nc.sync.dma_start(out=bw[:], in_=words_of(wb_words[0]))
+        nc.sync.dma_start(b_list[:], offs3)
+        load_scales(nc, b_sc, wb_scales, E * N)
+        nc.sync.dma_start(out=gate_sb[:], in_=gate)
+
+        xg = [keep.tile([P, T], U32, name=f"xg{s}", align_bytes=64) for s in range(PASSES)]
+        xg_sc = keep.tile([P, T], U8, name="xg_sc", align_bytes=64)
+        for s in range(PASSES):
+            nc.vector.tensor_copy(xg[s][:], xw[s][:].bitcast(U32).indirect(token_list[:]))
+        nc.vector.tensor_copy(xg_sc[:], xs[:].indirect(token_list[:]))
+
+        half_cols = HALF_BLOCKS * H
+        ag = [
+            [keep.tile([P, half_cols], U32, name=f"ag{s}_{hf}", align_bytes=64) for hf in range(HALVES)]
+            for s in range(PASSES)
+        ]
+        ag_sc = [keep.tile([P, half_cols], U8, name=f"ag_sc{hf}", align_bytes=64) for hf in range(HALVES)]
+        half_list = [slice(hf * half_cols // 16, (hf + 1) * half_cols // 16) for hf in range(HALVES)]
+        for s in range(PASSES):
+            for hf in range(HALVES):
+                nc.vector.tensor_copy(ag[s][hf][:], aw[s][:].bitcast(U32).indirect(a_list[:, half_list[hf]]))
+        for hf in range(HALVES):
+            nc.vector.tensor_copy(ag_sc[hf][:], a_sc[:].indirect(a_list[:, half_list[hf]]))
+
+        wq = [keep.tile([P, N], U32, name=f"wq{s}", align_bytes=64) for s in range(PASSES)]
+        wq_sc = [keep.tile([P, N], U8, name=f"wq_sc{s}", align_bytes=64) for s in range(PASSES)]
+        for s in range(PASSES):
+            w_bf = keep.tile([P, N, 4], BF16, name=f"w_bf{s}", align_bytes=64)
+            nc.scalar.copy(out=w_bf[:], in_=w_raw[s][:].rearrange("p j n -> p n j"))
+            nc.vector.quantize_mx(
+                out=wq[s][:].bitcast(FP8X4), scales=wq_sc[s][:], in_=w_bf[:].rearrange("p n j -> p (n j)")
+            )
+        base = [base_psum.tile([P, T], F32, name=f"base{c}") for c in range(CHUNKS)]
+        for c in range(CHUNKS):
+            cols = slice(c * P, (c + 1) * P)
+            for s in range(PASSES):
+                nc.tensor.matmul_mx(
+                    out=base[c][:],
+                    lhsT=wq[s][:, cols].bitcast(FP8X4),
+                    lhsT_scale=wq_sc[s][:, cols],
+                    rhs=xw[s][:, 0:T].bitcast(FP8X4),
+                    rhs_scale=xs[4 * s : P, 0:T],
+                    start=(s == 0),
+                    stop=(s == PASSES - 1),
+                )
+
+        h_words = []
+        for hf in range(HALVES):
+            h_sb = []
+            for b in range(HALF_BLOCKS):
+                slots = slice((hf * HALF_BLOCKS + b) * SLOTS, (hf * HALF_BLOCKS + b + 1) * SLOTS)
+                cols = slice(b * H, (b + 1) * H)
+                h_ps = work_psum.tile([P, H], F32, name="work")
+                for s in range(PASSES):
+                    nc.tensor.matmul_mx(
+                        out=h_ps[:],
+                        lhsT=xg[s][:, slots].bitcast(FP8X4),
+                        lhsT_scale=xg_sc[4 * s : P, slots],
+                        rhs=ag[s][hf][:, cols].bitcast(FP8X4),
+                        rhs_scale=ag_sc[hf][4 * s : P, cols],
+                        start=(s == 0),
+                        stop=(s == PASSES - 1),
+                    )
+                h_pairs = keep.tile([P, 2, P, 2], BF16, name=f"h_pairs{hf}_{b}", align_bytes=64)
+                nc.scalar.activation(
+                    out=h_pairs[:], in_=h_ps[:].rearrange("j (p u e) -> j u p e", u=2, e=2), func=RELU
+                )
+                h_sb.append(h_pairs)
+            turned = work_psum.tile([P, HALF_BLOCKS, 2, SLOTS], F32, name="work")
+            for b in range(HALF_BLOCKS):
+                pairs = h_sb[b][:].rearrange("j u p e -> j (u p e)").bitcast(F32)
+                for u in range(2):
+                    nc.tensor.transpose(turned[:, b, u, :], pairs[:, u * P : (u + 1) * P], ident[:])
+            h_in = keep.tile([P, HALF_BLOCKS, SLOTS, 2], F32, name=f"h_in{hf}", align_bytes=64)
+            nc.scalar.copy(out=h_in[:], in_=turned[:].rearrange("p b u j -> p b j u"))
+            h_words.append(h_in)
+
+        bg = [keep.tile([P, half_cols], U32, name=f"bg{hf}", align_bytes=64) for hf in range(HALVES)]
+        bg_sc = [keep.tile([P, half_cols], U8, name=f"bg_sc{hf}", align_bytes=64) for hf in range(HALVES)]
+        y_sb = []
+        for hf in range(HALVES):
+            nc.vector.tensor_copy(bg[hf][:], bw[:].bitcast(U32).indirect(b_list[:, half_list[hf]]))
+            nc.vector.tensor_copy(bg_sc[hf][:], b_sc[:].indirect(b_list[:, half_list[hf]]))
+            hq = keep.tile([P, HALF_SLOTS], U32, name=f"hq{hf}", align_bytes=64)
+            hq_sc = keep.tile([P, HALF_SLOTS], U8, name=f"hq_sc{hf}", align_bytes=64)
+            nc.vector.quantize_mx(
+                out=hq[:].bitcast(FP8X4),
+                scales=hq_sc[:],
+                in_=h_words[hf][:].rearrange("p b j u -> p (b j u)").bitcast(BF16),
+            )
+            y_half = []
+            for pair in range(CHUNKS // 2):
+                y_ps = work_psum.tile([P, 2, HALF_SLOTS], F32, name="work")
+                for cc in range(2):
+                    c = 2 * pair + cc
+                    for b in range(HALF_BLOCKS):
+                        cols = slice(b * N + c * P, b * N + (c + 1) * P)
+                        slots = slice(b * SLOTS, (b + 1) * SLOTS)
+                        nc.tensor.matmul_mx(
+                            out=y_ps[:, cc, slots],
+                            lhsT=bg[hf][:, cols].bitcast(FP8X4),
+                            lhsT_scale=bg_sc[hf][:, cols],
+                            rhs=hq[:, slots].bitcast(FP8X4),
+                            rhs_scale=hq_sc[:, slots],
+                            start=True,
+                            stop=True,
+                        )
+                y_pair = keep.tile([P, 2, HALF_SLOTS], F32, name=f"y{hf}_{pair}")
+                nc.scalar.copy(out=y_pair[:], in_=y_ps[:])
+                y_half.append(y_pair)
+            y_sb.append(y_half)
+
+        routed = [keep.tile([P, T], F32, name=f"routed{c}") for c in range(CHUNKS)]
+        for hf in range(HALVES):
+            tok = token_list[:, hf * HALF_SLOTS // 16 : (hf + 1) * HALF_SLOTS // 16]
+            for c in range(CHUNKS):
+                nc.vector.tensor_tensor(
+                    routed[c][:].indirect(tok),
+                    y_sb[hf][c // 2][:, c % 2, :],
+                    gate_sb[:, hf * HALF_SLOTS : (hf + 1) * HALF_SLOTS],
+                    MULT,
+                )
+                if hf == HALVES - 1:
+                    res = keep.tile([P, T], F32, name=f"res{c}")
+                    nc.vector.tensor_tensor(res[:], base[c][:], routed[c][:], ADD)
+                    nc.sync.dma_start(out=out[c * P : (c + 1) * P, :], in_=res[:])

@@ -47,8 +47,11 @@ def tile_moe_dyl_relu_kernel(
     with ExitStack() as ctx:
         lists = ctx.enter_context(tc.tile_pool(name="lists", bufs=1))
         keep = ctx.enter_context(tc.tile_pool(name="keep", bufs=1))
-        base_psum = ctx.enter_context(tc.psum_pool(name="base_psum", bufs=1))
-        work_psum = ctx.enter_context(tc.psum_pool(name="work_psum", bufs=4))
+        reused = ctx.enter_context(tc.tile_pool(name="reused", bufs=1))
+        psum = ctx.enter_context(tc.psum_pool(name="psum", bufs=1))
+
+        def bank(number, shape):
+            return psum.tile(shape, F32, name=f"bank{number}")
 
         token_list = lists.tile([P, T // 16], U16, name="token_list")
         a_list = lists.tile([P, B * H // 16], U16, name="a_list")
@@ -60,7 +63,9 @@ def tile_moe_dyl_relu_kernel(
         a_sc = keep.tile([P, E * H], U8, name="a_sc", align_bytes=64)
         bw = keep.tile([P, E * N], I32, name="bw", align_bytes=64)
         b_sc = keep.tile([P, E * N], U8, name="b_sc", align_bytes=64)
-        w_raw = [keep.tile([P, 4, N], F32, name=f"w_raw{s}") for s in range(PASSES)]
+        w_raw = [
+            reused.tile([P, 4, N], F32, name=f"w_raw{s}", align_bytes=64, offset=8192 * s) for s in range(PASSES)
+        ]
         gate_sb = keep.tile([P, T], F32, name="gate_sb")
         ident = keep.tile([P, P], F32, name="ident")
 
@@ -99,83 +104,118 @@ def tile_moe_dyl_relu_kernel(
             [keep.tile([P, half_cols], U32, name=f"ag{s}_{hf}", align_bytes=64) for hf in range(HALVES)]
             for s in range(PASSES)
         ]
-        ag_sc = [keep.tile([P, half_cols], U8, name=f"ag_sc{hf}", align_bytes=64) for hf in range(HALVES)]
         half_list = [slice(hf * half_cols // 16, (hf + 1) * half_cols // 16) for hf in range(HALVES)]
         for s in range(PASSES):
             for hf in range(HALVES):
                 nc.vector.tensor_copy(ag[s][hf][:], aw[s][:].bitcast(U32).indirect(a_list[:, half_list[hf]]))
-        for hf in range(HALVES):
-            nc.vector.tensor_copy(ag_sc[hf][:], a_sc[:].indirect(a_list[:, half_list[hf]]))
 
         wq = [keep.tile([P, N], U32, name=f"wq{s}", align_bytes=64) for s in range(PASSES)]
         wq_sc = [keep.tile([P, N], U8, name=f"wq_sc{s}", align_bytes=64) for s in range(PASSES)]
         for s in range(PASSES):
             w_bf = keep.tile([P, N, 4], BF16, name=f"w_bf{s}", align_bytes=64)
-            nc.scalar.copy(out=w_bf[:], in_=w_raw[s][:].rearrange("p j n -> p n j"))
+            nc.scalar.copy(
+                out=w_bf[:].rearrange("p (c i) j -> p c j i", i=4),
+                in_=w_raw[s][:].rearrange("p j (c i) -> p c j i", i=4),
+            )
             nc.vector.quantize_mx(
                 out=wq[s][:].bitcast(FP8X4), scales=wq_sc[s][:], in_=w_bf[:].rearrange("p n j -> p (n j)")
             )
-        base = [base_psum.tile([P, T], F32, name=f"base{c}") for c in range(CHUNKS)]
-        for c in range(CHUNKS):
-            cols = slice(c * P, (c + 1) * P)
-            for s in range(PASSES):
-                nc.tensor.matmul_mx(
-                    out=base[c][:],
-                    lhsT=wq[s][:, cols].bitcast(FP8X4),
-                    lhsT_scale=wq_sc[s][:, cols],
-                    rhs=xw[s][:, 0:T].bitcast(FP8X4),
-                    rhs_scale=xs[4 * s : P, 0:T],
-                    start=(s == 0),
-                    stop=(s == PASSES - 1),
-                )
 
-        h_words = []
+        ag_sc = []
         for hf in range(HALVES):
-            h_sb = []
-            for b in range(HALF_BLOCKS):
-                slots = slice((hf * HALF_BLOCKS + b) * SLOTS, (hf * HALF_BLOCKS + b + 1) * SLOTS)
-                cols = slice(b * H, (b + 1) * H)
-                h_ps = work_psum.tile([P, H], F32, name="work")
+            ag_sc.append(keep.tile([P, half_cols], U8, name=("ag_sc0", "w_bf1")[hf], align_bytes=64))
+            nc.vector.tensor_copy(ag_sc[hf][:], a_sc[:].indirect(a_list[:, half_list[hf]]))
+
+        last = CHUNKS - 1
+        turned_cols = last * P
+        base_t = []
+        for tb in range(T // P):
+            tokens = slice(tb * P, (tb + 1) * P)
+            base_ps = bank(4 + tb, [P, turned_cols])
+            for cols in (slice(0, 2 * P), slice(2 * P, turned_cols)):
                 for s in range(PASSES):
                     nc.tensor.matmul_mx(
-                        out=h_ps[:],
-                        lhsT=xg[s][:, slots].bitcast(FP8X4),
-                        lhsT_scale=xg_sc[4 * s : P, slots],
-                        rhs=ag[s][hf][:, cols].bitcast(FP8X4),
-                        rhs_scale=ag_sc[hf][4 * s : P, cols],
+                        out=base_ps[:, cols],
+                        lhsT=xw[s][:, tokens].bitcast(FP8X4),
+                        lhsT_scale=xs[4 * s : P, tokens],
+                        rhs=wq[s][:, cols].bitcast(FP8X4),
+                        rhs_scale=wq_sc[s][:, cols],
                         start=(s == 0),
                         stop=(s == PASSES - 1),
                     )
-                h_pairs = keep.tile([P, 2, P, 2], BF16, name=f"h_pairs{hf}_{b}", align_bytes=64)
-                nc.scalar.activation(
-                    out=h_pairs[:], in_=h_ps[:].rearrange("j (p u e) -> j u p e", u=2, e=2), func=RELU
-                )
-                h_sb.append(h_pairs)
-            turned = work_psum.tile([P, HALF_BLOCKS, 2, SLOTS], F32, name="work")
-            for b in range(HALF_BLOCKS):
-                pairs = h_sb[b][:].rearrange("j u p e -> j (u p e)").bitcast(F32)
-                for u in range(2):
-                    nc.tensor.transpose(turned[:, b, u, :], pairs[:, u * P : (u + 1) * P], ident[:])
-            h_in = keep.tile([P, HALF_BLOCKS, SLOTS, 2], F32, name=f"h_in{hf}", align_bytes=64)
-            nc.scalar.copy(out=h_in[:], in_=turned[:].rearrange("p b u j -> p b j u"))
-            h_words.append(h_in)
+            base_sb = reused.tile([P, turned_cols], F32, name=f"base_t{tb}", align_bytes=64, offset=16384 + 1536 * tb)
+            nc.scalar.copy(out=base_sb[:], in_=base_ps[:])
+            base_t.append(base_sb)
 
+        h_words = [
+            keep.tile([P, HALF_BLOCKS, SLOTS, 2], F32, name=f"h_in{hf}", align_bytes=64) for hf in range(HALVES)
+        ]
+        for m in range(B):
+            hf, b = divmod(m, HALF_BLOCKS)
+            slots = slice(m * SLOTS, (m + 1) * SLOTS)
+            cols = slice(b * H, (b + 1) * H)
+            h_ps = bank(m, [P, H])
+            for s in range(PASSES):
+                nc.tensor.matmul_mx(
+                    out=h_ps[:],
+                    lhsT=xg[s][:, slots].bitcast(FP8X4),
+                    lhsT_scale=xg_sc[4 * s : P, slots],
+                    rhs=ag[s][hf][:, cols].bitcast(FP8X4),
+                    rhs_scale=ag_sc[hf][4 * s : P, cols],
+                    start=(s == 0),
+                    stop=(s == PASSES - 1),
+                )
+            h_pairs = reused.tile([P, 2, P, 2], BF16, name=f"h_pairs{m}", align_bytes=64, offset=8192 + 1024 * m)
+            nc.scalar.activation(out=h_pairs[:], in_=h_ps[:].rearrange("j (p u e) -> j u p e", u=2, e=2), func=RELU)
+            turned = bank(4 + m, [P, 2, SLOTS])
+            pairs = h_pairs[:].rearrange("j u p e -> j (u p e)").bitcast(F32)
+            for u in range(2):
+                nc.tensor.transpose(turned[:, u, :], pairs[:, u * P : (u + 1) * P], ident[:])
+            nc.scalar.copy(out=h_words[hf][:, b], in_=turned[:].rearrange("p u j -> p j u"))
+
+        total = [bank(c, [P, T]) for c in range(CHUNKS)]
+        for c in range(last):
+            for tb in range(T // P):
+                nc.tensor.matmul(
+                    total[c][:, tb * P : (tb + 1) * P],
+                    lhsT=base_t[tb][:, c * P : (c + 1) * P],
+                    rhs=ident[:],
+                    is_transpose=True,
+                    start=(tb == 0),
+                    stop=False,
+                )
+        for s in range(PASSES):
+            nc.tensor.matmul_mx(
+                out=total[last][:],
+                lhsT=wq[s][:, turned_cols:N].bitcast(FP8X4),
+                lhsT_scale=wq_sc[s][:, turned_cols:N],
+                rhs=xw[s][:, 0:T].bitcast(FP8X4),
+                rhs_scale=xs[4 * s : P, 0:T],
+                start=(s == 0),
+                stop=(s == PASSES - 1),
+            )
+
+        bg_sc = []
         bg = [keep.tile([P, half_cols], U32, name=f"bg{hf}", align_bytes=64) for hf in range(HALVES)]
-        bg_sc = [keep.tile([P, half_cols], U8, name=f"bg_sc{hf}", align_bytes=64) for hf in range(HALVES)]
-        y_sb = []
+        hq = [keep.tile([P, HALF_SLOTS], U32, name=f"hq{hf}", align_bytes=64) for hf in range(HALVES)]
+        hq_sc = [keep.tile([P, HALF_SLOTS], U8, name=f"hq_sc{hf}", align_bytes=64) for hf in range(HALVES)]
         for hf in range(HALVES):
             nc.vector.tensor_copy(bg[hf][:], bw[:].bitcast(U32).indirect(b_list[:, half_list[hf]]))
-            nc.vector.tensor_copy(bg_sc[hf][:], b_sc[:].indirect(b_list[:, half_list[hf]]))
-            hq = keep.tile([P, HALF_SLOTS], U32, name=f"hq{hf}", align_bytes=64)
-            hq_sc = keep.tile([P, HALF_SLOTS], U8, name=f"hq_sc{hf}", align_bytes=64)
             nc.vector.quantize_mx(
-                out=hq[:].bitcast(FP8X4),
-                scales=hq_sc[:],
+                out=hq[hf][:].bitcast(FP8X4),
+                scales=hq_sc[hf][:],
                 in_=h_words[hf][:].rearrange("p b j u -> p (b j u)").bitcast(BF16),
             )
-            y_half = []
+            bg_sc.append(
+                reused.tile([P, half_cols], U8, name=f"bg_sc{hf}", align_bytes=64, offset=(0, 16384 + 1536 * 3)[hf])
+            )
+            nc.vector.tensor_copy(bg_sc[hf][:], b_sc[:].indirect(b_list[:, half_list[hf]]))
+
+        y_sb = keep.tile([P, CHUNKS, T], F32, name="y_sb")
+        for hf in range(HALVES):
+            half = slice(hf * HALF_SLOTS, (hf + 1) * HALF_SLOTS)
             for pair in range(CHUNKS // 2):
-                y_ps = work_psum.tile([P, 2, HALF_SLOTS], F32, name="work")
+                y_ps = bank(4 + 2 * hf + pair, [P, 2, HALF_SLOTS])
                 for cc in range(2):
                     c = 2 * pair + cc
                     for b in range(HALF_BLOCKS):
@@ -185,27 +225,43 @@ def tile_moe_dyl_relu_kernel(
                             out=y_ps[:, cc, slots],
                             lhsT=bg[hf][:, cols].bitcast(FP8X4),
                             lhsT_scale=bg_sc[hf][:, cols],
-                            rhs=hq[:, slots].bitcast(FP8X4),
-                            rhs_scale=hq_sc[:, slots],
+                            rhs=hq[hf][:, slots].bitcast(FP8X4),
+                            rhs_scale=hq_sc[hf][:, slots],
                             start=True,
                             stop=True,
                         )
-                y_pair = keep.tile([P, 2, HALF_SLOTS], F32, name=f"y{hf}_{pair}")
-                nc.scalar.copy(out=y_pair[:], in_=y_ps[:])
-                y_half.append(y_pair)
-            y_sb.append(y_half)
+                nc.scalar.copy(out=y_sb[:, 2 * pair : 2 * pair + 2, half], in_=y_ps[:])
 
-        routed = [keep.tile([P, T], F32, name=f"routed{c}") for c in range(CHUNKS)]
-        for hf in range(HALVES):
-            tok = token_list[:, hf * HALF_SLOTS // 16 : (hf + 1) * HALF_SLOTS // 16]
-            for c in range(CHUNKS):
-                nc.vector.tensor_tensor(
-                    routed[c][:].indirect(tok),
-                    y_sb[hf][c // 2][:, c % 2, :],
-                    gate_sb[:, hf * HALF_SLOTS : (hf + 1) * HALF_SLOTS],
-                    MULT,
-                )
-                if hf == HALVES - 1:
-                    res = keep.tile([P, T], F32, name=f"res{c}")
-                    nc.vector.tensor_tensor(res[:], base[c][:], routed[c][:], ADD)
-                    nc.sync.dma_start(out=out[c * P : (c + 1) * P, :], in_=res[:])
+        for c in range(CHUNKS):
+            routed = keep.tile([P, TOKEN_WINDOW], F32, name=f"routed{c}")
+            if c == 0:
+                for hf in range(HALVES):
+                    half = slice(hf * HALF_SLOTS, (hf + 1) * HALF_SLOTS)
+                    tok = token_list[:, hf * HALF_SLOTS // 16 : (hf + 1) * HALF_SLOTS // 16]
+                    nc.vector.tensor_tensor(routed[:].indirect(tok), y_sb[:, c, half], gate_sb[:, half], MULT)
+            else:
+                nc.vector.tensor_tensor(routed[:].indirect(token_list[:]), y_sb[:, c, :], gate_sb[:], MULT)
+            res = keep.tile([P, T], F32, name=f"res{c}")
+            rows = slice(c * P, (c + 1) * P)
+            if c == last:
+                for hf in range(2):
+                    half = slice(hf * T // 2, (hf + 1) * T // 2)
+                    nc.vector.tensor_tensor(res[:, half], total[c][:, half], routed[:, half], ADD)
+                    nc.sync.dma_start(out=out[rows, half], in_=res[:, half])
+            else:
+                routed_ps = bank(4, [P, T // P, P])
+                for tb in range(T // P):
+                    nc.tensor.transpose(routed_ps[:, tb, :], routed[:, tb * P : (tb + 1) * P], ident[:])
+                routed_t = keep.tile([P, T // P, P], F32, name=f"routed_t{c}")
+                nc.scalar.copy(out=routed_t[:], in_=routed_ps[:])
+                for tb in range(T // P):
+                    nc.tensor.matmul(
+                        total[c][:, tb * P : (tb + 1) * P],
+                        lhsT=routed_t[:, tb, :],
+                        rhs=ident[:],
+                        is_transpose=True,
+                        start=False,
+                        stop=(tb == T // P - 1),
+                    )
+                nc.scalar.copy(out=res[:], in_=total[c][:])
+                nc.scalar.dma_start(out=out[rows, :], in_=res[:])

@@ -47,7 +47,6 @@ def tile_moe_dyl_relu_kernel(
     with ExitStack() as ctx:
         lists = ctx.enter_context(tc.tile_pool(name="lists", bufs=1))
         keep = ctx.enter_context(tc.tile_pool(name="keep", bufs=1))
-        reused = ctx.enter_context(tc.tile_pool(name="reused", bufs=1))
         psum = ctx.enter_context(tc.psum_pool(name="psum", bufs=1))
 
         def bank(number, shape):
@@ -63,51 +62,45 @@ def tile_moe_dyl_relu_kernel(
         a_sc = keep.tile([P, E * H], U8, name="a_sc", align_bytes=64)
         bw = keep.tile([P, E * N], I32, name="bw", align_bytes=64)
         b_sc = keep.tile([P, E * N], U8, name="b_sc", align_bytes=64)
-        w_raw = [
-            reused.tile([P, 4, N], F32, name=f"w_raw{s}", align_bytes=64, offset=8192 * s) for s in range(PASSES)
-        ]
+        w_raw = [keep.tile([P, 4, N], F32, name=f"w_raw{s}") for s in range(PASSES)]
         gate_sb = keep.tile([P, T], F32, name="gate_sb")
         ident = keep.tile([P, P], F32, name="ident")
 
+        nc.vector.memset(b_sc[:].bitcast(I32), 0)
         nc.vector.memset(xs[:].bitcast(I32), 0)
         for s in range(PASSES):
             nc.vector.memset(xw[s][:, T:TOKEN_WINDOW], 0)
         nc.vector.memset(a_sc[:].bitcast(I32), 0)
-        nc.vector.memset(b_sc[:].bitcast(I32), 0)
         make_identity(nc, ident[:])
 
+        def load_w(s):
+            nc.sync.dma_start(out=w_raw[s][:], in_=w[512 * s : 512 * (s + 1), :].rearrange("(p j) n -> p j n", j=4))
+
         nc.sync.dma_start(token_list[:], offs)
-        for s in range(PASSES):
-            nc.sync.dma_start(out=xw[s][:, 0:T], in_=words_of(x_words[s]))
-        load_scales(nc, xs, x_scales, T)
-        nc.sync.dma_start(out=aw[0][:], in_=words_of(wa_words[0]))
-        nc.sync.dma_start(a_list[:], offs2)
-        nc.sync.dma_start(out=aw[1][:], in_=words_of(wa_words[1]))
-        load_scales(nc, a_sc, wa_scales, E * H)
-        for s in range(PASSES):
-            nc.sync.dma_start(
-                out=w_raw[s][:], in_=w[512 * s : 512 * (s + 1), :].rearrange("(p j) n -> p j n", j=4)
-            )
-        nc.sync.dma_start(out=bw[:], in_=words_of(wb_words[0]))
+        nc.sync.dma_start(out=xw[0][:, 0:T], in_=words_of(x_words[0]))
         nc.sync.dma_start(b_list[:], offs3)
         load_scales(nc, b_sc, wb_scales, E * N)
+        nc.sync.dma_start(out=xw[1][:, 0:T], in_=words_of(x_words[1]))
+        load_w(0)
+        load_scales(nc, xs, x_scales, T)
+        load_w(1)
+        nc.sync.dma_start(a_list[:], offs2)
+        load_scales(nc, a_sc, wa_scales, E * H)
+        for s in range(PASSES):
+            nc.sync.dma_start(out=aw[s][:], in_=words_of(wa_words[s]))
+        nc.sync.dma_start(out=bw[:], in_=words_of(wb_words[0]))
         nc.sync.dma_start(out=gate_sb[:], in_=gate)
 
         xg = [keep.tile([P, T], U32, name=f"xg{s}", align_bytes=64) for s in range(PASSES)]
         xg_sc = keep.tile([P, T], U8, name="xg_sc", align_bytes=64)
-        for s in range(PASSES):
-            nc.vector.tensor_copy(xg[s][:], xw[s][:].bitcast(U32).indirect(token_list[:]))
-        nc.vector.tensor_copy(xg_sc[:], xs[:].indirect(token_list[:]))
-
         half_cols = HALF_BLOCKS * H
-        ag = [
-            [keep.tile([P, half_cols], U32, name=f"ag{s}_{hf}", align_bytes=64) for hf in range(HALVES)]
-            for s in range(PASSES)
-        ]
         half_list = [slice(hf * half_cols // 16, (hf + 1) * half_cols // 16) for hf in range(HALVES)]
-        for s in range(PASSES):
-            for hf in range(HALVES):
-                nc.vector.tensor_copy(ag[s][hf][:], aw[s][:].bitcast(U32).indirect(a_list[:, half_list[hf]]))
+        bg_sc = [keep.tile([P, half_cols], U8, name=f"bg_sc{hf}", align_bytes=64) for hf in range(HALVES)]
+        nc.vector.tensor_copy(xg[0][:], xw[0][:].bitcast(U32).indirect(token_list[:]))
+        for hf in range(HALVES):
+            nc.vector.tensor_copy(bg_sc[hf][:], b_sc[:].indirect(b_list[:, half_list[hf]]))
+        nc.vector.tensor_copy(xg[1][:], xw[1][:].bitcast(U32).indirect(token_list[:]))
+        nc.vector.tensor_copy(xg_sc[:], xs[:].indirect(token_list[:]))
 
         wq = [keep.tile([P, N], U32, name=f"wq{s}", align_bytes=64) for s in range(PASSES)]
         wq_sc = [keep.tile([P, N], U8, name=f"wq_sc{s}", align_bytes=64) for s in range(PASSES)]
@@ -121,10 +114,20 @@ def tile_moe_dyl_relu_kernel(
                 out=wq[s][:].bitcast(FP8X4), scales=wq_sc[s][:], in_=w_bf[:].rearrange("p n j -> p (n j)")
             )
 
-        ag_sc = []
+        ag_sc = [keep.tile([P, half_cols], U8, name=f"ag_sc{hf}", align_bytes=64) for hf in range(HALVES)]
         for hf in range(HALVES):
-            ag_sc.append(keep.tile([P, half_cols], U8, name=("ag_sc0", "w_bf1")[hf], align_bytes=64))
             nc.vector.tensor_copy(ag_sc[hf][:], a_sc[:].indirect(a_list[:, half_list[hf]]))
+        ag = {}
+        for s, hf in ((0, 0), (1, 0), (1, 1)):
+            ag[s, hf] = keep.tile([P, half_cols], U32, name=f"ag{s}_{hf}", align_bytes=64)
+            nc.vector.tensor_copy(ag[s, hf][:], aw[s][:].bitcast(U32).indirect(a_list[:, half_list[hf]]))
+        ag[0, 1] = keep.tile([P, half_cols], U32, name="aw1", align_bytes=64)
+        for b in range(HALF_BLOCKS):
+            m = HALF_BLOCKS + b
+            nc.vector.tensor_copy(
+                ag[0, 1][:, b * H : (b + 1) * H],
+                aw[0][:].bitcast(U32).indirect(a_list[:, m * H // 16 : (m + 1) * H // 16]),
+            )
 
         last = CHUNKS - 1
         turned_cols = last * P
@@ -143,35 +146,9 @@ def tile_moe_dyl_relu_kernel(
                         start=(s == 0),
                         stop=(s == PASSES - 1),
                     )
-            base_sb = reused.tile([P, turned_cols], F32, name=f"base_t{tb}", align_bytes=64, offset=16384 + 1536 * tb)
+            base_sb = keep.tile([P, turned_cols], F32, name=f"base_t{tb}")
             nc.scalar.copy(out=base_sb[:], in_=base_ps[:])
             base_t.append(base_sb)
-
-        h_words = [
-            keep.tile([P, HALF_BLOCKS, SLOTS, 2], F32, name=f"h_in{hf}", align_bytes=64) for hf in range(HALVES)
-        ]
-        for m in range(B):
-            hf, b = divmod(m, HALF_BLOCKS)
-            slots = slice(m * SLOTS, (m + 1) * SLOTS)
-            cols = slice(b * H, (b + 1) * H)
-            h_ps = bank(m, [P, H])
-            for s in range(PASSES):
-                nc.tensor.matmul_mx(
-                    out=h_ps[:],
-                    lhsT=xg[s][:, slots].bitcast(FP8X4),
-                    lhsT_scale=xg_sc[4 * s : P, slots],
-                    rhs=ag[s][hf][:, cols].bitcast(FP8X4),
-                    rhs_scale=ag_sc[hf][4 * s : P, cols],
-                    start=(s == 0),
-                    stop=(s == PASSES - 1),
-                )
-            h_pairs = reused.tile([P, 2, P, 2], BF16, name=f"h_pairs{m}", align_bytes=64, offset=8192 + 1024 * m)
-            nc.scalar.activation(out=h_pairs[:], in_=h_ps[:].rearrange("j (p u e) -> j u p e", u=2, e=2), func=RELU)
-            turned = bank(4 + m, [P, 2, SLOTS])
-            pairs = h_pairs[:].rearrange("j u p e -> j (u p e)").bitcast(F32)
-            for u in range(2):
-                nc.tensor.transpose(turned[:, u, :], pairs[:, u * P : (u + 1) * P], ident[:])
-            nc.scalar.copy(out=h_words[hf][:, b], in_=turned[:].rearrange("p u j -> p j u"))
 
         total = [bank(c, [P, T]) for c in range(CHUNKS)]
         for c in range(last):
@@ -195,21 +172,44 @@ def tile_moe_dyl_relu_kernel(
                 stop=(s == PASSES - 1),
             )
 
-        bg_sc = []
-        bg = [keep.tile([P, half_cols], U32, name=f"bg{hf}", align_bytes=64) for hf in range(HALVES)]
+        h_words = [
+            keep.tile([P, HALF_BLOCKS, SLOTS, 2], F32, name=f"h_in{hf}", align_bytes=64) for hf in range(HALVES)
+        ]
+        for m in range(B):
+            hf, b = divmod(m, HALF_BLOCKS)
+            slots = slice(m * SLOTS, (m + 1) * SLOTS)
+            cols = slice(b * H, (b + 1) * H)
+            h_ps = bank(4 + m, [P, H])
+            order = (0, 1) if hf == 0 else (1, 0)
+            for s in order:
+                nc.tensor.matmul_mx(
+                    out=h_ps[:],
+                    lhsT=xg[s][:, slots].bitcast(FP8X4),
+                    lhsT_scale=xg_sc[4 * s : P, slots],
+                    rhs=ag[s, hf][:, cols].bitcast(FP8X4),
+                    rhs_scale=ag_sc[hf][4 * s : P, cols],
+                    start=(s == order[0]),
+                    stop=(s == order[-1]),
+                )
+            h_pairs = keep.tile([P, 2, P, 2], BF16, name=f"h_pairs{m}", align_bytes=64)
+            nc.scalar.activation(out=h_pairs[:], in_=h_ps[:].rearrange("j (p u e) -> j u p e", u=2, e=2), func=RELU)
+            turned = bank(4 + m, [P, 2, SLOTS])
+            pairs = h_pairs[:].rearrange("j u p e -> j (u p e)").bitcast(F32)
+            for u in range(2):
+                nc.tensor.transpose(turned[:, u, :], pairs[:, u * P : (u + 1) * P], ident[:])
+            nc.scalar.copy(out=h_words[hf][:, b], in_=turned[:].rearrange("p u j -> p j u"))
+
         hq = [keep.tile([P, HALF_SLOTS], U32, name=f"hq{hf}", align_bytes=64) for hf in range(HALVES)]
         hq_sc = [keep.tile([P, HALF_SLOTS], U8, name=f"hq_sc{hf}", align_bytes=64) for hf in range(HALVES)]
+        bg = []
         for hf in range(HALVES):
+            bg.append(keep.tile([P, half_cols], U32, name=("bg0", "h_in0")[hf], align_bytes=64))
             nc.vector.tensor_copy(bg[hf][:], bw[:].bitcast(U32).indirect(b_list[:, half_list[hf]]))
             nc.vector.quantize_mx(
                 out=hq[hf][:].bitcast(FP8X4),
                 scales=hq_sc[hf][:],
                 in_=h_words[hf][:].rearrange("p b j u -> p (b j u)").bitcast(BF16),
             )
-            bg_sc.append(
-                reused.tile([P, half_cols], U8, name=f"bg_sc{hf}", align_bytes=64, offset=(0, 16384 + 1536 * 3)[hf])
-            )
-            nc.vector.tensor_copy(bg_sc[hf][:], b_sc[:].indirect(b_list[:, half_list[hf]]))
 
         y_sb = keep.tile([P, CHUNKS, T], F32, name="y_sb")
         for hf in range(HALVES):
@@ -233,7 +233,7 @@ def tile_moe_dyl_relu_kernel(
                 nc.scalar.copy(out=y_sb[:, 2 * pair : 2 * pair + 2, half], in_=y_ps[:])
 
         for c in range(CHUNKS):
-            routed = keep.tile([P, TOKEN_WINDOW], F32, name=f"routed{c}")
+            routed = keep.tile([P, TOKEN_WINDOW], F32, name="h_in1" if c == 0 else f"routed{c}", align_bytes=64)
             if c == 0:
                 for hf in range(HALVES):
                     half = slice(hf * HALF_SLOTS, (hf + 1) * HALF_SLOTS)

@@ -14,7 +14,7 @@ U16 = mybir.dt.uint16
 U8 = mybir.dt.uint8
 FP8X4 = mybir.dt.float8_e4m3fn_x4
 RELU = mybir.ActivationFunctionType.Relu
-MULT = mybir.AluOpType.mult
+COPY = mybir.ActivationFunctionType.Copy
 ADD = mybir.AluOpType.add
 
 P = 128
@@ -25,6 +25,7 @@ HALF_BLOCKS = B // HALVES
 HALF_SLOTS = HALF_BLOCKS * SLOTS
 TOKEN_WINDOW = 704
 CHUNKS = N // P
+HALF_N = N // 2
 
 
 def words_of(dram_pass):
@@ -52,216 +53,194 @@ def tile_moe_dyl_relu_kernel(
         def bank(number, shape):
             return psum.tile(shape, F32, name=f"bank{number}")
 
+        def sbuf(name, shape, dtype):
+            return keep.tile(shape, dtype, name=name, align_bytes=64)
+
         token_list = lists.tile([P, T // 16], U16, name="token_list")
         a_list = lists.tile([P, B * H // 16], U16, name="a_list")
         b_list = lists.tile([P, B * N // 16], U16, name="b_list")
 
-        xw = [keep.tile([P, TOKEN_WINDOW], I32, name=f"xw{s}", align_bytes=64) for s in range(PASSES)]
-        xs = keep.tile([P, TOKEN_WINDOW], U8, name="xs", align_bytes=64)
-        aw = [keep.tile([P, E * H], I32, name=f"aw{s}", align_bytes=64) for s in range(PASSES)]
-        a_sc = keep.tile([P, E * H], U8, name="a_sc", align_bytes=64)
-        bw = keep.tile([P, E * N], I32, name="bw", align_bytes=64)
-        b_sc = keep.tile([P, E * N], U8, name="b_sc", align_bytes=64)
-        w_raw = [keep.tile([P, 4, N], F32, name=f"w_raw{s}") for s in range(PASSES)]
-        gate_sb = keep.tile([P, T], F32, name="gate_sb")
-        ident = keep.tile([P, P], F32, name="ident")
+        xw = [sbuf(f"xw{s}", [P, TOKEN_WINDOW], I32) for s in range(PASSES)]
+        xs = sbuf("xs", [P, TOKEN_WINDOW], U8)
+        aw = [sbuf(f"aw{s}", [P, E * H], I32) for s in range(PASSES)]
+        a_sc = sbuf("a_sc", [P, E * H], U8)
+        bw = sbuf("bw", [P, E * N], I32)
+        b_sc = sbuf("b_sc", [P, E * N], U8)
+        w_raw = [sbuf(f"w_raw{part}", [P, PASSES, 4, HALF_N], F32) for part in range(2)]
+        gate_rows = sbuf("gate_rows", [P, SLOTS], F32)
+        ident = sbuf("ident", [P, P], F32)
 
-        nc.vector.memset(b_sc[:].bitcast(I32), 0)
-        nc.vector.memset(xs[:].bitcast(I32), 0)
+        nc.gpsimd.memset(xs[:].bitcast(I32), 0)
+        nc.gpsimd.memset(b_sc[:].bitcast(I32), 0)
         for s in range(PASSES):
             nc.vector.memset(xw[s][:, T:TOKEN_WINDOW], 0)
         nc.vector.memset(a_sc[:].bitcast(I32), 0)
+        nc.gpsimd.memset(gate_rows[:], 0.0)
         make_identity(nc, ident[:])
 
-        def load_w(s):
-            nc.sync.dma_start(out=w_raw[s][:], in_=w[512 * s : 512 * (s + 1), :].rearrange("(p j) n -> p j n", j=4))
+        def load_w(part, s):
+            rows = w[512 * s : 512 * (s + 1), part * HALF_N : (part + 1) * HALF_N]
+            nc.sync.dma_start(out=w_raw[part][:, s], in_=rows.rearrange("(p j) n -> p j n", j=4))
 
         nc.sync.dma_start(token_list[:], offs)
         nc.sync.dma_start(out=xw[0][:, 0:T], in_=words_of(x_words[0]))
-        nc.sync.dma_start(b_list[:], offs3)
-        load_scales(nc, b_sc, wb_scales, E * N)
         nc.sync.dma_start(out=xw[1][:, 0:T], in_=words_of(x_words[1]))
-        load_w(0)
         load_scales(nc, xs, x_scales, T)
-        load_w(1)
+        nc.sync.dma_start(b_list[:], offs3)
+        load_w(0, 0)
+        load_scales(nc, b_sc, wb_scales, E * N)
+        load_w(0, 1)
         nc.sync.dma_start(a_list[:], offs2)
         load_scales(nc, a_sc, wa_scales, E * H)
-        for s in range(PASSES):
-            nc.sync.dma_start(out=aw[s][:], in_=words_of(wa_words[s]))
+        nc.sync.dma_start(out=aw[0][:], in_=words_of(wa_words[0]))
+        nc.sync.dma_start(out=gate_rows[0:B, :], in_=gate[0].rearrange("(m j) -> m j", m=B))
+        nc.sync.dma_start(out=aw[1][:], in_=words_of(wa_words[1]))
         nc.sync.dma_start(out=bw[:], in_=words_of(wb_words[0]))
-        nc.sync.dma_start(out=gate_sb[:], in_=gate)
+        for s in range(PASSES):
+            load_w(1, s)
 
-        xg = [keep.tile([P, T], U32, name=f"xg{s}", align_bytes=64) for s in range(PASSES)]
-        xg_sc = keep.tile([P, T], U8, name="xg_sc", align_bytes=64)
         half_cols = HALF_BLOCKS * H
         half_list = [slice(hf * half_cols // 16, (hf + 1) * half_cols // 16) for hf in range(HALVES)]
-        bg_sc = [keep.tile([P, half_cols], U8, name=f"bg_sc{hf}", align_bytes=64) for hf in range(HALVES)]
-        nc.vector.tensor_copy(xg[0][:], xw[0][:].bitcast(U32).indirect(token_list[:]))
+        block_list = [slice(m * H // 16, (m + 1) * H // 16) for m in range(B)]
+
+        xg = [sbuf(f"xg{s}", [P, T], U32) for s in range(PASSES)]
+        for s in range(PASSES):
+            nc.vector.tensor_copy(xg[s][:], xw[s][:].bitcast(U32).indirect(token_list[:]))
+        xg_sc = sbuf("xg_sc", [P, T], U8)
+        nc.vector.tensor_copy(xg_sc[:], xs[:].indirect(token_list[:]))
+        bg_sc = [sbuf(f"bg_sc{hf}", [P, half_cols], U8) for hf in range(HALVES)]
         for hf in range(HALVES):
             nc.vector.tensor_copy(bg_sc[hf][:], b_sc[:].indirect(b_list[:, half_list[hf]]))
-        nc.vector.tensor_copy(xg[1][:], xw[1][:].bitcast(U32).indirect(token_list[:]))
-        nc.vector.tensor_copy(xg_sc[:], xs[:].indirect(token_list[:]))
-
-        wq = [keep.tile([P, N], U32, name=f"wq{s}", align_bytes=64) for s in range(PASSES)]
-        wq_sc = [keep.tile([P, N], U8, name=f"wq_sc{s}", align_bytes=64) for s in range(PASSES)]
-        for s in range(PASSES):
-            w_bf = keep.tile([P, N, 4], BF16, name=f"w_bf{s}", align_bytes=64)
-            nc.scalar.copy(
-                out=w_bf[:].rearrange("p (c i) j -> p c j i", i=4),
-                in_=w_raw[s][:].rearrange("p j (c i) -> p c j i", i=4),
-            )
-            nc.vector.quantize_mx(
-                out=wq[s][:].bitcast(FP8X4), scales=wq_sc[s][:], in_=w_bf[:].rearrange("p n j -> p (n j)")
-            )
-
-        ag_sc = [keep.tile([P, half_cols], U8, name=f"ag_sc{hf}", align_bytes=64) for hf in range(HALVES)]
+        ag_sc = [sbuf(f"ag_sc{hf}", [P, half_cols], U8) for hf in range(HALVES)]
         for hf in range(HALVES):
             nc.vector.tensor_copy(ag_sc[hf][:], a_sc[:].indirect(a_list[:, half_list[hf]]))
-        ag = {}
-        for s, hf in ((0, 0), (1, 0), (1, 1)):
-            ag[s, hf] = keep.tile([P, half_cols], U32, name=f"ag{s}_{hf}", align_bytes=64)
-            nc.vector.tensor_copy(ag[s, hf][:], aw[s][:].bitcast(U32).indirect(a_list[:, half_list[hf]]))
-        ag[0, 1] = keep.tile([P, half_cols], U32, name="aw1", align_bytes=64)
-        for b in range(HALF_BLOCKS):
-            m = HALF_BLOCKS + b
-            nc.vector.tensor_copy(
-                ag[0, 1][:, b * H : (b + 1) * H],
-                aw[0][:].bitcast(U32).indirect(a_list[:, m * H // 16 : (m + 1) * H // 16]),
+
+        def quantise_w(c, buffer_name):
+            part, first = divmod(c * P, HALF_N)
+            w_bf = sbuf(buffer_name, [P, PASSES, P, 4], BF16)
+            nc.scalar.copy(
+                out=w_bf[:].rearrange("p s (c i) j -> p s c j i", i=4),
+                in_=w_raw[part][:, :, :, first : first + P].rearrange("p s j (c i) -> p s c j i", i=4),
             )
+            wq = sbuf(f"wq{c}", [P, PASSES * P], U32)
+            wq_sc = sbuf(f"wq_sc{c}", [P, PASSES * P], U8)
+            nc.vector.quantize_mx(out=wq[:].bitcast(FP8X4), scales=wq_sc[:], in_=w_bf[:].rearrange("p s n j -> p (s n j)"))
+            return wq, wq_sc
 
-        last = CHUNKS - 1
-        turned_cols = last * P
-        base_t = []
-        for tb in range(T // P):
-            tokens = slice(tb * P, (tb + 1) * P)
-            base_ps = bank(4 + tb, [P, turned_cols])
-            for cols in (slice(0, 2 * P), slice(2 * P, turned_cols)):
-                for s in range(PASSES):
-                    nc.tensor.matmul_mx(
-                        out=base_ps[:, cols],
-                        lhsT=xw[s][:, tokens].bitcast(FP8X4),
-                        lhsT_scale=xs[4 * s : P, tokens],
-                        rhs=wq[s][:, cols].bitcast(FP8X4),
-                        rhs_scale=wq_sc[s][:, cols],
-                        start=(s == 0),
-                        stop=(s == PASSES - 1),
-                    )
-            base_sb = keep.tile([P, turned_cols], F32, name=f"base_t{tb}")
-            nc.scalar.copy(out=base_sb[:], in_=base_ps[:])
-            base_t.append(base_sb)
-
-        total = [bank(c, [P, T]) for c in range(CHUNKS)]
-        for c in range(last):
-            for tb in range(T // P):
-                nc.tensor.matmul(
-                    total[c][:, tb * P : (tb + 1) * P],
-                    lhsT=base_t[tb][:, c * P : (c + 1) * P],
-                    rhs=ident[:],
-                    is_transpose=True,
-                    start=(tb == 0),
-                    stop=False,
+        def frozen_layer(c, wq, wq_sc, bank_number):
+            base_ps = bank(bank_number, [P, T])
+            for s in range(PASSES):
+                nc.tensor.matmul_mx(
+                    out=base_ps[:],
+                    lhsT=wq[:, s * P : (s + 1) * P].bitcast(FP8X4),
+                    lhsT_scale=wq_sc[:, s * P : (s + 1) * P],
+                    rhs=xg[s][:].bitcast(FP8X4),
+                    rhs_scale=xg_sc[4 * s : P, :],
+                    start=(s == 0),
+                    stop=(s == PASSES - 1),
                 )
-        for s in range(PASSES):
-            nc.tensor.matmul_mx(
-                out=total[last][:],
-                lhsT=wq[s][:, turned_cols:N].bitcast(FP8X4),
-                lhsT_scale=wq_sc[s][:, turned_cols:N],
-                rhs=xw[s][:, 0:T].bitcast(FP8X4),
-                rhs_scale=xs[4 * s : P, 0:T],
-                start=(s == 0),
-                stop=(s == PASSES - 1),
-            )
+            base_sb = sbuf(f"base{c}", [P, T], F32)
+            nc.scalar.copy(out=base_sb[:], in_=base_ps[:])
+            return base_sb
 
-        h_words = [
-            keep.tile([P, HALF_BLOCKS, SLOTS, 2], F32, name=f"h_in{hf}", align_bytes=64) for hf in range(HALVES)
-        ]
+        early = range(CHUNKS // 2)
+        late = range(CHUNKS // 2, CHUNKS)
+        early_w = [quantise_w(c, f"w_bf{c}") for c in early]
+
+        ag0 = [sbuf(f"ag0_{hf}", [P, half_cols], U32) for hf in range(HALVES)]
+        for hf in range(HALVES):
+            nc.vector.tensor_copy(ag0[hf][:], aw[0][:].bitcast(U32).indirect(a_list[:, half_list[hf]]))
+        ag1 = [sbuf(f"ag1_{m}", [P, H], U32) for m in range(B)]
+        for m in range(B):
+            nc.vector.tensor_copy(ag1[m][:], aw[1][:].bitcast(U32).indirect(a_list[:, block_list[m]]))
+
+        base = {c: frozen_layer(c, *early_w[c], c) for c in early}
+        gate_ps = bank(2, [P, P])
+        nc.tensor.transpose(gate_ps[:], gate_rows[:], ident[:])
+        gate_col = sbuf("gate_col", [P, B], F32)
+        nc.scalar.copy(out=gate_col[:], in_=gate_ps[:, 0:B])
+
+        h_words = []
         for m in range(B):
             hf, b = divmod(m, HALF_BLOCKS)
             slots = slice(m * SLOTS, (m + 1) * SLOTS)
             cols = slice(b * H, (b + 1) * H)
-            h_ps = bank(4 + m, [P, H])
-            order = (0, 1) if hf == 0 else (1, 0)
-            for s in order:
+            h_ps = bank(4 + m % 2, [P, H])
+            for s, words in enumerate((ag0[hf][:, cols], ag1[m][:])):
                 nc.tensor.matmul_mx(
                     out=h_ps[:],
                     lhsT=xg[s][:, slots].bitcast(FP8X4),
                     lhsT_scale=xg_sc[4 * s : P, slots],
-                    rhs=ag[s, hf][:, cols].bitcast(FP8X4),
+                    rhs=words.bitcast(FP8X4),
                     rhs_scale=ag_sc[hf][4 * s : P, cols],
-                    start=(s == order[0]),
-                    stop=(s == order[-1]),
+                    start=(s == 0),
+                    stop=(s == PASSES - 1),
                 )
-            h_pairs = keep.tile([P, 2, P, 2], BF16, name=f"h_pairs{m}", align_bytes=64)
+            h_pairs = sbuf(f"h_pairs{m}", [P, 2, P, 2], BF16)
             nc.scalar.activation(out=h_pairs[:], in_=h_ps[:].rearrange("j (p u e) -> j u p e", u=2, e=2), func=RELU)
-            turned = bank(4 + m, [P, 2, SLOTS])
+            turned = bank(6 + m % 2, [P, 2, SLOTS])
             pairs = h_pairs[:].rearrange("j u p e -> j (u p e)").bitcast(F32)
             for u in range(2):
                 nc.tensor.transpose(turned[:, u, :], pairs[:, u * P : (u + 1) * P], ident[:])
-            nc.scalar.copy(out=h_words[hf][:, b], in_=turned[:].rearrange("p u j -> p j u"))
+            h_words.append(sbuf(f"h_words{m}", [P, SLOTS, 2], F32))
+            nc.scalar.copy(out=h_words[m][:], in_=turned[:].rearrange("p u j -> p j u"))
 
-        hq = [keep.tile([P, HALF_SLOTS], U32, name=f"hq{hf}", align_bytes=64) for hf in range(HALVES)]
-        hq_sc = [keep.tile([P, HALF_SLOTS], U8, name=f"hq_sc{hf}", align_bytes=64) for hf in range(HALVES)]
-        bg = []
-        for hf in range(HALVES):
-            bg.append(keep.tile([P, half_cols], U32, name=("bg0", "h_in0")[hf], align_bytes=64))
-            nc.vector.tensor_copy(bg[hf][:], bw[:].bitcast(U32).indirect(b_list[:, half_list[hf]]))
+        bgs = [sbuf(f"bg{m}", [P, N], U32) for m in range(B)]
+        for m in range(B):
+            nc.vector.tensor_copy(bgs[m][:], bw[:].bitcast(U32).indirect(b_list[:, block_list[m]]))
+        hq_first = sbuf("hq_first", [P, SLOTS], U32)
+        hq_rest = sbuf("bw", [P, B - 1, SLOTS], U32)
+        hqs = [hq_first[:]] + [hq_rest[:, m] for m in range(B - 1)]
+        gy = {}
+        gy_early = sbuf("gy_early", [P, len(early), T], F32)
+        result = {c: sbuf(f"result{c}", [P, 2 * T], F32) for c in early}
+
+        def second_layer(m, bank_number):
+            hf, b = divmod(m, HALF_BLOCKS)
+            hq_sc = sbuf(f"hq_sc{m}", [P, SLOTS], U8)
             nc.vector.quantize_mx(
-                out=hq[hf][:].bitcast(FP8X4),
-                scales=hq_sc[hf][:],
-                in_=h_words[hf][:].rearrange("p b j u -> p (b j u)").bitcast(BF16),
+                out=hqs[m].bitcast(FP8X4), scales=hq_sc[:], in_=h_words[m][:].rearrange("p j u -> p (j u)").bitcast(BF16)
             )
+            y_ps = bank(bank_number, [P, N])
+            nc.tensor.matmul_mx(
+                out=y_ps[:],
+                lhsT=hqs[m].bitcast(FP8X4),
+                lhsT_scale=hq_sc[:],
+                rhs=bgs[m][:].bitcast(FP8X4),
+                rhs_scale=bg_sc[hf][:, b * N : (b + 1) * N],
+                start=True,
+                stop=True,
+            )
+            gy[m] = sbuf(f"gy{m}", [P, N], F32)
+            nc.scalar.activation(out=gy[m][:], in_=y_ps[:], func=COPY, scale=gate_col[:, m : m + 1])
 
-        y_sb = keep.tile([P, CHUNKS, T], F32, name="y_sb")
-        for hf in range(HALVES):
-            half = slice(hf * HALF_SLOTS, (hf + 1) * HALF_SLOTS)
-            for pair in range(CHUNKS // 2):
-                y_ps = bank(4 + 2 * hf + pair, [P, 2, HALF_SLOTS])
-                for cc in range(2):
-                    c = 2 * pair + cc
-                    for b in range(HALF_BLOCKS):
-                        cols = slice(b * N + c * P, b * N + (c + 1) * P)
-                        slots = slice(b * SLOTS, (b + 1) * SLOTS)
-                        nc.tensor.matmul_mx(
-                            out=y_ps[:, cc, slots],
-                            lhsT=bg[hf][:, cols].bitcast(FP8X4),
-                            lhsT_scale=bg_sc[hf][:, cols],
-                            rhs=hq[hf][:, slots].bitcast(FP8X4),
-                            rhs_scale=hq_sc[hf][:, slots],
-                            start=True,
-                            stop=True,
-                        )
-                nc.scalar.copy(out=y_sb[:, 2 * pair : 2 * pair + 2, half], in_=y_ps[:])
+        def scatter(c, gated, first, count):
+            tokens = token_list[:, first // 16 : (first + count) // 16]
+            nc.vector.tensor_tensor(result[c][:].indirect(tokens), gated, base[c][:, first : first + count], ADD)
 
-        for c in range(CHUNKS):
-            routed = keep.tile([P, TOKEN_WINDOW], F32, name="h_in1" if c == 0 else f"routed{c}", align_bytes=64)
-            if c == 0:
-                for hf in range(HALVES):
-                    half = slice(hf * HALF_SLOTS, (hf + 1) * HALF_SLOTS)
-                    tok = token_list[:, hf * HALF_SLOTS // 16 : (hf + 1) * HALF_SLOTS // 16]
-                    nc.vector.tensor_tensor(routed[:].indirect(tok), y_sb[:, c, half], gate_sb[:, half], MULT)
-            else:
-                nc.vector.tensor_tensor(routed[:].indirect(token_list[:]), y_sb[:, c, :], gate_sb[:], MULT)
-            res = keep.tile([P, T], F32, name=f"res{c}")
-            rows = slice(c * P, (c + 1) * P)
-            if c == last:
-                for hf in range(2):
-                    half = slice(hf * T // 2, (hf + 1) * T // 2)
-                    nc.vector.tensor_tensor(res[:, half], total[c][:, half], routed[:, half], ADD)
-                    nc.sync.dma_start(out=out[rows, half], in_=res[:, half])
-            else:
-                routed_ps = bank(4, [P, T // P, P])
-                for tb in range(T // P):
-                    nc.tensor.transpose(routed_ps[:, tb, :], routed[:, tb * P : (tb + 1) * P], ident[:])
-                routed_t = keep.tile([P, T // P, P], F32, name=f"routed_t{c}")
-                nc.scalar.copy(out=routed_t[:], in_=routed_ps[:])
-                for tb in range(T // P):
-                    nc.tensor.matmul(
-                        total[c][:, tb * P : (tb + 1) * P],
-                        lhsT=routed_t[:, tb, :],
-                        rhs=ident[:],
-                        is_transpose=True,
-                        start=False,
-                        stop=(tb == T // P - 1),
-                    )
-                nc.scalar.copy(out=res[:], in_=total[c][:])
-                nc.scalar.dma_start(out=out[rows, :], in_=res[:])
+        for blocks, y_banks, piece_bank in (((0,), (2,), 0), ((1,), (2,), 1), ((2, 3), (0, 2), 3)):
+            first, count = blocks[0] * SLOTS, len(blocks) * SLOTS
+            for m, y_bank in zip(blocks, y_banks):
+                second_layer(m, y_bank)
+            piece = bank(piece_bank, [P, len(early), count])
+            for c in early:
+                for i, m in enumerate(blocks):
+                    nc.tensor.transpose(piece[:, c, i * SLOTS : (i + 1) * SLOTS], gy[m][:, c * P : (c + 1) * P], ident[:])
+            nc.scalar.copy(out=gy_early[:, :, first : first + count], in_=piece[:])
+            for c in early:
+                scatter(c, gy_early[:, c, first : first + count], first, count)
+        for c in early:
+            nc.sync.dma_start(out=out[c * P : (c + 1) * P, :], in_=result[c][:, 0:T])
+        gy_late = {}
+        for c in late:
+            whole = bank(2 + c, [P, T])
+            for m in range(B):
+                nc.tensor.transpose(whole[:, m * SLOTS : (m + 1) * SLOTS], gy[m][:, c * P : (c + 1) * P], ident[:])
+            gy_late[c] = sbuf(f"gy_late{c}", [P, T], F32)
+            nc.scalar.copy(out=gy_late[c][:], in_=whole[:])
+        for c, buffer_name in zip(late, ("gy1", "gy3")):
+            base[c] = frozen_layer(c, *quantise_w(c, buffer_name), 4 + c)
+        for c, buffer_name in zip(late, ("gy3", "result3")):
+            result[c] = sbuf(buffer_name, [P, 2 * T], F32)
+            scatter(c, gy_late[c][:], 0, T)
+            nc.sync.dma_start(out=out[c * P : (c + 1) * P, :], in_=result[c][:, 0:T])

@@ -26,10 +26,16 @@ HALF_SLOTS = HALF_BLOCKS * SLOTS
 TOKEN_WINDOW = 704
 CHUNKS = N // P
 HALF_N = N // 2
+B_ROW = 8
 
 
 def words_of(dram_pass):
     return dram_pass.rearrange("p c d -> p (c d)").bitcast(I32)
+
+
+def load_scale_rows(nc, tile, first_row, dram_pass):
+    for r in range(4):
+        nc.sync.dma_start(out=tile[first_row + r : P : 32, :].bitcast(I32), in_=dram_pass[r:16:4, :].bitcast(I32))
 
 
 def load_scales(nc, tile, dram_scales, width):
@@ -85,13 +91,14 @@ def tile_moe_dyl_relu_kernel(
         nc.sync.dma_start(token_list[:], offs)
         nc.sync.dma_start(out=xw[0][:, 0:T], in_=words_of(x_words[0]))
         nc.sync.dma_start(out=xw[1][:, 0:T], in_=words_of(x_words[1]))
-        load_scales(nc, xs, x_scales, T)
         nc.sync.dma_start(b_list[:], offs3)
-        load_w(0, 0)
-        load_scales(nc, b_sc, wb_scales, E * N)
-        load_w(0, 1)
+        load_scales(nc, xs, x_scales, T)
+        load_scale_rows(nc, b_sc, B_ROW, wb_scales[0])
         nc.sync.dma_start(a_list[:], offs2)
-        load_scales(nc, a_sc, wa_scales, E * H)
+        for s in range(PASSES):
+            load_scale_rows(nc, a_sc, 4 * s, wa_scales[s])
+        for s in range(PASSES):
+            load_w(0, s)
         nc.sync.dma_start(out=aw[0][:], in_=words_of(wa_words[0]))
         nc.sync.dma_start(out=gate_rows[0:B, :], in_=gate[0].rearrange("(m j) -> m j", m=B))
         nc.sync.dma_start(out=aw[1][:], in_=words_of(wa_words[1]))
@@ -207,7 +214,7 @@ def tile_moe_dyl_relu_kernel(
                 lhsT=hqs[m].bitcast(FP8X4),
                 lhsT_scale=hq_sc[:],
                 rhs=bgs[m][:].bitcast(FP8X4),
-                rhs_scale=bg_sc[hf][:, b * N : (b + 1) * N],
+                rhs_scale=bg_sc[hf][B_ROW:P, b * N : (b + 1) * N],
                 start=True,
                 stop=True,
             )

@@ -16,6 +16,7 @@ FP8X4 = mybir.dt.float8_e4m3fn_x4
 RELU = mybir.ActivationFunctionType.Relu
 COPY = mybir.ActivationFunctionType.Copy
 ADD = mybir.AluOpType.add
+MULT = mybir.AluOpType.mult
 
 P = 128
 PASSES = K // 512
@@ -72,7 +73,8 @@ def tile_moe_dyl_relu_kernel(
         a_sc = sbuf("a_sc", [P, E * H], U8)
         bw = sbuf("bw", [P, E * N], I32)
         b_sc = sbuf("b_sc", [P, E * N], U8)
-        w_raw = [sbuf(f"w_raw{part}", [P, PASSES, 4, HALF_N], F32) for part in range(2)]
+        w_parts = [(0, HALF_N), (HALF_N, P), (HALF_N + P, P)]
+        w_raw = [sbuf(f"w_raw{i}", [P, PASSES, 4, width], F32) for i, (start, width) in enumerate(w_parts)]
         gate_rows = sbuf("gate_rows", [P, SLOTS], F32)
         ident = sbuf("ident", [P, P], F32)
 
@@ -85,7 +87,8 @@ def tile_moe_dyl_relu_kernel(
         make_identity(nc, ident[:])
 
         def load_w(part, s):
-            rows = w[512 * s : 512 * (s + 1), part * HALF_N : (part + 1) * HALF_N]
+            start, width = w_parts[part]
+            rows = w[512 * s : 512 * (s + 1), start : start + width]
             nc.sync.dma_start(out=w_raw[part][:, s], in_=rows.rearrange("(p j) n -> p j n", j=4))
 
         nc.sync.dma_start(token_list[:], offs)
@@ -103,8 +106,9 @@ def tile_moe_dyl_relu_kernel(
         nc.sync.dma_start(out=gate_rows[0:B, :], in_=gate[0].rearrange("(m j) -> m j", m=B))
         nc.sync.dma_start(out=aw[1][:], in_=words_of(wa_words[1]))
         nc.sync.dma_start(out=bw[:], in_=words_of(wb_words[0]))
-        for s in range(PASSES):
-            load_w(1, s)
+        for part in (1, 2):
+            for s in range(PASSES):
+                load_w(part, s)
 
         half_cols = HALF_BLOCKS * H
         half_list = [slice(hf * half_cols // 16, (hf + 1) * half_cols // 16) for hf in range(HALVES)]
@@ -122,14 +126,18 @@ def tile_moe_dyl_relu_kernel(
         for hf in range(HALVES):
             nc.vector.tensor_copy(ag_sc[hf][:], a_sc[:].indirect(a_list[:, half_list[hf]]))
 
-        def quantise_w(c, buffer_name):
-            part, first = divmod(c * P, HALF_N)
+        def round_w(c, buffer_name):
+            part = max(c - 1, 0)
+            first = c * P - w_parts[part][0]
             w_bf = sbuf(buffer_name, [P, PASSES, P, 4], BF16)
             nc.scalar.copy(
                 out=w_bf[:].rearrange("p s (c i) j -> p s c j i", i=4),
                 in_=w_raw[part][:, :, :, first : first + P].rearrange("p s j (c i) -> p s c j i", i=4),
             )
-            wq = sbuf(f"wq{c}", [P, PASSES * P], U32)
+            return w_bf
+
+        def quantise_w(c, w_bf, codes_name):
+            wq = sbuf(codes_name, [P, PASSES * P], U32)
             wq_sc = sbuf(f"wq_sc{c}", [P, PASSES * P], U8)
             nc.vector.quantize_mx(out=wq[:].bitcast(FP8X4), scales=wq_sc[:], in_=w_bf[:].rearrange("p s n j -> p (s n j)"))
             return wq, wq_sc
@@ -152,7 +160,7 @@ def tile_moe_dyl_relu_kernel(
 
         early = range(CHUNKS // 2)
         late = range(CHUNKS // 2, CHUNKS)
-        early_w = [quantise_w(c, f"w_bf{c}") for c in early]
+        early_w = [quantise_w(c, round_w(c, f"w_bf{c}"), f"wq{c}") for c in early]
 
         ag0 = [sbuf(f"ag0_{hf}", [P, half_cols], U32) for hf in range(HALVES)]
         for hf in range(HALVES):
@@ -166,13 +174,17 @@ def tile_moe_dyl_relu_kernel(
         nc.tensor.transpose(gate_ps[:], gate_rows[:], ident[:])
         gate_col = sbuf("gate_col", [P, B], F32)
         nc.scalar.copy(out=gate_col[:], in_=gate_ps[:, 0:B])
+        spread_ps = bank(3, [P, SLOTS])
+        nc.tensor.transpose(spread_ps[:], gate_col[:, 0:1].to_broadcast([P, P]), ident[:])
+        gate_first = sbuf("gate_first", [P, SLOTS], F32)
+        nc.scalar.copy(out=gate_first[:], in_=spread_ps[:])
 
         h_words = []
         for m in range(B):
             hf, b = divmod(m, HALF_BLOCKS)
             slots = slice(m * SLOTS, (m + 1) * SLOTS)
             cols = slice(b * H, (b + 1) * H)
-            h_ps = bank(4 + m % 2, [P, H])
+            h_ps = bank(4 + m, [P, H])
             for s, words in enumerate((ag0[hf][:, cols], ag1[m][:])):
                 nc.tensor.matmul_mx(
                     out=h_ps[:],
@@ -185,7 +197,7 @@ def tile_moe_dyl_relu_kernel(
                 )
             h_pairs = sbuf(f"h_pairs{m}", [P, 2, P, 2], BF16)
             nc.scalar.activation(out=h_pairs[:], in_=h_ps[:].rearrange("j (p u e) -> j u p e", u=2, e=2), func=RELU)
-            turned = bank(6 + m % 2, [P, 2, SLOTS])
+            turned = bank(4 + m, [P, 2, SLOTS])
             pairs = h_pairs[:].rearrange("j u p e -> j (u p e)").bitcast(F32)
             for u in range(2):
                 nc.tensor.transpose(turned[:, u, :], pairs[:, u * P : (u + 1) * P], ident[:])
@@ -195,40 +207,62 @@ def tile_moe_dyl_relu_kernel(
         bgs = [sbuf(f"bg{m}", [P, N], U32) for m in range(B)]
         for m in range(B):
             nc.vector.tensor_copy(bgs[m][:], bw[:].bitcast(U32).indirect(b_list[:, block_list[m]]))
-        hq_first = sbuf("hq_first", [P, SLOTS], U32)
-        hq_rest = sbuf("bw", [P, B - 1, SLOTS], U32)
-        hqs = [hq_first[:]] + [hq_rest[:, m] for m in range(B - 1)]
+        hq_all = sbuf("bw", [P, B, SLOTS], U32)
+        hqs = [hq_all[:, m] for m in range(B)]
         gy = {}
         gy_early = sbuf("gy_early", [P, len(early), T], F32)
         result = {c: sbuf(f"result{c}", [P, 2 * T], F32) for c in early}
 
-        def second_layer(m, bank_number):
-            hf, b = divmod(m, HALF_BLOCKS)
-            hq_sc = sbuf(f"hq_sc{m}", [P, SLOTS], U8)
+        hq_sc = [sbuf(f"hq_sc{m}", [P, SLOTS], U8) for m in range(B)]
+
+        def quantise_h(m):
             nc.vector.quantize_mx(
-                out=hqs[m].bitcast(FP8X4), scales=hq_sc[:], in_=h_words[m][:].rearrange("p j u -> p (j u)").bitcast(BF16)
+                out=hqs[m].bitcast(FP8X4), scales=hq_sc[m][:], in_=h_words[m][:].rearrange("p j u -> p (j u)").bitcast(BF16)
             )
-            y_ps = bank(bank_number, [P, N])
+
+        def second_layer(m, bank_number, first_col):
+            hf, b = divmod(m, HALF_BLOCKS)
+            y_ps = bank(bank_number, [P, N - first_col])
             nc.tensor.matmul_mx(
                 out=y_ps[:],
                 lhsT=hqs[m].bitcast(FP8X4),
-                lhsT_scale=hq_sc[:],
-                rhs=bgs[m][:].bitcast(FP8X4),
-                rhs_scale=bg_sc[hf][B_ROW:P, b * N : (b + 1) * N],
+                lhsT_scale=hq_sc[m][:],
+                rhs=bgs[m][:, first_col:N].bitcast(FP8X4),
+                rhs_scale=bg_sc[hf][B_ROW:P, b * N + first_col : (b + 1) * N],
                 start=True,
                 stop=True,
             )
-            gy[m] = sbuf(f"gy{m}", [P, N], F32)
-            nc.scalar.activation(out=gy[m][:], in_=y_ps[:], func=COPY, scale=gate_col[:, m : m + 1])
+            gy[m] = sbuf("w_raw1" if m == 1 else f"gy{m}", [P, N], F32)
+            nc.scalar.activation(out=gy[m][:, first_col:N], in_=y_ps[:], func=COPY, scale=gate_col[:, m : m + 1])
 
         def scatter(c, gated, first, count):
             tokens = token_list[:, first // 16 : (first + count) // 16]
             nc.vector.tensor_tensor(result[c][:].indirect(tokens), gated, base[c][:, first : first + count], ADD)
 
-        for blocks, y_banks, piece_bank in (((0,), (2,), 0), ((1,), (2,), 1), ((2, 3), (0, 2), 3)):
+        w_bf_next = round_w(late[0], "w_bf2")
+        for m in range(B):
+            quantise_h(m)
+        direct = bank(0, [P, len(early), SLOTS])
+        for c in early:
+            nc.tensor.matmul_mx(
+                out=direct[:, c, :],
+                lhsT=bgs[0][:, c * P : (c + 1) * P].bitcast(FP8X4),
+                lhsT_scale=bg_sc[0][B_ROW:P, c * P : (c + 1) * P],
+                rhs=hqs[0].bitcast(FP8X4),
+                rhs_scale=hq_sc[0][:],
+                start=True,
+                stop=True,
+            )
+        gy_first = sbuf("h_words3", [P, len(early), SLOTS], F32)
+        nc.vector.tensor_tensor(
+            gy_first[:], direct[:], gate_first[:].unsqueeze(1).to_broadcast([P, len(early), SLOTS]), MULT
+        )
+        for c in early:
+            scatter(c, gy_first[:, c, :], 0, SLOTS)
+        for blocks, y_banks, piece_bank in (((1,), (2,), 1), ((2, 3), (6, 7), 3)):
             first, count = blocks[0] * SLOTS, len(blocks) * SLOTS
             for m, y_bank in zip(blocks, y_banks):
-                second_layer(m, y_bank)
+                second_layer(m, y_bank, 0)
             piece = bank(piece_bank, [P, len(early), count])
             for c in early:
                 for i, m in enumerate(blocks):
@@ -238,15 +272,18 @@ def tile_moe_dyl_relu_kernel(
                 scatter(c, gy_early[:, c, first : first + count], first, count)
         for c in early:
             nc.sync.dma_start(out=out[c * P : (c + 1) * P, :], in_=result[c][:, 0:T])
-        gy_late = {}
+        second_layer(0, 1, HALF_N)
+        gy_late, late_w = {}, {}
         for c in late:
             whole = bank(2 + c, [P, T])
             for m in range(B):
                 nc.tensor.transpose(whole[:, m * SLOTS : (m + 1) * SLOTS], gy[m][:, c * P : (c + 1) * P], ident[:])
             gy_late[c] = sbuf(f"gy_late{c}", [P, T], F32)
             nc.scalar.copy(out=gy_late[c][:], in_=whole[:])
-        for c, buffer_name in zip(late, ("gy1", "gy3")):
-            base[c] = frozen_layer(c, *quantise_w(c, buffer_name), 4 + c)
+        late_w[late[0]] = quantise_w(late[0], w_bf_next, "h_words3")
+        base[late[0]] = frozen_layer(late[0], *late_w[late[0]], 3)
+        late_w[late[1]] = quantise_w(late[1], round_w(late[1], "gy3"), "wq3")
+        base[late[1]] = frozen_layer(late[1], *late_w[late[1]], 2)
         for c, buffer_name in zip(late, ("gy3", "result3")):
             result[c] = sbuf(buffer_name, [P, 2 * T], F32)
             scatter(c, gy_late[c][:], 0, T)

@@ -26,8 +26,9 @@ HALF_BLOCKS = B // HALVES
 HALF_SLOTS = HALF_BLOCKS * SLOTS
 TOKEN_WINDOW = 704
 CHUNKS = N // P
-HALF_N = N // 2
 B_ROW = 8
+PIECE_BANK = ((3, 1), (0, 5), (4, 6))
+BASE_BANK = (2, 7, 2, 3)
 
 
 def words_of(dram_pass):
@@ -73,7 +74,7 @@ def tile_moe_dyl_relu_kernel(
         a_sc = sbuf("a_sc", [P, E * H], U8)
         bw = sbuf("bw", [P, E * N], I32)
         b_sc = sbuf("b_sc", [P, E * N], U8)
-        w_parts = [(0, HALF_N), (HALF_N, P), (HALF_N + P, P)]
+        w_parts = [(0, P), (P, N - P)]
         w_raw = [sbuf(f"w_raw{i}", [P, PASSES, 4, width], F32) for i, (start, width) in enumerate(w_parts)]
         gate_rows = sbuf("gate_rows", [P, SLOTS], F32)
         ident = sbuf("ident", [P, P], F32)
@@ -100,13 +101,11 @@ def tile_moe_dyl_relu_kernel(
         nc.sync.dma_start(a_list[:], offs2)
         for s in range(PASSES):
             load_scale_rows(nc, a_sc, 4 * s, wa_scales[s])
-        for s in range(PASSES):
-            load_w(0, s)
         nc.sync.dma_start(out=aw[0][:], in_=words_of(wa_words[0]))
         nc.sync.dma_start(out=gate_rows[0:B, :], in_=gate[0].rearrange("(m j) -> m j", m=B))
         nc.sync.dma_start(out=aw[1][:], in_=words_of(wa_words[1]))
         nc.sync.dma_start(out=bw[:], in_=words_of(wb_words[0]))
-        for part in (1, 2):
+        for part in range(len(w_parts)):
             for s in range(PASSES):
                 load_w(part, s)
 
@@ -119,15 +118,14 @@ def tile_moe_dyl_relu_kernel(
             nc.vector.tensor_copy(xg[s][:], xw[s][:].bitcast(U32).indirect(token_list[:]))
         xg_sc = sbuf("xg_sc", [P, T], U8)
         nc.vector.tensor_copy(xg_sc[:], xs[:].indirect(token_list[:]))
-        bg_sc = [sbuf(f"bg_sc{hf}", [P, half_cols], U8) for hf in range(HALVES)]
-        for hf in range(HALVES):
-            nc.vector.tensor_copy(bg_sc[hf][:], b_sc[:].indirect(b_list[:, half_list[hf]]))
+        bg_sc = [sbuf("bg_sc0", [P, half_cols], U8)]
+        nc.vector.tensor_copy(bg_sc[0][:], b_sc[:].indirect(b_list[:, half_list[0]]))
         ag_sc = [sbuf(f"ag_sc{hf}", [P, half_cols], U8) for hf in range(HALVES)]
         for hf in range(HALVES):
             nc.vector.tensor_copy(ag_sc[hf][:], a_sc[:].indirect(a_list[:, half_list[hf]]))
 
         def round_w(c, buffer_name):
-            part = max(c - 1, 0)
+            part = min(c, 1)
             first = c * P - w_parts[part][0]
             w_bf = sbuf(buffer_name, [P, PASSES, P, 4], BF16)
             nc.scalar.copy(
@@ -142,25 +140,25 @@ def tile_moe_dyl_relu_kernel(
             nc.vector.quantize_mx(out=wq[:].bitcast(FP8X4), scales=wq_sc[:], in_=w_bf[:].rearrange("p s n j -> p (s n j)"))
             return wq, wq_sc
 
-        def frozen_layer(c, wq, wq_sc, bank_number):
+        def frozen_passes(wq, wq_sc, tokens, token_scales, bank_number):
             base_ps = bank(bank_number, [P, T])
             for s in range(PASSES):
                 nc.tensor.matmul_mx(
                     out=base_ps[:],
                     lhsT=wq[:, s * P : (s + 1) * P].bitcast(FP8X4),
                     lhsT_scale=wq_sc[:, s * P : (s + 1) * P],
-                    rhs=xg[s][:].bitcast(FP8X4),
-                    rhs_scale=xg_sc[4 * s : P, :],
+                    rhs=tokens[s][:, 0:T].bitcast(FP8X4),
+                    rhs_scale=token_scales[4 * s : P, 0:T],
                     start=(s == 0),
                     stop=(s == PASSES - 1),
                 )
-            base_sb = sbuf(f"base{c}", [P, T], F32)
-            nc.scalar.copy(out=base_sb[:], in_=base_ps[:])
-            return base_sb
+            return base_ps
 
-        early = range(CHUNKS // 2)
-        late = range(CHUNKS // 2, CHUNKS)
-        early_w = [quantise_w(c, round_w(c, f"w_bf{c}"), f"wq{c}") for c in early]
+        def to_sbuf(name, source, width):
+            staged = sbuf(name, [P, width], F32)
+            nc.scalar.copy(out=staged[:], in_=source[:])
+            return staged
+
 
         ag0 = [sbuf(f"ag0_{hf}", [P, half_cols], U32) for hf in range(HALVES)]
         for hf in range(HALVES):
@@ -169,15 +167,15 @@ def tile_moe_dyl_relu_kernel(
         for m in range(B):
             nc.vector.tensor_copy(ag1[m][:], aw[1][:].bitcast(U32).indirect(a_list[:, block_list[m]]))
 
-        base = {c: frozen_layer(c, *early_w[c], c) for c in early}
         gate_ps = bank(2, [P, P])
         nc.tensor.transpose(gate_ps[:], gate_rows[:], ident[:])
         gate_col = sbuf("gate_col", [P, B], F32)
         nc.scalar.copy(out=gate_col[:], in_=gate_ps[:, 0:B])
-        spread_ps = bank(3, [P, SLOTS])
-        nc.tensor.transpose(spread_ps[:], gate_col[:, 0:1].to_broadcast([P, P]), ident[:])
-        gate_first = sbuf("gate_first", [P, SLOTS], F32)
-        nc.scalar.copy(out=gate_first[:], in_=spread_ps[:])
+        spread_ps = bank(3, [P, B, SLOTS])
+        for m in range(B):
+            nc.tensor.transpose(spread_ps[:, m, :], gate_col[:, m : m + 1].to_broadcast([P, P]), ident[:])
+        gate_all = sbuf("gate_all", [P, T], F32)
+        nc.scalar.copy(out=gate_all[:], in_=spread_ps[:].rearrange("p m j -> p (m j)"))
 
         h_words = []
         for m in range(B):
@@ -209,82 +207,76 @@ def tile_moe_dyl_relu_kernel(
             nc.vector.tensor_copy(bgs[m][:], bw[:].bitcast(U32).indirect(b_list[:, block_list[m]]))
         hq_all = sbuf("bw", [P, B, SLOTS], U32)
         hqs = [hq_all[:, m] for m in range(B)]
-        gy = {}
-        gy_early = sbuf("gy_early", [P, len(early), T], F32)
-        result = {c: sbuf(f"result{c}", [P, 2 * T], F32) for c in early}
-
         hq_sc = [sbuf(f"hq_sc{m}", [P, SLOTS], U8) for m in range(B)]
-
-        def quantise_h(m):
+        w_bf = round_w(0, "w_bf0")
+        for m in range(B):
             nc.vector.quantize_mx(
                 out=hqs[m].bitcast(FP8X4), scales=hq_sc[m][:], in_=h_words[m][:].rearrange("p j u -> p (j u)").bitcast(BF16)
             )
+        wq = quantise_w(0, w_bf, "wq0")
+        bg_sc.append(sbuf("h_words3", [P, half_cols], U8))
+        nc.vector.tensor_copy(bg_sc[1][:], b_sc[:].indirect(b_list[:, half_list[1]]))
 
-        def second_layer(m, bank_number, first_col):
-            hf, b = divmod(m, HALF_BLOCKS)
-            y_ps = bank(bank_number, [P, N - first_col])
-            nc.tensor.matmul_mx(
-                out=y_ps[:],
-                lhsT=hqs[m].bitcast(FP8X4),
-                lhsT_scale=hq_sc[m][:],
-                rhs=bgs[m][:, first_col:N].bitcast(FP8X4),
-                rhs_scale=bg_sc[hf][B_ROW:P, b * N + first_col : (b + 1) * N],
-                start=True,
-                stop=True,
-            )
-            gy[m] = sbuf("w_raw1" if m == 1 else f"gy{m}", [P, N], F32)
-            nc.scalar.activation(out=gy[m][:, first_col:N], in_=y_ps[:], func=COPY, scale=gate_col[:, m : m + 1])
+        halves = [slice(hf * HALF_SLOTS, (hf + 1) * HALF_SLOTS) for hf in range(HALVES)]
+        half_tokens = [token_list[:, hf * HALF_SLOTS // 16 : (hf + 1) * HALF_SLOTS // 16] for hf in range(HALVES)]
+        result = [sbuf(f"result{c}", [P, TOKEN_WINDOW], F32) for c in range(CHUNKS)]
+        direct = CHUNKS - 1
+        turned_cols = direct * P
 
-        def scatter(c, gated, first, count):
-            tokens = token_list[:, first // 16 : (first + count) // 16]
-            nc.vector.tensor_tensor(result[c][:].indirect(tokens), gated, base[c][:, first : first + count], ADD)
+        for hf in range(HALVES):
+            y_ps = bank(hf, [P, HALF_SLOTS])
+            for b in range(HALF_BLOCKS):
+                m = hf * HALF_BLOCKS + b
+                nc.tensor.matmul_mx(
+                    out=y_ps[:, b * SLOTS : (b + 1) * SLOTS],
+                    lhsT=bgs[m][:, turned_cols:N].bitcast(FP8X4),
+                    lhsT_scale=bg_sc[hf][B_ROW:P, b * N + turned_cols : (b + 1) * N],
+                    rhs=hqs[m].bitcast(FP8X4),
+                    rhs_scale=hq_sc[m][:],
+                    start=True,
+                    stop=True,
+                )
+            y_sb = to_sbuf(f"y_direct{hf}", y_ps, HALF_SLOTS)
+            nc.vector.tensor_tensor(result[direct][:].indirect(half_tokens[hf]), y_sb[:], gate_all[:, halves[hf]], MULT)
 
-        w_bf_next = round_w(late[0], "w_bf2")
-        for m in range(B):
-            quantise_h(m)
-        direct = bank(0, [P, len(early), SLOTS])
-        for c in early:
-            nc.tensor.matmul_mx(
-                out=direct[:, c, :],
-                lhsT=bgs[0][:, c * P : (c + 1) * P].bitcast(FP8X4),
-                lhsT_scale=bg_sc[0][B_ROW:P, c * P : (c + 1) * P],
-                rhs=hqs[0].bitcast(FP8X4),
-                rhs_scale=hq_sc[0][:],
-                start=True,
-                stop=True,
-            )
-        gy_first = sbuf("h_words3", [P, len(early), SLOTS], F32)
-        nc.vector.tensor_tensor(
-            gy_first[:], direct[:], gate_first[:].unsqueeze(1).to_broadcast([P, len(early), SLOTS]), MULT
-        )
-        for c in early:
-            scatter(c, gy_first[:, c, :], 0, SLOTS)
-        for blocks, y_banks, piece_bank in (((1,), (2,), 1), ((2, 3), (6, 7), 3)):
-            first, count = blocks[0] * SLOTS, len(blocks) * SLOTS
-            for m, y_bank in zip(blocks, y_banks):
-                second_layer(m, y_bank, 0)
-            piece = bank(piece_bank, [P, len(early), count])
-            for c in early:
-                for i, m in enumerate(blocks):
-                    nc.tensor.transpose(piece[:, c, i * SLOTS : (i + 1) * SLOTS], gy[m][:, c * P : (c + 1) * P], ident[:])
-            nc.scalar.copy(out=gy_early[:, :, first : first + count], in_=piece[:])
-            for c in early:
-                scatter(c, gy_early[:, c, first : first + count], first, count)
-        for c in early:
-            nc.sync.dma_start(out=out[c * P : (c + 1) * P, :], in_=result[c][:, 0:T])
-        second_layer(0, 1, HALF_N)
-        gy_late, late_w = {}, {}
-        for c in late:
-            whole = bank(2 + c, [P, T])
-            for m in range(B):
-                nc.tensor.transpose(whole[:, m * SLOTS : (m + 1) * SLOTS], gy[m][:, c * P : (c + 1) * P], ident[:])
-            gy_late[c] = sbuf(f"gy_late{c}", [P, T], F32)
-            nc.scalar.copy(out=gy_late[c][:], in_=whole[:])
-        late_w[late[0]] = quantise_w(late[0], w_bf_next, "h_words3")
-        base[late[0]] = frozen_layer(late[0], *late_w[late[0]], 3)
-        late_w[late[1]] = quantise_w(late[1], round_w(late[1], "gy3"), "wq3")
-        base[late[1]] = frozen_layer(late[1], *late_w[late[1]], 2)
-        for c, buffer_name in zip(late, ("gy3", "result3")):
-            result[c] = sbuf(buffer_name, [P, 2 * T], F32)
-            scatter(c, gy_late[c][:], 0, T)
+        pieces = {}
+
+        def gated_pieces(hf):
+            gy = []
+            for b in range(HALF_BLOCKS):
+                m = hf * HALF_BLOCKS + b
+                y_ps = bank(4 + m, [P, turned_cols])
+                for first, stop in ((0, 2 * P), (2 * P, turned_cols)):
+                    nc.tensor.matmul_mx(
+                        out=y_ps[:, first:stop],
+                        lhsT=hqs[m].bitcast(FP8X4),
+                        lhsT_scale=hq_sc[m][:],
+                        rhs=bgs[m][:, first:stop].bitcast(FP8X4),
+                        rhs_scale=bg_sc[hf][B_ROW:P, b * N + first : b * N + stop],
+                        start=True,
+                        stop=True,
+                    )
+                gy.append(sbuf(f"gy{m}", [P, turned_cols], F32))
+                nc.scalar.activation(out=gy[b][:], in_=y_ps[:], func=COPY, scale=gate_col[:, m : m + 1])
+            for c in range(direct):
+                pieces[c, hf] = bank(PIECE_BANK[c][hf], [P, HALF_SLOTS])
+                for b in range(HALF_BLOCKS):
+                    nc.tensor.transpose(pieces[c, hf][:, b * SLOTS : (b + 1) * SLOTS], gy[b][:, c * P : (c + 1) * P], ident[:])
+
+        gated_pieces(0)
+        for c in range(direct):
+            base = to_sbuf(f"base{c}", frozen_passes(*wq, xg, xg_sc, BASE_BANK[c]), T)
+            for hf in range(HALVES):
+                gated = to_sbuf("w_raw1" if (c, hf) == (1, 1) else f"gated{c}_{hf}", pieces[c, hf], HALF_SLOTS)
+                nc.vector.tensor_tensor(result[c][:].indirect(half_tokens[hf]), gated[:], base[:, halves[hf]], ADD)
+                if (c, hf) == (0, 0):
+                    gated_pieces(1)
+                if hf == 0 and c + 1 < direct:
+                    wq = quantise_w(c + 1, round_w(c + 1, "gy1"), f"wq{c + 1}")
+                if (c, hf) == (0, 1):
+                    direct_ps = frozen_passes(*quantise_w(direct, round_w(direct, "gy1"), "wq3"), xw, xs, BASE_BANK[direct])
+                if (c, hf) == (1, 1):
+                    total = sbuf("total", [P, T], F32)
+                    nc.vector.tensor_tensor(total[:], direct_ps[:], result[direct][:, 0:T], ADD)
+                    nc.sync.dma_start(out=out[turned_cols:N, :], in_=total[:])
             nc.sync.dma_start(out=out[c * P : (c + 1) * P, :], in_=result[c][:, 0:T])

@@ -265,10 +265,16 @@ def tile_moe_dyl_relu_kernel(
 
         gated_pieces(0)
         for c in range(direct):
-            base = to_sbuf(f"base{c}", frozen_passes(*wq, xg, xg_sc, BASE_BANK[c]), T)
+            if c == direct - 1:
+                last_ps = frozen_passes(*wq, xw, xs, BASE_BANK[c])
+            else:
+                base = to_sbuf(f"base{c}", frozen_passes(*wq, xg, xg_sc, BASE_BANK[c]), T)
             for hf in range(HALVES):
                 gated = to_sbuf("w_raw1" if (c, hf) == (1, 1) else f"gated{c}_{hf}", pieces[c, hf], HALF_SLOTS)
-                nc.vector.tensor_tensor(result[c][:].indirect(half_tokens[hf]), gated[:], base[:, halves[hf]], ADD)
+                if c == direct - 1:
+                    nc.vector.tensor_copy(result[c][:].indirect(half_tokens[hf]), gated[:])
+                else:
+                    nc.vector.tensor_tensor(result[c][:].indirect(half_tokens[hf]), gated[:], base[:, halves[hf]], ADD)
                 if (c, hf) == (0, 0):
                     gated_pieces(1)
                 if hf == 0 and c + 1 < direct:
@@ -279,4 +285,9 @@ def tile_moe_dyl_relu_kernel(
                     total = sbuf("total", [P, T], F32)
                     nc.vector.tensor_tensor(total[:], direct_ps[:], result[direct][:, 0:T], ADD)
                     nc.sync.dma_start(out=out[turned_cols:N, :], in_=total[:])
-            nc.sync.dma_start(out=out[c * P : (c + 1) * P, :], in_=result[c][:, 0:T])
+            if c == direct - 1:
+                last = sbuf("last", [P, T], F32)
+                nc.vector.tensor_tensor(last[:], last_ps[:], result[c][:, 0:T], ADD)
+                nc.sync.dma_start(out=out[c * P : (c + 1) * P, :], in_=last[:])
+            else:
+                nc.sync.dma_start(out=out[c * P : (c + 1) * P, :], in_=result[c][:, 0:T])

@@ -27,8 +27,7 @@ HALF_SLOTS = HALF_BLOCKS * SLOTS
 TOKEN_WINDOW = 704
 CHUNKS = N // P
 B_ROW = 8
-PIECE_BANK = ((3, 1), (0, 5), (4, 6))
-BASE_BANK = (2, 7, 2, 3)
+TOTAL_BANK = (3, 0, 1)
 
 
 def words_of(dram_pass):
@@ -74,8 +73,7 @@ def tile_moe_dyl_relu_kernel(
         a_sc = sbuf("a_sc", [P, E * H], U8)
         bw = sbuf("bw", [P, E * N], I32)
         b_sc = sbuf("b_sc", [P, E * N], U8)
-        w_parts = [(0, P), (P, N - P)]
-        w_raw = [sbuf(f"w_raw{i}", [P, PASSES, 4, width], F32) for i, (start, width) in enumerate(w_parts)]
+        w_raw = [sbuf(f"w_raw{c}", [P, PASSES, 4, P], F32) for c in range(CHUNKS)]
         gate_rows = sbuf("gate_rows", [P, SLOTS], F32)
         ident = sbuf("ident", [P, P], F32)
 
@@ -87,10 +85,9 @@ def tile_moe_dyl_relu_kernel(
         nc.gpsimd.memset(gate_rows[:], 0.0)
         make_identity(nc, ident[:])
 
-        def load_w(part, s):
-            start, width = w_parts[part]
-            rows = w[512 * s : 512 * (s + 1), start : start + width]
-            nc.sync.dma_start(out=w_raw[part][:, s], in_=rows.rearrange("(p j) n -> p j n", j=4))
+        def load_w(c, s):
+            rows = w[512 * s : 512 * (s + 1), c * P : (c + 1) * P]
+            nc.sync.dma_start(out=w_raw[c][:, s], in_=rows.rearrange("(p j) n -> p j n", j=4))
 
         nc.sync.dma_start(token_list[:], offs)
         nc.sync.dma_start(out=xw[0][:, 0:T], in_=words_of(x_words[0]))
@@ -105,9 +102,9 @@ def tile_moe_dyl_relu_kernel(
         nc.sync.dma_start(out=gate_rows[0:B, :], in_=gate[0].rearrange("(m j) -> m j", m=B))
         nc.sync.dma_start(out=aw[1][:], in_=words_of(wa_words[1]))
         nc.sync.dma_start(out=bw[:], in_=words_of(wb_words[0]))
-        for part in range(len(w_parts)):
+        for c in range(CHUNKS):
             for s in range(PASSES):
-                load_w(part, s)
+                load_w(c, s)
 
         half_cols = HALF_BLOCKS * H
         half_list = [slice(hf * half_cols // 16, (hf + 1) * half_cols // 16) for hf in range(HALVES)]
@@ -124,35 +121,18 @@ def tile_moe_dyl_relu_kernel(
         for hf in range(HALVES):
             nc.vector.tensor_copy(ag_sc[hf][:], a_sc[:].indirect(a_list[:, half_list[hf]]))
 
-        def round_w(c, buffer_name):
-            part = min(c, 1)
-            first = c * P - w_parts[part][0]
-            w_bf = sbuf(buffer_name, [P, PASSES, P, 4], BF16)
+        def round_w(c, w_bf):
             nc.scalar.copy(
-                out=w_bf[:].rearrange("p s (c i) j -> p s c j i", i=4),
-                in_=w_raw[part][:, :, :, first : first + P].rearrange("p s j (c i) -> p s c j i", i=4),
+                out=w_bf.rearrange("p s (c i) j -> p s c j i", i=4),
+                in_=w_raw[c][:].rearrange("p s j (c i) -> p s c j i", i=4),
             )
             return w_bf
 
         def quantise_w(c, w_bf, codes_name):
             wq = sbuf(codes_name, [P, PASSES * P], U32)
             wq_sc = sbuf(f"wq_sc{c}", [P, PASSES * P], U8)
-            nc.vector.quantize_mx(out=wq[:].bitcast(FP8X4), scales=wq_sc[:], in_=w_bf[:].rearrange("p s n j -> p (s n j)"))
+            nc.vector.quantize_mx(out=wq[:].bitcast(FP8X4), scales=wq_sc[:], in_=w_bf.rearrange("p s n j -> p (s n j)"))
             return wq, wq_sc
-
-        def frozen_passes(wq, wq_sc, tokens, token_scales, bank_number):
-            base_ps = bank(bank_number, [P, T])
-            for s in range(PASSES):
-                nc.tensor.matmul_mx(
-                    out=base_ps[:],
-                    lhsT=wq[:, s * P : (s + 1) * P].bitcast(FP8X4),
-                    lhsT_scale=wq_sc[:, s * P : (s + 1) * P],
-                    rhs=tokens[s][:, 0:T].bitcast(FP8X4),
-                    rhs_scale=token_scales[4 * s : P, 0:T],
-                    start=(s == 0),
-                    stop=(s == PASSES - 1),
-                )
-            return base_ps
 
         def to_sbuf(name, source, width):
             staged = sbuf(name, [P, width], F32)
@@ -208,22 +188,20 @@ def tile_moe_dyl_relu_kernel(
         hq_all = sbuf("bw", [P, B, SLOTS], U32)
         hqs = [hq_all[:, m] for m in range(B)]
         hq_sc = [sbuf(f"hq_sc{m}", [P, SLOTS], U8) for m in range(B)]
-        w_bf = round_w(0, "w_bf0")
+        w_bf = [round_w(c, sbuf(name, [P, PASSES, P, 4], BF16)[:]) for c, name in enumerate(("h_pairs3", "w_bf1"))]
         for m in range(B):
             nc.vector.quantize_mx(
                 out=hqs[m].bitcast(FP8X4), scales=hq_sc[m][:], in_=h_words[m][:].rearrange("p j u -> p (j u)").bitcast(BF16)
             )
-        wq = quantise_w(0, w_bf, "wq0")
-        bg_sc.append(sbuf("h_words3", [P, half_cols], U8))
+        bg_sc.append(sbuf("h_words2", [P, half_cols], U8))
         nc.vector.tensor_copy(bg_sc[1][:], b_sc[:].indirect(b_list[:, half_list[1]]))
 
-        halves = [slice(hf * HALF_SLOTS, (hf + 1) * HALF_SLOTS) for hf in range(HALVES)]
-        half_tokens = [token_list[:, hf * HALF_SLOTS // 16 : (hf + 1) * HALF_SLOTS // 16] for hf in range(HALVES)]
-        result = [sbuf(f"result{c}", [P, TOKEN_WINDOW], F32) for c in range(CHUNKS)]
         direct = CHUNKS - 1
         turned_cols = direct * P
-
+        gated = sbuf("gated", [P, T], F32)
+        wq = []
         for hf in range(HALVES):
+            half = slice(hf * HALF_SLOTS, (hf + 1) * HALF_SLOTS)
             y_ps = bank(hf, [P, HALF_SLOTS])
             for b in range(HALF_BLOCKS):
                 m = hf * HALF_BLOCKS + b
@@ -236,58 +214,89 @@ def tile_moe_dyl_relu_kernel(
                     start=True,
                     stop=True,
                 )
-            y_sb = to_sbuf(f"y_direct{hf}", y_ps, HALF_SLOTS)
-            nc.vector.tensor_tensor(result[direct][:].indirect(half_tokens[hf]), y_sb[:], gate_all[:, halves[hf]], MULT)
+            nc.vector.tensor_tensor(gated[:, half], y_ps[:], gate_all[:, half], MULT)
+            wq.append(quantise_w(hf, w_bf[hf], f"wq{hf}"))
 
-        pieces = {}
+        def scatter(buffer_name, values):
+            window = sbuf(buffer_name, [P, TOKEN_WINDOW], F32)
+            nc.vector.tensor_copy(window[:].indirect(token_list[:]), values[:])
+            return window
 
-        def gated_pieces(hf):
-            gy = []
-            for b in range(HALF_BLOCKS):
-                m = hf * HALF_BLOCKS + b
-                y_ps = bank(4 + m, [P, turned_cols])
-                for first, stop in ((0, 2 * P), (2 * P, turned_cols)):
+        routed = scatter("h_pairs3", gated)
+
+        gy = []
+        for m in range(B):
+            hf, b = divmod(m, HALF_BLOCKS)
+            y_ps = bank(4 + m, [P, turned_cols])
+            for first, stop in ((0, 2 * P), (2 * P, turned_cols)):
+                nc.tensor.matmul_mx(
+                    out=y_ps[:, first:stop],
+                    lhsT=hqs[m].bitcast(FP8X4),
+                    lhsT_scale=hq_sc[m][:],
+                    rhs=bgs[m][:, first:stop].bitcast(FP8X4),
+                    rhs_scale=bg_sc[hf][B_ROW:P, b * N + first : b * N + stop],
+                    start=True,
+                    stop=True,
+                )
+            gy.append(sbuf(f"gy{m}", [P, turned_cols], F32))
+            nc.scalar.activation(out=gy[m][:], in_=y_ps[:], func=COPY, scale=gate_col[:, m : m + 1])
+
+        def summed_chunk(c):
+            codes, scales = wq[c]
+            base_ps = bank(2, [P, B * P])
+            for m in range(B):
+                slots = slice(m * SLOTS, (m + 1) * SLOTS)
+                for s in range(PASSES):
                     nc.tensor.matmul_mx(
-                        out=y_ps[:, first:stop],
-                        lhsT=hqs[m].bitcast(FP8X4),
-                        lhsT_scale=hq_sc[m][:],
-                        rhs=bgs[m][:, first:stop].bitcast(FP8X4),
-                        rhs_scale=bg_sc[hf][B_ROW:P, b * N + first : b * N + stop],
-                        start=True,
-                        stop=True,
+                        out=base_ps[:, m * P : (m + 1) * P],
+                        lhsT=xg[s][:, slots].bitcast(FP8X4),
+                        lhsT_scale=xg_sc[4 * s : P, slots],
+                        rhs=codes[:, s * P : (s + 1) * P].bitcast(FP8X4),
+                        rhs_scale=scales[:, s * P : (s + 1) * P],
+                        start=(s == 0),
+                        stop=(s == PASSES - 1),
                     )
-                gy.append(sbuf(f"gy{m}", [P, turned_cols], F32))
-                nc.scalar.activation(out=gy[b][:], in_=y_ps[:], func=COPY, scale=gate_col[:, m : m + 1])
-            for c in range(direct):
-                pieces[c, hf] = bank(PIECE_BANK[c][hf], [P, HALF_SLOTS])
-                for b in range(HALF_BLOCKS):
-                    nc.tensor.transpose(pieces[c, hf][:, b * SLOTS : (b + 1) * SLOTS], gy[b][:, c * P : (c + 1) * P], ident[:])
+            base = to_sbuf(f"base{c}", base_ps, B * P)
+            total_ps = bank(TOTAL_BANK[c], [P, T])
+            terms = [(m, gy[m][:, c * P : (c + 1) * P]) for m in range(B)]
+            terms = terms + [(m, base[:, m * P : (m + 1) * P]) for m in range(B)]
+            for i, (m, term) in enumerate(terms):
+                nc.tensor.matmul(
+                    total_ps[:, m * SLOTS : (m + 1) * SLOTS],
+                    lhsT=term,
+                    rhs=ident[:],
+                    is_transpose=True,
+                    start=(i == 0),
+                    stop=(i == len(terms) - 1),
+                )
+            return to_sbuf(f"total{c}", total_ps, T)
 
-        gated_pieces(0)
-        for c in range(direct):
-            if c == direct - 1:
-                last_ps = frozen_passes(*wq, xw, xs, BASE_BANK[c])
-            else:
-                base = to_sbuf(f"base{c}", frozen_passes(*wq, xg, xg_sc, BASE_BANK[c]), T)
-            for hf in range(HALVES):
-                gated = to_sbuf("w_raw1" if (c, hf) == (1, 1) else f"gated{c}_{hf}", pieces[c, hf], HALF_SLOTS)
-                if c == direct - 1:
-                    nc.vector.tensor_copy(result[c][:].indirect(half_tokens[hf]), gated[:])
-                else:
-                    nc.vector.tensor_tensor(result[c][:].indirect(half_tokens[hf]), gated[:], base[:, halves[hf]], ADD)
-                if (c, hf) == (0, 0):
-                    gated_pieces(1)
-                if hf == 0 and c + 1 < direct:
-                    wq = quantise_w(c + 1, round_w(c + 1, "gy1"), f"wq{c + 1}")
-                if (c, hf) == (0, 1):
-                    direct_ps = frozen_passes(*quantise_w(direct, round_w(direct, "gy1"), "wq3"), xw, xs, BASE_BANK[direct])
-                if (c, hf) == (1, 1):
-                    total = sbuf("total", [P, T], F32)
-                    nc.vector.tensor_tensor(total[:], direct_ps[:], result[direct][:, 0:T], ADD)
-                    nc.sync.dma_start(out=out[turned_cols:N, :], in_=total[:])
-            if c == direct - 1:
-                last = sbuf("last", [P, T], F32)
-                nc.vector.tensor_tensor(last[:], last_ps[:], result[c][:, 0:T], ADD)
-                nc.sync.dma_start(out=out[c * P : (c + 1) * P, :], in_=last[:])
-            else:
-                nc.sync.dma_start(out=out[c * P : (c + 1) * P, :], in_=result[c][:, 0:T])
+        def store(c, values):
+            nc.sync.dma_start(out=out[c * P : (c + 1) * P, :], in_=values[:, 0:T])
+
+        result = {}
+        result[0] = scatter("result0", summed_chunk(0))
+        store(0, result[0])
+        total = summed_chunk(1)
+        w_bf_late = sbuf("base0", [P, 2, PASSES, P, 4], BF16)
+        wq.append(quantise_w(2, round_w(2, w_bf_late[:, 0]), "wq2"))
+        codes, scales = quantise_w(direct, round_w(direct, w_bf_late[:, 1]), "wq3")
+        result[1] = scatter("base0", total)
+        store(1, result[1])
+        total = summed_chunk(2)
+        direct_ps = bank(2, [P, T])
+        for s in range(PASSES):
+            nc.tensor.matmul_mx(
+                out=direct_ps[:],
+                lhsT=codes[:, s * P : (s + 1) * P].bitcast(FP8X4),
+                lhsT_scale=scales[:, s * P : (s + 1) * P],
+                rhs=xw[s][:, 0:T].bitcast(FP8X4),
+                rhs_scale=xs[4 * s : P, 0:T],
+                start=(s == 0),
+                stop=(s == PASSES - 1),
+            )
+        summed = sbuf("summed", [P, T], F32)
+        nc.vector.tensor_tensor(summed[:], direct_ps[:], routed[:, 0:T], ADD)
+        store(direct, summed)
+        result[2] = scatter("result2", total)
+        store(2, result[2])

@@ -198,10 +198,8 @@ def tile_moe_dyl_relu_kernel(
 
         direct = CHUNKS - 1
         turned_cols = direct * P
-        gated = sbuf("gated", [P, T], F32)
-        wq = []
-        for hf in range(HALVES):
-            half = slice(hf * HALF_SLOTS, (hf + 1) * HALF_SLOTS)
+
+        def direct_half(hf):
             y_ps = bank(hf, [P, HALF_SLOTS])
             for b in range(HALF_BLOCKS):
                 m = hf * HALF_BLOCKS + b
@@ -214,15 +212,17 @@ def tile_moe_dyl_relu_kernel(
                     start=True,
                     stop=True,
                 )
-            nc.vector.tensor_tensor(gated[:, half], y_ps[:], gate_all[:, half], MULT)
-            wq.append(quantise_w(hf, w_bf[hf], f"wq{hf}"))
+            return y_ps
 
-        def scatter(buffer_name, values):
-            window = sbuf(buffer_name, [P, TOKEN_WINDOW], F32)
-            nc.vector.tensor_copy(window[:].indirect(token_list[:]), values[:])
-            return window
-
-        routed = scatter("h_pairs3", gated)
+        half_tokens = [token_list[:, hf * HALF_SLOTS // 16 : (hf + 1) * HALF_SLOTS // 16] for hf in range(HALVES)]
+        gated = sbuf("gated", [P, HALF_SLOTS], F32)
+        nc.vector.tensor_tensor(gated[:], direct_half(0)[:], gate_all[:, 0:HALF_SLOTS], MULT)
+        wq = [quantise_w(0, w_bf[0], "wq0")]
+        routed = sbuf("h_words3", [P, TOKEN_WINDOW], F32)
+        nc.vector.tensor_copy(routed[:].indirect(half_tokens[0]), gated[:])
+        wq.append(quantise_w(1, w_bf[1], "wq1"))
+        y_sb = to_sbuf("y_direct", direct_half(1), HALF_SLOTS)
+        nc.vector.tensor_tensor(routed[:].indirect(half_tokens[1]), y_sb[:], gate_all[:, HALF_SLOTS:T], MULT)
 
         gy = []
         for m in range(B):
@@ -241,62 +241,44 @@ def tile_moe_dyl_relu_kernel(
             gy.append(sbuf(f"gy{m}", [P, turned_cols], F32))
             nc.scalar.activation(out=gy[m][:], in_=y_ps[:], func=COPY, scale=gate_col[:, m : m + 1])
 
-        def summed_chunk(c):
-            codes, scales = wq[c]
-            base_ps = bank(2, [P, B * P])
-            for m in range(B):
-                slots = slice(m * SLOTS, (m + 1) * SLOTS)
-                for s in range(PASSES):
-                    nc.tensor.matmul_mx(
-                        out=base_ps[:, m * P : (m + 1) * P],
-                        lhsT=xg[s][:, slots].bitcast(FP8X4),
-                        lhsT_scale=xg_sc[4 * s : P, slots],
-                        rhs=codes[:, s * P : (s + 1) * P].bitcast(FP8X4),
-                        rhs_scale=scales[:, s * P : (s + 1) * P],
-                        start=(s == 0),
-                        stop=(s == PASSES - 1),
-                    )
-            base = to_sbuf(f"base{c}", base_ps, B * P)
-            total_ps = bank(TOTAL_BANK[c], [P, T])
-            terms = [(m, gy[m][:, c * P : (c + 1) * P]) for m in range(B)]
-            terms = terms + [(m, base[:, m * P : (m + 1) * P]) for m in range(B)]
-            for i, (m, term) in enumerate(terms):
-                nc.tensor.matmul(
-                    total_ps[:, m * SLOTS : (m + 1) * SLOTS],
-                    lhsT=term,
-                    rhs=ident[:],
-                    is_transpose=True,
-                    start=(i == 0),
-                    stop=(i == len(terms) - 1),
+        def frozen_passes(codes, scales, tokens, token_scales):
+            base_ps = bank(2, [P, T])
+            for s in range(PASSES):
+                nc.tensor.matmul_mx(
+                    out=base_ps[:],
+                    lhsT=codes[:, s * P : (s + 1) * P].bitcast(FP8X4),
+                    lhsT_scale=scales[:, s * P : (s + 1) * P],
+                    rhs=tokens[s][:, 0:T].bitcast(FP8X4),
+                    rhs_scale=token_scales[4 * s : P, 0:T],
+                    start=(s == 0),
+                    stop=(s == PASSES - 1),
                 )
-            return to_sbuf(f"total{c}", total_ps, T)
+            return base_ps
+
+        def terms(c):
+            turned_ps = bank(TOTAL_BANK[c], [P, T])
+            for m in range(B):
+                nc.tensor.transpose(turned_ps[:, m * SLOTS : (m + 1) * SLOTS], gy[m][:, c * P : (c + 1) * P], ident[:])
+            return to_sbuf(f"base{c}", frozen_passes(*wq[c], xg, xg_sc), T), to_sbuf(f"gated{c}", turned_ps, T)
 
         def store(c, values):
             nc.sync.dma_start(out=out[c * P : (c + 1) * P, :], in_=values[:, 0:T])
 
         result = {}
-        result[0] = scatter("result0", summed_chunk(0))
-        store(0, result[0])
-        total = summed_chunk(1)
-        w_bf_late = sbuf("base0", [P, 2, PASSES, P, 4], BF16)
+
+        def scatter(c, buffer_name, base, gated_rows):
+            result[c] = sbuf(buffer_name, [P, 2 * T], F32)
+            nc.vector.tensor_tensor(result[c][:].indirect(token_list[:]), gated_rows[:], base[:], ADD)
+            store(c, result[c])
+
+        scatter(0, "result0", *terms(0))
+        second = terms(1)
+        w_bf_late = sbuf("gy3", [P, 2, PASSES, P, 4], BF16)
         wq.append(quantise_w(2, round_w(2, w_bf_late[:, 0]), "wq2"))
-        codes, scales = quantise_w(direct, round_w(direct, w_bf_late[:, 1]), "wq3")
-        result[1] = scatter("base0", total)
-        store(1, result[1])
-        total = summed_chunk(2)
-        direct_ps = bank(2, [P, T])
-        for s in range(PASSES):
-            nc.tensor.matmul_mx(
-                out=direct_ps[:],
-                lhsT=codes[:, s * P : (s + 1) * P].bitcast(FP8X4),
-                lhsT_scale=scales[:, s * P : (s + 1) * P],
-                rhs=xw[s][:, 0:T].bitcast(FP8X4),
-                rhs_scale=xs[4 * s : P, 0:T],
-                start=(s == 0),
-                stop=(s == PASSES - 1),
-            )
+        wq.append(quantise_w(direct, round_w(direct, w_bf_late[:, 1]), "wq3"))
+        scatter(1, "gy3", *second)
+        third = terms(2)
         summed = sbuf("summed", [P, T], F32)
-        nc.vector.tensor_tensor(summed[:], direct_ps[:], routed[:, 0:T], ADD)
+        nc.vector.tensor_tensor(summed[:], frozen_passes(*wq[direct], xw, xs)[:], routed[:, 0:T], ADD)
         store(direct, summed)
-        result[2] = scatter("result2", total)
-        store(2, result[2])
+        scatter(2, "result2", *third)

@@ -92,13 +92,13 @@ def tile_moe_dyl_relu_kernel(
         nc.sync.dma_start(token_list[:], offs)
         nc.sync.dma_start(out=xw[0][:, 0:T], in_=words_of(x_words[0]))
         nc.sync.dma_start(out=xw[1][:, 0:T], in_=words_of(x_words[1]))
-        nc.sync.dma_start(b_list[:], offs3)
         load_scales(nc, xs, x_scales, T)
-        load_scale_rows(nc, b_sc, B_ROW, wb_scales[0])
         nc.sync.dma_start(a_list[:], offs2)
         for s in range(PASSES):
             load_scale_rows(nc, a_sc, 4 * s, wa_scales[s])
         nc.sync.dma_start(out=aw[0][:], in_=words_of(wa_words[0]))
+        nc.sync.dma_start(b_list[:], offs3)
+        load_scale_rows(nc, b_sc, B_ROW, wb_scales[0])
         nc.sync.dma_start(out=gate_rows[0:B, :], in_=gate[0].rearrange("(m j) -> m j", m=B))
         nc.sync.dma_start(out=aw[1][:], in_=words_of(wa_words[1]))
         nc.sync.dma_start(out=bw[:], in_=words_of(wb_words[0]))
@@ -115,8 +115,6 @@ def tile_moe_dyl_relu_kernel(
             nc.vector.tensor_copy(xg[s][:], xw[s][:].bitcast(U32).indirect(token_list[:]))
         xg_sc = sbuf("xg_sc", [P, T], U8)
         nc.vector.tensor_copy(xg_sc[:], xs[:].indirect(token_list[:]))
-        bg_sc = [sbuf("bg_sc0", [P, half_cols], U8)]
-        nc.vector.tensor_copy(bg_sc[0][:], b_sc[:].indirect(b_list[:, half_list[0]]))
         ag_sc = [sbuf(f"ag_sc{hf}", [P, half_cols], U8) for hf in range(HALVES)]
         for hf in range(HALVES):
             nc.vector.tensor_copy(ag_sc[hf][:], a_sc[:].indirect(a_list[:, half_list[hf]]))
@@ -143,6 +141,8 @@ def tile_moe_dyl_relu_kernel(
         ag0 = [sbuf(f"ag0_{hf}", [P, half_cols], U32) for hf in range(HALVES)]
         for hf in range(HALVES):
             nc.vector.tensor_copy(ag0[hf][:], aw[0][:].bitcast(U32).indirect(a_list[:, half_list[hf]]))
+        bg_sc = [sbuf("bg_sc0", [P, half_cols], U8)]
+        nc.vector.tensor_copy(bg_sc[0][:], b_sc[:].indirect(b_list[:, half_list[0]]))
         ag1 = [sbuf(f"ag1_{m}", [P, H], U32) for m in range(B)]
         for m in range(B):
             nc.vector.tensor_copy(ag1[m][:], aw[1][:].bitcast(U32).indirect(a_list[:, block_list[m]]))
@@ -278,7 +278,37 @@ def tile_moe_dyl_relu_kernel(
         wq.append(quantise_w(direct, round_w(direct, w_bf_late[:, 1]), "wq3"))
         scatter(1, "gy3", *second)
         third = terms(2)
-        summed = sbuf("summed", [P, T], F32)
-        nc.vector.tensor_tensor(summed[:], frozen_passes(*wq[direct], xw, xs)[:], routed[:, 0:T], ADD)
-        store(direct, summed)
         scatter(2, "result2", *third)
+
+        routed_ps = bank(TOTAL_BANK[1], [P, T])
+        for tb in range(T // P):
+            tokens = slice(tb * P, (tb + 1) * P)
+            nc.tensor.transpose(routed_ps[:, tokens], routed[:, tokens], ident[:])
+        base_ps = bank(7, [P, T])
+        codes, scales = wq[direct]
+        for tb in range(T // P):
+            tokens = slice(tb * P, (tb + 1) * P)
+            for s in range(PASSES):
+                nc.tensor.matmul_mx(
+                    out=base_ps[:, tokens],
+                    lhsT=xw[s][:, tokens].bitcast(FP8X4),
+                    lhsT_scale=xs[4 * s : P, tokens],
+                    rhs=codes[:, s * P : (s + 1) * P].bitcast(FP8X4),
+                    rhs_scale=scales[:, s * P : (s + 1) * P],
+                    start=(s == 0),
+                    stop=(s == PASSES - 1),
+                )
+        turned_terms = [to_sbuf("routed_t", routed_ps, T), to_sbuf("base_t", base_ps, T)]
+        sum_ps = bank(TOTAL_BANK[0], [P, T])
+        for i, term in enumerate(turned_terms):
+            for tb in range(T // P):
+                tokens = slice(tb * P, (tb + 1) * P)
+                nc.tensor.matmul(
+                    sum_ps[:, tokens],
+                    lhsT=term[:, tokens],
+                    rhs=ident[:],
+                    is_transpose=True,
+                    start=(i == 0 and tb == 0),
+                    stop=(i == 1 and tb == T // P - 1),
+                )
+        nc.scalar.dma_start(out=out[turned_cols:N, :], in_=to_sbuf("summed", sum_ps, T)[:])

@@ -34,9 +34,12 @@ def words_of(dram_pass):
     return dram_pass.rearrange("p c d -> p (c d)").bitcast(I32)
 
 
-def load_scale_rows(nc, tile, first_row, dram_pass):
+def load_scale_rows(nc, tile, first_row, dram_scales):
     for r in range(4):
-        nc.sync.dma_start(out=tile[first_row + r : P : 32, :].bitcast(I32), in_=dram_pass[r:16:4, :].bitcast(I32))
+        for s in range(dram_scales.shape[0]):
+            nc.sync.dma_start(
+                out=tile[first_row + 4 * s + r : P : 32, :].bitcast(I32), in_=dram_scales[s, r:16:4, :].bitcast(I32)
+            )
 
 
 def load_scales(nc, tile, dram_scales, width):
@@ -89,16 +92,15 @@ def tile_moe_dyl_relu_kernel(
             rows = w[512 * s : 512 * (s + 1), c * P : (c + 1) * P]
             nc.sync.dma_start(out=w_raw[c][:, s], in_=rows.rearrange("(p j) n -> p j n", j=4))
 
-        nc.sync.dma_start(token_list[:], offs)
         nc.sync.dma_start(out=xw[0][:, 0:T], in_=words_of(x_words[0]))
+        nc.sync.dma_start(token_list[:], offs)
         nc.sync.dma_start(out=xw[1][:, 0:T], in_=words_of(x_words[1]))
         load_scales(nc, xs, x_scales, T)
         nc.sync.dma_start(a_list[:], offs2)
-        for s in range(PASSES):
-            load_scale_rows(nc, a_sc, 4 * s, wa_scales[s])
+        load_scale_rows(nc, a_sc, 0, wa_scales)
         nc.sync.dma_start(out=aw[0][:], in_=words_of(wa_words[0]))
         nc.sync.dma_start(b_list[:], offs3)
-        load_scale_rows(nc, b_sc, B_ROW, wb_scales[0])
+        load_scale_rows(nc, b_sc, B_ROW, wb_scales)
         nc.sync.dma_start(out=gate_rows[0:B, :], in_=gate[0].rearrange("(m j) -> m j", m=B))
         nc.sync.dma_start(out=aw[1][:], in_=words_of(wa_words[1]))
         nc.sync.dma_start(out=bw[:], in_=words_of(wb_words[0]))

@@ -27,7 +27,6 @@ HALF_SLOTS = HALF_BLOCKS * SLOTS
 TOKEN_WINDOW = 704
 CHUNKS = N // P
 B_ROW = 8
-TOTAL_BANK = (3, 0, 1)
 
 
 def words_of(dram_pass):
@@ -128,23 +127,23 @@ def tile_moe_dyl_relu_kernel(
             )
             return w_bf
 
-        def quantise_w(c, w_bf, codes_name):
-            wq = sbuf(codes_name, [P, PASSES * P], U32)
-            wq_sc = sbuf(f"wq_sc{c}", [P, PASSES * P], U8)
-            nc.vector.quantize_mx(out=wq[:].bitcast(FP8X4), scales=wq_sc[:], in_=w_bf.rearrange("p s n j -> p (s n j)"))
-            return wq, wq_sc
+        def quantise_w(c, w_bf):
+            codes = sbuf(f"wq{c}", [P, PASSES * P], U32)
+            scales = sbuf(f"wq_sc{c}", [P, PASSES * P], U8)
+            nc.vector.quantize_mx(out=codes[:].bitcast(FP8X4), scales=scales[:], in_=w_bf.rearrange("p s n j -> p (s n j)"))
+            return codes, scales
 
         def to_sbuf(name, source, width):
             staged = sbuf(name, [P, width], F32)
             nc.scalar.copy(out=staged[:], in_=source[:])
             return staged
 
-
         ag0 = [sbuf(f"ag0_{hf}", [P, half_cols], U32) for hf in range(HALVES)]
         for hf in range(HALVES):
             nc.vector.tensor_copy(ag0[hf][:], aw[0][:].bitcast(U32).indirect(a_list[:, half_list[hf]]))
-        bg_sc = [sbuf("bg_sc0", [P, half_cols], U8)]
-        nc.vector.tensor_copy(bg_sc[0][:], b_sc[:].indirect(b_list[:, half_list[0]]))
+        early_cols = (B - 1) * N
+        bg_sc = sbuf("bg_sc", [P, early_cols], U8)
+        nc.vector.tensor_copy(bg_sc[:], b_sc[:].indirect(b_list[:, 0 : early_cols // 16]))
         ag1 = [sbuf(f"ag1_{m}", [P, H], U32) for m in range(B)]
         for m in range(B):
             nc.vector.tensor_copy(ag1[m][:], aw[1][:].bitcast(U32).indirect(a_list[:, block_list[m]]))
@@ -190,127 +189,128 @@ def tile_moe_dyl_relu_kernel(
         hq_all = sbuf("bw", [P, B, SLOTS], U32)
         hqs = [hq_all[:, m] for m in range(B)]
         hq_sc = [sbuf(f"hq_sc{m}", [P, SLOTS], U8) for m in range(B)]
-        w_bf = [round_w(c, sbuf(name, [P, PASSES, P, 4], BF16)[:]) for c, name in enumerate(("h_pairs3", "w_bf1"))]
+        w_shape = [P, PASSES, P, 4]
+        w_bf_first = round_w(0, sbuf("h_pairs3", w_shape, BF16)[:])
         for m in range(B):
             nc.vector.quantize_mx(
                 out=hqs[m].bitcast(FP8X4), scales=hq_sc[m][:], in_=h_words[m][:].rearrange("p j u -> p (j u)").bitcast(BF16)
             )
-        bg_sc.append(sbuf("h_words2", [P, half_cols], U8))
-        nc.vector.tensor_copy(bg_sc[1][:], b_sc[:].indirect(b_list[:, half_list[1]]))
+        bg_sc_last = sbuf("h_words2", [P, N], U8)
+        nc.vector.tensor_copy(bg_sc_last[:], b_sc[:].indirect(b_list[:, block_list[B - 1]]))
+        b_scales = [bg_sc[:, m * N : (m + 1) * N] for m in range(B - 1)] + [bg_sc_last[:]]
+        wq = {0: quantise_w(0, w_bf_first)}
 
-        direct = CHUNKS - 1
-        turned_cols = direct * P
-
-        def direct_half(hf):
-            y_ps = bank(hf, [P, HALF_SLOTS])
-            for b in range(HALF_BLOCKS):
-                m = hf * HALF_BLOCKS + b
-                nc.tensor.matmul_mx(
-                    out=y_ps[:, b * SLOTS : (b + 1) * SLOTS],
-                    lhsT=bgs[m][:, turned_cols:N].bitcast(FP8X4),
-                    lhsT_scale=bg_sc[hf][B_ROW:P, b * N + turned_cols : (b + 1) * N],
-                    rhs=hqs[m].bitcast(FP8X4),
-                    rhs_scale=hq_sc[m][:],
-                    start=True,
-                    stop=True,
-                )
-            return y_ps
-
-        half_tokens = [token_list[:, hf * HALF_SLOTS // 16 : (hf + 1) * HALF_SLOTS // 16] for hf in range(HALVES)]
-        gated = sbuf("gated", [P, HALF_SLOTS], F32)
-        nc.vector.tensor_tensor(gated[:], direct_half(0)[:], gate_all[:, 0:HALF_SLOTS], MULT)
-        wq = [quantise_w(0, w_bf[0], "wq0")]
-        routed = sbuf("h_words3", [P, TOKEN_WINDOW], F32)
-        nc.vector.tensor_copy(routed[:].indirect(half_tokens[0]), gated[:])
-        wq.append(quantise_w(1, w_bf[1], "wq1"))
-        y_sb = to_sbuf("y_direct", direct_half(1), HALF_SLOTS)
-        nc.vector.tensor_tensor(routed[:].indirect(half_tokens[1]), y_sb[:], gate_all[:, HALF_SLOTS:T], MULT)
+        turned_chunks, direct_chunks = (0, 1), (2, 3)
+        turned_cols = len(turned_chunks) * P
+        routed = {c: sbuf(f"routed{c}", [P, TOKEN_WINDOW], F32) for c in direct_chunks}
+        for hf in range(HALVES):
+            half = slice(hf * HALF_SLOTS, (hf + 1) * HALF_SLOTS)
+            for i, c in enumerate(direct_chunks):
+                y_ps = bank(2 * hf + i, [P, HALF_SLOTS])
+                for b in range(HALF_BLOCKS):
+                    m = hf * HALF_BLOCKS + b
+                    nc.tensor.matmul_mx(
+                        out=y_ps[:, b * SLOTS : (b + 1) * SLOTS],
+                        lhsT=bgs[m][:, c * P : (c + 1) * P].bitcast(FP8X4),
+                        lhsT_scale=b_scales[m][B_ROW:P, c * P : (c + 1) * P],
+                        rhs=hqs[m].bitcast(FP8X4),
+                        rhs_scale=hq_sc[m][:],
+                        start=True,
+                        stop=True,
+                    )
+                y_sb = to_sbuf(f"y_direct{c}_{hf}", y_ps, HALF_SLOTS)
+                tokens = token_list[:, half.start // 16 : half.stop // 16]
+                nc.vector.tensor_tensor(routed[c][:].indirect(tokens), y_sb[:], gate_all[:, half], MULT)
+                w_chunk = len(direct_chunks) * hf + i
+                if w_chunk in (1, 2):
+                    wq[w_chunk] = quantise_w(w_chunk, round_w(w_chunk, sbuf(f"w_bf{w_chunk}", w_shape, BF16)[:]))
 
         gy = []
         for m in range(B):
-            hf, b = divmod(m, HALF_BLOCKS)
             y_ps = bank(4 + m, [P, turned_cols])
-            for first, stop in ((0, 2 * P), (2 * P, turned_cols)):
-                nc.tensor.matmul_mx(
-                    out=y_ps[:, first:stop],
-                    lhsT=hqs[m].bitcast(FP8X4),
-                    lhsT_scale=hq_sc[m][:],
-                    rhs=bgs[m][:, first:stop].bitcast(FP8X4),
-                    rhs_scale=bg_sc[hf][B_ROW:P, b * N + first : b * N + stop],
-                    start=True,
-                    stop=True,
-                )
+            nc.tensor.matmul_mx(
+                out=y_ps[:],
+                lhsT=hqs[m].bitcast(FP8X4),
+                lhsT_scale=hq_sc[m][:],
+                rhs=bgs[m][:, 0:turned_cols].bitcast(FP8X4),
+                rhs_scale=b_scales[m][B_ROW:P, 0:turned_cols],
+                start=True,
+                stop=True,
+            )
             gy.append(sbuf(f"gy{m}", [P, turned_cols], F32))
             nc.scalar.activation(out=gy[m][:], in_=y_ps[:], func=COPY, scale=gate_col[:, m : m + 1])
 
-        def frozen_passes(codes, scales, tokens, token_scales):
-            base_ps = bank(2, [P, T])
+        def gated_rows(c):
+            turned_ps = bank(c, [P, T])
+            for m in range(B):
+                nc.tensor.transpose(turned_ps[:, m * SLOTS : (m + 1) * SLOTS], gy[m][:, c * P : (c + 1) * P], ident[:])
+            return to_sbuf(f"gated{c}", turned_ps, T)
+
+        def base_rows(c):
+            codes, scales = wq[c]
+            base_ps = bank(2 + c, [P, T])
             for s in range(PASSES):
                 nc.tensor.matmul_mx(
                     out=base_ps[:],
                     lhsT=codes[:, s * P : (s + 1) * P].bitcast(FP8X4),
                     lhsT_scale=scales[:, s * P : (s + 1) * P],
-                    rhs=tokens[s][:, 0:T].bitcast(FP8X4),
-                    rhs_scale=token_scales[4 * s : P, 0:T],
+                    rhs=xg[s][:].bitcast(FP8X4),
+                    rhs_scale=xg_sc[4 * s : P, :],
                     start=(s == 0),
                     stop=(s == PASSES - 1),
                 )
-            return base_ps
+            return to_sbuf(f"base{c}", base_ps, T)
 
-        def terms(c):
-            turned_ps = bank(TOTAL_BANK[c], [P, T])
-            for m in range(B):
-                nc.tensor.transpose(turned_ps[:, m * SLOTS : (m + 1) * SLOTS], gy[m][:, c * P : (c + 1) * P], ident[:])
-            return to_sbuf(f"base{c}", frozen_passes(*wq[c], xg, xg_sc), T), to_sbuf(f"gated{c}", turned_ps, T)
+        def scatter_sum(c, base, gated):
+            result = sbuf(f"result{c}", [P, 2 * T], F32)
+            nc.vector.tensor_tensor(result[:].indirect(token_list[:]), gated[:], base[:], ADD)
+            nc.sync.dma_start(out=out[c * P : (c + 1) * P, :], in_=result[:, 0:T])
 
-        def store(c, values):
-            nc.sync.dma_start(out=out[c * P : (c + 1) * P, :], in_=values[:, 0:T])
-
-        result = {}
-
-        def scatter(c, buffer_name, base, gated_rows):
-            result[c] = sbuf(buffer_name, [P, 2 * T], F32)
-            nc.vector.tensor_tensor(result[c][:].indirect(token_list[:]), gated_rows[:], base[:], ADD)
-            store(c, result[c])
-
-        scatter(0, "result0", *terms(0))
-        second = terms(1)
-        w_bf_late = sbuf("gy3", [P, 2, PASSES, P, 4], BF16)
-        wq.append(quantise_w(2, round_w(2, w_bf_late[:, 0]), "wq2"))
-        wq.append(quantise_w(direct, round_w(direct, w_bf_late[:, 1]), "wq3"))
-        scatter(1, "gy3", *second)
-        third = terms(2)
-        scatter(2, "result2", *third)
-
-        routed_ps = bank(TOTAL_BANK[1], [P, T])
-        for tb in range(T // P):
-            tokens = slice(tb * P, (tb + 1) * P)
-            nc.tensor.transpose(routed_ps[:, tokens], routed[:, tokens], ident[:])
-        base_ps = bank(7, [P, T])
-        codes, scales = wq[direct]
-        for tb in range(T // P):
-            tokens = slice(tb * P, (tb + 1) * P)
-            for s in range(PASSES):
-                nc.tensor.matmul_mx(
-                    out=base_ps[:, tokens],
-                    lhsT=xw[s][:, tokens].bitcast(FP8X4),
-                    lhsT_scale=xs[4 * s : P, tokens],
-                    rhs=codes[:, s * P : (s + 1) * P].bitcast(FP8X4),
-                    rhs_scale=scales[:, s * P : (s + 1) * P],
-                    start=(s == 0),
-                    stop=(s == PASSES - 1),
-                )
-        turned_terms = [to_sbuf("routed_t", routed_ps, T), to_sbuf("base_t", base_ps, T)]
-        sum_ps = bank(TOTAL_BANK[0], [P, T])
-        for i, term in enumerate(turned_terms):
+        def routed_turned(c):
+            routed_ps = bank(c - 2, [P, T])
             for tb in range(T // P):
                 tokens = slice(tb * P, (tb + 1) * P)
-                nc.tensor.matmul(
-                    sum_ps[:, tokens],
-                    lhsT=term[:, tokens],
-                    rhs=ident[:],
-                    is_transpose=True,
-                    start=(i == 0 and tb == 0),
-                    stop=(i == 1 and tb == T // P - 1),
-                )
-        nc.scalar.dma_start(out=out[turned_cols:N, :], in_=to_sbuf("summed", sum_ps, T)[:])
+                nc.tensor.transpose(routed_ps[:, tokens], routed[c][:, tokens], ident[:])
+            return to_sbuf(f"routed_t{c}", routed_ps, T)
+
+        def base_turned(c):
+            base_ps = bank(c + 2, [P, T])
+            codes, scales = wq[c]
+            for tb in range(T // P):
+                tokens = slice(tb * P, (tb + 1) * P)
+                for s in range(PASSES):
+                    nc.tensor.matmul_mx(
+                        out=base_ps[:, tokens],
+                        lhsT=xw[s][:, tokens].bitcast(FP8X4),
+                        lhsT_scale=xs[4 * s : P, tokens],
+                        rhs=codes[:, s * P : (s + 1) * P].bitcast(FP8X4),
+                        rhs_scale=scales[:, s * P : (s + 1) * P],
+                        start=(s == 0),
+                        stop=(s == PASSES - 1),
+                    )
+            return to_sbuf(f"base_t{c}", base_ps, T)
+
+        def finish_direct(c, *turned_terms):
+            sum_ps = bank(c, [P, T])
+            for i, term in enumerate(turned_terms):
+                for tb in range(T // P):
+                    tokens = slice(tb * P, (tb + 1) * P)
+                    nc.tensor.matmul(
+                        sum_ps[:, tokens],
+                        lhsT=term[:, tokens],
+                        rhs=ident[:],
+                        is_transpose=True,
+                        start=(i == 0 and tb == 0),
+                        stop=(i == 1 and tb == T // P - 1),
+                    )
+            nc.scalar.dma_start(out=out[c * P : (c + 1) * P, :], in_=to_sbuf(f"summed{c}", sum_ps, T)[:])
+
+        first_base = base_rows(0)
+        wq[3] = quantise_w(3, round_w(3, sbuf("w_bf3", w_shape, BF16)[:]))
+        scatter_sum(0, first_base, gated_rows(0))
+        second_gated = gated_rows(1)
+        scatter_sum(1, base_rows(1), second_gated)
+        routed_t = [routed_turned(c) for c in direct_chunks]
+        base_t = [base_turned(c) for c in direct_chunks]
+        for i, c in enumerate(direct_chunks):
+            finish_direct(c, routed_t[i], base_t[i])

@@ -75,37 +75,52 @@ def tile_moe_dyl_relu_kernel(
         a_sc = sbuf("a_sc", [P, E * H], U8)
         bw = sbuf("bw", [P, E * N], I32)
         b_sc = sbuf("b_sc", [P, E * N], U8)
-        w_raw = [sbuf(f"w_raw{c}", [P, PASSES, 4, P], F32) for c in range(CHUNKS)]
+        w_raw = [sbuf(f"w_raw{s}", [P, 4, N], F32) for s in range(PASSES)]
         gate_rows = sbuf("gate_rows", [P, SLOTS], F32)
         ident = sbuf("ident", [P, P], F32)
 
         nc.gpsimd.memset(xs[:].bitcast(I32), 0)
         nc.gpsimd.memset(b_sc[:].bitcast(I32), 0)
+        nc.vector.memset(a_sc[:].bitcast(I32), 0)
         for s in range(PASSES):
             nc.vector.memset(xw[s][:, T:TOKEN_WINDOW], 0)
-        nc.vector.memset(a_sc[:].bitcast(I32), 0)
         nc.gpsimd.memset(gate_rows[:], 0.0)
         make_identity(nc, ident[:])
 
-        def load_w(c, s):
-            rows = w[512 * s : 512 * (s + 1), c * P : (c + 1) * P]
-            nc.sync.dma_start(out=w_raw[c][:, s], in_=rows.rearrange("(p j) n -> p j n", j=4))
+        def load_w(s, first, count):
+            rows = w[512 * s : 512 * (s + 1), :].rearrange("(p j) n -> p j n", j=4)
+            nc.sync.dma_start(out=w_raw[s][:, first : first + count], in_=rows[:, first : first + count])
 
+        def scale_row_loads(tile, first_row, dram_scales):
+            return [
+                (tile[first_row + 4 * s + r : P : 32, :].bitcast(I32), dram_scales[s, r:16:4, :].bitcast(I32))
+                for r in range(4)
+                for s in range(dram_scales.shape[0])
+            ]
+
+        def load_all(loads):
+            for target, source in loads:
+                nc.sync.dma_start(out=target, in_=source)
+
+        a_rows = scale_row_loads(a_sc, 0, wa_scales)
+        b_rows = scale_row_loads(b_sc, B_ROW, wb_scales)
         nc.sync.dma_start(out=xw[0][:, 0:T], in_=words_of(x_words[0]))
         nc.sync.dma_start(token_list[:], offs)
         nc.sync.dma_start(out=xw[1][:, 0:T], in_=words_of(x_words[1]))
         load_scales(nc, xs, x_scales, T)
+        load_w(0, 0, 2)
         nc.sync.dma_start(a_list[:], offs2)
-        load_scale_rows(nc, a_sc, 0, wa_scales)
-        nc.sync.dma_start(out=aw[0][:], in_=words_of(wa_words[0]))
+        load_all(a_rows[0:5])
+        load_w(0, 2, 2)
+        load_all(a_rows[5:8])
         nc.sync.dma_start(b_list[:], offs3)
-        load_scale_rows(nc, b_sc, B_ROW, wb_scales)
+        load_all(b_rows[0:2])
+        load_w(1, 0, 4)
+        load_all(b_rows[2:4])
         nc.sync.dma_start(out=gate_rows[0:B, :], in_=gate[0].rearrange("(m j) -> m j", m=B))
+        nc.sync.dma_start(out=aw[0][:], in_=words_of(wa_words[0]))
         nc.sync.dma_start(out=aw[1][:], in_=words_of(wa_words[1]))
         nc.sync.dma_start(out=bw[:], in_=words_of(wb_words[0]))
-        for c in range(CHUNKS):
-            for s in range(PASSES):
-                load_w(c, s)
 
         half_cols = HALF_BLOCKS * H
         half_list = [slice(hf * half_cols // 16, (hf + 1) * half_cols // 16) for hf in range(HALVES)]
@@ -119,44 +134,82 @@ def tile_moe_dyl_relu_kernel(
         ag_sc = [sbuf(f"ag_sc{hf}", [P, half_cols], U8) for hf in range(HALVES)]
         for hf in range(HALVES):
             nc.vector.tensor_copy(ag_sc[hf][:], a_sc[:].indirect(a_list[:, half_list[hf]]))
-
-        def round_w(c, w_bf):
-            nc.scalar.copy(
-                out=w_bf.rearrange("p s (c i) j -> p s c j i", i=4),
-                in_=w_raw[c][:].rearrange("p s j (c i) -> p s c j i", i=4),
-            )
-            return w_bf
-
-        def quantise_w(c, w_bf):
-            codes = sbuf(f"wq{c}", [P, PASSES * P], U32)
-            scales = sbuf(f"wq_sc{c}", [P, PASSES * P], U8)
-            nc.vector.quantize_mx(out=codes[:].bitcast(FP8X4), scales=scales[:], in_=w_bf.rearrange("p s n j -> p (s n j)"))
-            return codes, scales
-
-        def to_sbuf(name, source, width):
-            staged = sbuf(name, [P, width], F32)
-            nc.scalar.copy(out=staged[:], in_=source[:])
-            return staged
-
-        ag0 = [sbuf(f"ag0_{hf}", [P, half_cols], U32) for hf in range(HALVES)]
-        for hf in range(HALVES):
-            nc.vector.tensor_copy(ag0[hf][:], aw[0][:].bitcast(U32).indirect(a_list[:, half_list[hf]]))
         early_cols = (B - 1) * N
         bg_sc = sbuf("bg_sc", [P, early_cols], U8)
         nc.vector.tensor_copy(bg_sc[:], b_sc[:].indirect(b_list[:, 0 : early_cols // 16]))
-        ag1 = [sbuf(f"ag1_{m}", [P, H], U32) for m in range(B)]
-        for m in range(B):
-            nc.vector.tensor_copy(ag1[m][:], aw[1][:].bitcast(U32).indirect(a_list[:, block_list[m]]))
+        b_scales = [bg_sc[:, m * N : (m + 1) * N] for m in range(B - 1)]
 
-        gate_ps = bank(2, [P, P])
+        wq, wq_sc = [], []
+        for s in range(PASSES):
+            w_bf = sbuf(f"w_bf{s}", [P, N, 4], BF16)
+            nc.scalar.copy(
+                out=w_bf[:].rearrange("p (c i) j -> p c j i", i=4),
+                in_=w_raw[s][:].rearrange("p j (c i) -> p c j i", i=4),
+            )
+            wq.append(sbuf(f"wq{s}", [P, N], U32))
+            wq_sc.append(sbuf(f"wq_sc{s}", [P, N], U8))
+            nc.vector.quantize_mx(out=wq[s][:].bitcast(FP8X4), scales=wq_sc[s][:], in_=w_bf[:].rearrange("p n j -> p (n j)"))
+
+        def to_sbuf(name, source, shape):
+            staged = sbuf(name, shape, F32)
+            nc.scalar.copy(out=staged[:], in_=source[:])
+            return staged
+
+        gate_ps = bank(4, [P, P])
         nc.tensor.transpose(gate_ps[:], gate_rows[:], ident[:])
         gate_col = sbuf("gate_col", [P, B], F32)
         nc.scalar.copy(out=gate_col[:], in_=gate_ps[:, 0:B])
-        spread_ps = bank(3, [P, B, SLOTS])
+        spread_ps = bank(5, [P, B, SLOTS])
         for m in range(B):
             nc.tensor.transpose(spread_ps[:, m, :], gate_col[:, m : m + 1].to_broadcast([P, P]), ident[:])
         gate_all = sbuf("gate_all", [P, T], F32)
         nc.scalar.copy(out=gate_all[:], in_=spread_ps[:].rearrange("p m j -> p (m j)"))
+
+        turned_chunks, direct_chunks = (0, 1), (2, 3)
+        turned_cols = len(turned_chunks) * P
+
+        base_turned = []
+        for hf in range(HALVES):
+            base_ps = bank(2 + hf, [P, HALF_BLOCKS, turned_cols])
+            for b in range(HALF_BLOCKS):
+                m = hf * HALF_BLOCKS + b
+                slots = slice(m * SLOTS, (m + 1) * SLOTS)
+                for s in range(PASSES):
+                    nc.tensor.matmul_mx(
+                        out=base_ps[:, b, :],
+                        lhsT=xg[s][:, slots].bitcast(FP8X4),
+                        lhsT_scale=xg_sc[4 * s : P, slots],
+                        rhs=wq[s][:, 0:turned_cols].bitcast(FP8X4),
+                        rhs_scale=wq_sc[s][:, 0:turned_cols],
+                        start=(s == 0),
+                        stop=(s == PASSES - 1),
+                    )
+            base_turned.append(to_sbuf(f"base_turned{hf}", base_ps, [P, HALF_BLOCKS, turned_cols]))
+        base_rows = []
+        for i, c in enumerate(direct_chunks):
+            base_ps = bank(i, [P, T])
+            for s in range(PASSES):
+                nc.tensor.matmul_mx(
+                    out=base_ps[:],
+                    lhsT=wq[s][:, c * P : (c + 1) * P].bitcast(FP8X4),
+                    lhsT_scale=wq_sc[s][:, c * P : (c + 1) * P],
+                    rhs=xg[s][:].bitcast(FP8X4),
+                    rhs_scale=xg_sc[4 * s : P, :],
+                    start=(s == 0),
+                    stop=(s == PASSES - 1),
+                )
+            base_rows.append(to_sbuf(f"base_rows{c}", base_ps, [P, T]))
+
+        ag0 = [sbuf(f"ag0_{hf}", [P, half_cols], U32) for hf in range(HALVES)]
+        for hf in range(HALVES):
+            nc.vector.tensor_copy(ag0[hf][:], aw[0][:].bitcast(U32).indirect(a_list[:, half_list[hf]]))
+
+        def gather_a1(m, name):
+            words = sbuf(name, [P, H], U32)
+            nc.vector.tensor_copy(words[:], aw[1][:].bitcast(U32).indirect(a_list[:, block_list[m]]))
+            return words
+
+        ag1 = [gather_a1(m, f"ag1_{m}") for m in range(B - 1)]
 
         h_words = []
         for m in range(B):
@@ -182,135 +235,94 @@ def tile_moe_dyl_relu_kernel(
                 nc.tensor.transpose(turned[:, u, :], pairs[:, u * P : (u + 1) * P], ident[:])
             h_words.append(sbuf(f"h_words{m}", [P, SLOTS, 2], F32))
             nc.scalar.copy(out=h_words[m][:], in_=turned[:].rearrange("p u j -> p j u"))
+            if m == 0:
+                bg_sc_last = sbuf("ag1_0", [P, N], U8)
+                nc.vector.tensor_copy(bg_sc_last[:], b_sc[:].indirect(b_list[:, block_list[B - 1]]))
+                b_scales.append(bg_sc_last[:])
+                ag1.append(gather_a1(B - 1, "h_pairs0"))
 
-        bgs = [sbuf(f"bg{m}", [P, N], U32) for m in range(B)]
+        y_rows = [bank(hf, [P, len(direct_chunks), HALF_SLOTS]) for hf in range(HALVES)]
+        y_turned = []
         for m in range(B):
-            nc.vector.tensor_copy(bgs[m][:], bw[:].bitcast(U32).indirect(b_list[:, block_list[m]]))
-        hq_all = sbuf("bw", [P, B, SLOTS], U32)
-        hqs = [hq_all[:, m] for m in range(B)]
-        hq_sc = [sbuf(f"hq_sc{m}", [P, SLOTS], U8) for m in range(B)]
-        w_shape = [P, PASSES, P, 4]
-        w_bf_first = round_w(0, sbuf("h_pairs3", w_shape, BF16)[:])
-        for m in range(B):
+            hf, b = divmod(m, HALF_BLOCKS)
+            bg = sbuf(f"bg{m}", [P, N], U32)
+            nc.vector.tensor_copy(bg[:], bw[:].bitcast(U32).indirect(b_list[:, block_list[m]]))
+            hq = sbuf(f"hq{m % 2}", [P, SLOTS], U32)
+            hq_sc = sbuf(f"hq_sc{m}", [P, SLOTS], U8)
             nc.vector.quantize_mx(
-                out=hqs[m].bitcast(FP8X4), scales=hq_sc[m][:], in_=h_words[m][:].rearrange("p j u -> p (j u)").bitcast(BF16)
+                out=hq[:].bitcast(FP8X4), scales=hq_sc[:], in_=h_words[m][:].rearrange("p j u -> p (j u)").bitcast(BF16)
             )
-        bg_sc_last = sbuf("h_words2", [P, N], U8)
-        nc.vector.tensor_copy(bg_sc_last[:], b_sc[:].indirect(b_list[:, block_list[B - 1]]))
-        b_scales = [bg_sc[:, m * N : (m + 1) * N] for m in range(B - 1)] + [bg_sc_last[:]]
-        wq = {0: quantise_w(0, w_bf_first)}
-
-        turned_chunks, direct_chunks = (0, 1), (2, 3)
-        turned_cols = len(turned_chunks) * P
-        routed = {c: sbuf(f"routed{c}", [P, TOKEN_WINDOW], F32) for c in direct_chunks}
-        for hf in range(HALVES):
-            half = slice(hf * HALF_SLOTS, (hf + 1) * HALF_SLOTS)
-            for i, c in enumerate(direct_chunks):
-                y_ps = bank(2 * hf + i, [P, HALF_SLOTS])
-                for b in range(HALF_BLOCKS):
-                    m = hf * HALF_BLOCKS + b
-                    nc.tensor.matmul_mx(
-                        out=y_ps[:, b * SLOTS : (b + 1) * SLOTS],
-                        lhsT=bgs[m][:, c * P : (c + 1) * P].bitcast(FP8X4),
-                        lhsT_scale=b_scales[m][B_ROW:P, c * P : (c + 1) * P],
-                        rhs=hqs[m].bitcast(FP8X4),
-                        rhs_scale=hq_sc[m][:],
-                        start=True,
-                        stop=True,
-                    )
-                y_sb = to_sbuf(f"y_direct{c}_{hf}", y_ps, HALF_SLOTS)
-                tokens = token_list[:, half.start // 16 : half.stop // 16]
-                nc.vector.tensor_tensor(routed[c][:].indirect(tokens), y_sb[:], gate_all[:, half], MULT)
-                w_chunk = len(direct_chunks) * hf + i
-                if w_chunk in (1, 2):
-                    wq[w_chunk] = quantise_w(w_chunk, round_w(w_chunk, sbuf(f"w_bf{w_chunk}", w_shape, BF16)[:]))
-
-        gy = []
-        for m in range(B):
-            y_ps = bank(4 + m, [P, turned_cols])
+            y_turned.append(bank(4 + m, [P, turned_cols]))
             nc.tensor.matmul_mx(
-                out=y_ps[:],
-                lhsT=hqs[m].bitcast(FP8X4),
-                lhsT_scale=hq_sc[m][:],
-                rhs=bgs[m][:, 0:turned_cols].bitcast(FP8X4),
+                out=y_turned[m][:],
+                lhsT=hq[:].bitcast(FP8X4),
+                lhsT_scale=hq_sc[:],
+                rhs=bg[:, 0:turned_cols].bitcast(FP8X4),
                 rhs_scale=b_scales[m][B_ROW:P, 0:turned_cols],
                 start=True,
                 stop=True,
             )
-            gy.append(sbuf(f"gy{m}", [P, turned_cols], F32))
-            nc.scalar.activation(out=gy[m][:], in_=y_ps[:], func=COPY, scale=gate_col[:, m : m + 1])
-
-        def gated_rows(c):
-            turned_ps = bank(c, [P, T])
-            for m in range(B):
-                nc.tensor.transpose(turned_ps[:, m * SLOTS : (m + 1) * SLOTS], gy[m][:, c * P : (c + 1) * P], ident[:])
-            return to_sbuf(f"gated{c}", turned_ps, T)
-
-        def base_rows(c):
-            codes, scales = wq[c]
-            base_ps = bank(2 + c, [P, T])
-            for s in range(PASSES):
+            for i, c in enumerate(direct_chunks):
                 nc.tensor.matmul_mx(
-                    out=base_ps[:],
-                    lhsT=codes[:, s * P : (s + 1) * P].bitcast(FP8X4),
-                    lhsT_scale=scales[:, s * P : (s + 1) * P],
-                    rhs=xg[s][:].bitcast(FP8X4),
-                    rhs_scale=xg_sc[4 * s : P, :],
-                    start=(s == 0),
-                    stop=(s == PASSES - 1),
+                    out=y_rows[hf][:, i, b * SLOTS : (b + 1) * SLOTS],
+                    lhsT=bg[:, c * P : (c + 1) * P].bitcast(FP8X4),
+                    lhsT_scale=b_scales[m][B_ROW:P, c * P : (c + 1) * P],
+                    rhs=hq[:].bitcast(FP8X4),
+                    rhs_scale=hq_sc[:],
+                    start=True,
+                    stop=True,
                 )
-            return to_sbuf(f"base{c}", base_ps, T)
 
-        def scatter_sum(c, base, gated):
-            result = sbuf(f"result{c}", [P, 2 * T], F32)
-            nc.vector.tensor_tensor(result[:].indirect(token_list[:]), gated[:], base[:], ADD)
-            nc.sync.dma_start(out=out[c * P : (c + 1) * P, :], in_=result[:, 0:T])
+        result = {c: sbuf(f"result{c}", [P, T], F32) for c in turned_chunks}
+        groups = ((0,), (1,), (2, 3))
 
-        def routed_turned(c):
-            routed_ps = bank(c - 2, [P, T])
-            for tb in range(T // P):
-                tokens = slice(tb * P, (tb + 1) * P)
-                nc.tensor.transpose(routed_ps[:, tokens], routed[c][:, tokens], ident[:])
-            return to_sbuf(f"routed_t{c}", routed_ps, T)
+        def gated_turned(m):
+            gy = sbuf(f"gy{m}", [P, turned_cols], F32)
+            nc.scalar.activation(out=gy[:], in_=y_turned[m][:], func=COPY, scale=gate_col[:, m : m + 1])
+            return gy
 
-        def base_turned(c):
-            base_ps = bank(c + 2, [P, T])
-            codes, scales = wq[c]
-            for tb in range(T // P):
-                tokens = slice(tb * P, (tb + 1) * P)
-                for s in range(PASSES):
-                    nc.tensor.matmul_mx(
-                        out=base_ps[:, tokens],
-                        lhsT=xw[s][:, tokens].bitcast(FP8X4),
-                        lhsT_scale=xs[4 * s : P, tokens],
-                        rhs=codes[:, s * P : (s + 1) * P].bitcast(FP8X4),
-                        rhs_scale=scales[:, s * P : (s + 1) * P],
-                        start=(s == 0),
-                        stop=(s == PASSES - 1),
-                    )
-            return to_sbuf(f"base_t{c}", base_ps, T)
+        def summed(g, gys):
+            blocks = groups[g]
+            shape = [P, len(turned_chunks), len(blocks) * SLOTS]
+            sum_ps = bank(2 + g % 2, shape)
+            terms = [[base_turned[m // HALF_BLOCKS][:, m % HALF_BLOCKS, :] for m in blocks], [gy[:] for gy in gys]]
+            steps = [(t, b, i) for t in range(2) for b in reversed(range(len(blocks))) for i in range(len(turned_chunks))]
+            for t, b, i in steps:
+                nc.tensor.matmul(
+                    sum_ps[:, i, b * SLOTS : (b + 1) * SLOTS],
+                    lhsT=terms[t][b][:, i * P : (i + 1) * P],
+                    rhs=ident[:],
+                    is_transpose=True,
+                    start=((t, b, i) == steps[0]),
+                    stop=((t, b, i) == steps[-1]),
+                )
+            return to_sbuf(f"summed{g}", sum_ps, shape)
 
-        def finish_direct(c, *turned_terms):
-            sum_ps = bank(c, [P, T])
-            for i, term in enumerate(turned_terms):
-                for tb in range(T // P):
-                    tokens = slice(tb * P, (tb + 1) * P)
-                    nc.tensor.matmul(
-                        sum_ps[:, tokens],
-                        lhsT=term[:, tokens],
-                        rhs=ident[:],
-                        is_transpose=True,
-                        start=(i == 0 and tb == 0),
-                        stop=(i == 1 and tb == T // P - 1),
-                    )
-            nc.scalar.dma_start(out=out[c * P : (c + 1) * P, :], in_=to_sbuf(f"summed{c}", sum_ps, T)[:])
+        def scatter_turned(g, sums):
+            blocks = groups[g]
+            tokens = token_list[:, blocks[0] * SLOTS // 16 : (blocks[-1] + 1) * SLOTS // 16]
+            for i, c in enumerate(turned_chunks):
+                nc.scalar.activation(out=result[c][:].indirect(tokens), in_=sums[:, i, :], func=COPY)
+                if g == len(groups) - 1:
+                    nc.sync.dma_start(out=out[c * P : (c + 1) * P, :], in_=result[c][:])
 
-        first_base = base_rows(0)
-        wq[3] = quantise_w(3, round_w(3, sbuf("w_bf3", w_shape, BF16)[:]))
-        scatter_sum(0, first_base, gated_rows(0))
-        second_gated = gated_rows(1)
-        scatter_sum(1, base_rows(1), second_gated)
-        routed_t = [routed_turned(c) for c in direct_chunks]
-        base_t = [base_turned(c) for c in direct_chunks]
+        sums = summed(0, [gated_turned(m) for m in groups[0]])
+        for g in range(len(groups)):
+            gys = [gated_turned(m) for m in groups[g + 1]] if g + 1 < len(groups) else None
+            scatter_turned(g, sums)
+            if gys:
+                sums = summed(g + 1, gys)
+
+        gated = sbuf("gated", [P, len(direct_chunks), T], F32)
+        for hf in range(HALVES):
+            half = slice(hf * HALF_SLOTS, (hf + 1) * HALF_SLOTS)
+            nc.vector.tensor_tensor(
+                gated[:, :, half],
+                y_rows[hf][:],
+                gate_all[:, half].unsqueeze(1).to_broadcast([P, len(direct_chunks), HALF_SLOTS]),
+                MULT,
+            )
         for i, c in enumerate(direct_chunks):
-            finish_direct(c, routed_t[i], base_t[i])
+            wide = sbuf(f"result{c}", [P, 2 * T], F32)
+            nc.vector.tensor_tensor(wide[:].indirect(token_list[:]), gated[:, i, :], base_rows[i][:], ADD)
+            nc.sync.dma_start(out=out[c * P : (c + 1) * P, :], in_=wide[:, 0:T])

@@ -26,6 +26,7 @@ HALF_BLOCKS = B // HALVES
 HALF_SLOTS = HALF_BLOCKS * SLOTS
 TOKEN_WINDOW = 704
 CHUNKS = N // P
+SCALAR_W_COLS = 256
 B_ROW = 8
 
 
@@ -87,9 +88,8 @@ def tile_moe_dyl_relu_kernel(
         nc.gpsimd.memset(gate_rows[:], 0.0)
         make_identity(nc, ident[:])
 
-        def load_w(s, first, count):
-            rows = w[512 * s : 512 * (s + 1), :].rearrange("(p j) n -> p j n", j=4)
-            nc.sync.dma_start(out=w_raw[s][:, first : first + count], in_=rows[:, first : first + count])
+        def load_w(s):
+            nc.sync.dma_start(out=w_raw[s][:], in_=w[512 * s : 512 * (s + 1), :].rearrange("(p j) n -> p j n", j=4))
 
         def scale_row_loads(tile, first_row, dram_scales):
             return [
@@ -107,20 +107,17 @@ def tile_moe_dyl_relu_kernel(
         nc.sync.dma_start(out=xw[0][:, 0:T], in_=words_of(x_words[0]))
         nc.sync.dma_start(token_list[:], offs)
         nc.sync.dma_start(out=xw[1][:, 0:T], in_=words_of(x_words[1]))
-        load_scales(nc, xs, x_scales, T)
-        load_w(0, 0, 2)
         nc.sync.dma_start(a_list[:], offs2)
-        load_all(a_rows[0:5])
-        load_w(0, 2, 2)
-        load_all(a_rows[5:8])
+        load_all(a_rows)
+        load_scales(nc, xs, x_scales, T)
         nc.sync.dma_start(b_list[:], offs3)
-        load_all(b_rows[0:2])
-        load_w(1, 0, 4)
-        load_all(b_rows[2:4])
-        nc.sync.dma_start(out=gate_rows[0:B, :], in_=gate[0].rearrange("(m j) -> m j", m=B))
+        load_all(b_rows)
         nc.sync.dma_start(out=aw[0][:], in_=words_of(wa_words[0]))
+        nc.sync.dma_start(out=gate_rows[0:B, :], in_=gate[0].rearrange("(m j) -> m j", m=B))
         nc.sync.dma_start(out=aw[1][:], in_=words_of(wa_words[1]))
         nc.sync.dma_start(out=bw[:], in_=words_of(wb_words[0]))
+        for s in range(PASSES):
+            load_w(s)
 
         half_cols = HALF_BLOCKS * H
         half_list = [slice(hf * half_cols // 16, (hf + 1) * half_cols // 16) for hf in range(HALVES)]
@@ -129,76 +126,25 @@ def tile_moe_dyl_relu_kernel(
         xg = [sbuf(f"xg{s}", [P, T], U32) for s in range(PASSES)]
         for s in range(PASSES):
             nc.vector.tensor_copy(xg[s][:], xw[s][:].bitcast(U32).indirect(token_list[:]))
-        xg_sc = sbuf("xg_sc", [P, T], U8)
-        nc.vector.tensor_copy(xg_sc[:], xs[:].indirect(token_list[:]))
         ag_sc = [sbuf(f"ag_sc{hf}", [P, half_cols], U8) for hf in range(HALVES)]
         for hf in range(HALVES):
             nc.vector.tensor_copy(ag_sc[hf][:], a_sc[:].indirect(a_list[:, half_list[hf]]))
+        xg_sc = sbuf("xg_sc", [P, T], U8)
+        nc.vector.tensor_copy(xg_sc[:], xs[:].indirect(token_list[:]))
         early_cols = (B - 1) * N
         bg_sc = sbuf("bg_sc", [P, early_cols], U8)
         nc.vector.tensor_copy(bg_sc[:], b_sc[:].indirect(b_list[:, 0 : early_cols // 16]))
         b_scales = [bg_sc[:, m * N : (m + 1) * N] for m in range(B - 1)]
 
-        wq, wq_sc = [], []
-        for s in range(PASSES):
-            w_bf = sbuf(f"w_bf{s}", [P, N, 4], BF16)
-            nc.scalar.copy(
-                out=w_bf[:].rearrange("p (c i) j -> p c j i", i=4),
-                in_=w_raw[s][:].rearrange("p j (c i) -> p c j i", i=4),
-            )
-            wq.append(sbuf(f"wq{s}", [P, N], U32))
-            wq_sc.append(sbuf(f"wq_sc{s}", [P, N], U8))
-            nc.vector.quantize_mx(out=wq[s][:].bitcast(FP8X4), scales=wq_sc[s][:], in_=w_bf[:].rearrange("p n j -> p (n j)"))
-
-        def to_sbuf(name, source, shape):
-            staged = sbuf(name, shape, F32)
-            nc.scalar.copy(out=staged[:], in_=source[:])
-            return staged
-
-        gate_ps = bank(4, [P, P])
+        gate_ps = bank(2, [P, P])
         nc.tensor.transpose(gate_ps[:], gate_rows[:], ident[:])
         gate_col = sbuf("gate_col", [P, B], F32)
         nc.scalar.copy(out=gate_col[:], in_=gate_ps[:, 0:B])
-        spread_ps = bank(5, [P, B, SLOTS])
+        spread_ps = bank(3, [P, B, SLOTS])
         for m in range(B):
             nc.tensor.transpose(spread_ps[:, m, :], gate_col[:, m : m + 1].to_broadcast([P, P]), ident[:])
         gate_all = sbuf("gate_all", [P, T], F32)
         nc.scalar.copy(out=gate_all[:], in_=spread_ps[:].rearrange("p m j -> p (m j)"))
-
-        turned_chunks, direct_chunks = (0, 1), (2, 3)
-        turned_cols = len(turned_chunks) * P
-
-        base_turned = []
-        for hf in range(HALVES):
-            base_ps = bank(2 + hf, [P, HALF_BLOCKS, turned_cols])
-            for b in range(HALF_BLOCKS):
-                m = hf * HALF_BLOCKS + b
-                slots = slice(m * SLOTS, (m + 1) * SLOTS)
-                for s in range(PASSES):
-                    nc.tensor.matmul_mx(
-                        out=base_ps[:, b, :],
-                        lhsT=xg[s][:, slots].bitcast(FP8X4),
-                        lhsT_scale=xg_sc[4 * s : P, slots],
-                        rhs=wq[s][:, 0:turned_cols].bitcast(FP8X4),
-                        rhs_scale=wq_sc[s][:, 0:turned_cols],
-                        start=(s == 0),
-                        stop=(s == PASSES - 1),
-                    )
-            base_turned.append(to_sbuf(f"base_turned{hf}", base_ps, [P, HALF_BLOCKS, turned_cols]))
-        base_rows = []
-        for i, c in enumerate(direct_chunks):
-            base_ps = bank(i, [P, T])
-            for s in range(PASSES):
-                nc.tensor.matmul_mx(
-                    out=base_ps[:],
-                    lhsT=wq[s][:, c * P : (c + 1) * P].bitcast(FP8X4),
-                    lhsT_scale=wq_sc[s][:, c * P : (c + 1) * P],
-                    rhs=xg[s][:].bitcast(FP8X4),
-                    rhs_scale=xg_sc[4 * s : P, :],
-                    start=(s == 0),
-                    stop=(s == PASSES - 1),
-                )
-            base_rows.append(to_sbuf(f"base_rows{c}", base_ps, [P, T]))
 
         ag0 = [sbuf(f"ag0_{hf}", [P, half_cols], U32) for hf in range(HALVES)]
         for hf in range(HALVES):
@@ -241,30 +187,24 @@ def tile_moe_dyl_relu_kernel(
                 b_scales.append(bg_sc_last[:])
                 ag1.append(gather_a1(B - 1, "h_pairs0"))
 
-        y_rows = [bank(hf, [P, len(direct_chunks), HALF_SLOTS]) for hf in range(HALVES)]
-        y_turned = []
-        for m in range(B):
-            hf, b = divmod(m, HALF_BLOCKS)
-            bg = sbuf(f"bg{m}", [P, N], U32)
-            nc.vector.tensor_copy(bg[:], bw[:].bitcast(U32).indirect(b_list[:, block_list[m]]))
+        first_chunks, last_chunks = (0, 1), (2, 3)
+        groups = ((0,), (1,), (2, 3))
+        y_first = [bank(g, [P, len(first_chunks), len(blocks) * SLOTS]) for g, blocks in enumerate(groups)]
+        y_last = {c: bank(c + 1, [P, T]) for c in last_chunks}
+
+        def second_layer(m):
+            bg = sbuf(f"bg{m % 2}", [P, N], U32)
             hq = sbuf(f"hq{m % 2}", [P, SLOTS], U32)
             hq_sc = sbuf(f"hq_sc{m}", [P, SLOTS], U8)
             nc.vector.quantize_mx(
                 out=hq[:].bitcast(FP8X4), scales=hq_sc[:], in_=h_words[m][:].rearrange("p j u -> p (j u)").bitcast(BF16)
             )
-            y_turned.append(bank(4 + m, [P, turned_cols]))
-            nc.tensor.matmul_mx(
-                out=y_turned[m][:],
-                lhsT=hq[:].bitcast(FP8X4),
-                lhsT_scale=hq_sc[:],
-                rhs=bg[:, 0:turned_cols].bitcast(FP8X4),
-                rhs_scale=b_scales[m][B_ROW:P, 0:turned_cols],
-                start=True,
-                stop=True,
-            )
-            for i, c in enumerate(direct_chunks):
+            nc.vector.tensor_copy(bg[:], bw[:].bitcast(U32).indirect(b_list[:, block_list[m]]))
+            g = min(m, len(groups) - 1)
+            place = slice((m - groups[g][0]) * SLOTS, (m - groups[g][0] + 1) * SLOTS)
+            for c in range(CHUNKS):
                 nc.tensor.matmul_mx(
-                    out=y_rows[hf][:, i, b * SLOTS : (b + 1) * SLOTS],
+                    out=y_first[g][:, c, place] if c in first_chunks else y_last[c][:, m * SLOTS : (m + 1) * SLOTS],
                     lhsT=bg[:, c * P : (c + 1) * P].bitcast(FP8X4),
                     lhsT_scale=b_scales[m][B_ROW:P, c * P : (c + 1) * P],
                     rhs=hq[:].bitcast(FP8X4),
@@ -273,56 +213,83 @@ def tile_moe_dyl_relu_kernel(
                     stop=True,
                 )
 
-        result = {c: sbuf(f"result{c}", [P, T], F32) for c in turned_chunks}
-        groups = ((0,), (1,), (2, 3))
+        def slots_of(blocks):
+            return slice(blocks[0] * SLOTS, (blocks[-1] + 1) * SLOTS)
 
-        def gated_turned(m):
-            gy = sbuf(f"gy{m}", [P, turned_cols], F32)
-            nc.scalar.activation(out=gy[:], in_=y_turned[m][:], func=COPY, scale=gate_col[:, m : m + 1])
-            return gy
+        def tokens_of(slots):
+            return token_list[:, slots.start // 16 : slots.stop // 16]
 
-        def summed(g, gys):
-            blocks = groups[g]
-            shape = [P, len(turned_chunks), len(blocks) * SLOTS]
-            sum_ps = bank(2 + g % 2, shape)
-            terms = [[base_turned[m // HALF_BLOCKS][:, m % HALF_BLOCKS, :] for m in blocks], [gy[:] for gy in gys]]
-            steps = [(t, b, i) for t in range(2) for b in reversed(range(len(blocks))) for i in range(len(turned_chunks))]
-            for t, b, i in steps:
-                nc.tensor.matmul(
-                    sum_ps[:, i, b * SLOTS : (b + 1) * SLOTS],
-                    lhsT=terms[t][b][:, i * P : (i + 1) * P],
-                    rhs=ident[:],
-                    is_transpose=True,
-                    start=((t, b, i) == steps[0]),
-                    stop=((t, b, i) == steps[-1]),
-                )
-            return to_sbuf(f"summed{g}", sum_ps, shape)
+        def gated_first(g):
+            slots = slots_of(groups[g])
+            shape = [P, len(first_chunks), slots.stop - slots.start]
+            gated = sbuf(f"gated_first{g}", shape, F32)
+            nc.vector.tensor_tensor(gated[:], y_first[g][:], gate_all[:, slots].unsqueeze(1).to_broadcast(shape), MULT)
+            return gated
 
-        def scatter_turned(g, sums):
-            blocks = groups[g]
-            tokens = token_list[:, blocks[0] * SLOTS // 16 : (blocks[-1] + 1) * SLOTS // 16]
-            for i, c in enumerate(turned_chunks):
-                nc.scalar.activation(out=result[c][:].indirect(tokens), in_=sums[:, i, :], func=COPY)
-                if g == len(groups) - 1:
-                    nc.sync.dma_start(out=out[c * P : (c + 1) * P, :], in_=result[c][:])
+        def gated_last(c, slots, name):
+            gated = sbuf(name, [P, slots.stop - slots.start], F32)
+            nc.vector.tensor_tensor(gated[:], y_last[c][:, slots], gate_all[:, slots], MULT)
+            return gated
 
-        sums = summed(0, [gated_turned(m) for m in groups[0]])
-        for g in range(len(groups)):
-            gys = [gated_turned(m) for m in groups[g + 1]] if g + 1 < len(groups) else None
-            scatter_turned(g, sums)
-            if gys:
-                sums = summed(g + 1, gys)
+        routed = [sbuf(f"routed{c}", [P, T], F32) for c in range(CHUNKS)]
 
-        gated = sbuf("gated", [P, len(direct_chunks), T], F32)
-        for hf in range(HALVES):
-            half = slice(hf * HALF_SLOTS, (hf + 1) * HALF_SLOTS)
-            nc.vector.tensor_tensor(
-                gated[:, :, half],
-                y_rows[hf][:],
-                gate_all[:, half].unsqueeze(1).to_broadcast([P, len(direct_chunks), HALF_SLOTS]),
-                MULT,
+        def scatter_on_scalar(c, slots, values):
+            nc.scalar.activation(out=routed[c][:].indirect(tokens_of(slots)), in_=values, func=COPY)
+
+        def scatter_first(g, gated):
+            for c in first_chunks:
+                scatter_on_scalar(c, slots_of(groups[g]), gated[:, c, :])
+
+        w_bf = [sbuf(f"w_bf{s}", [P, N, 4], BF16) for s in range(PASSES)]
+
+        def rounding_views(s, cols):
+            return (
+                w_bf[s][:, cols, :].rearrange("p (c i) j -> p c j i", i=4),
+                w_raw[s][:, :, cols].rearrange("p j (c i) -> p c j i", i=4),
             )
-        for i, c in enumerate(direct_chunks):
-            wide = sbuf(f"result{c}", [P, 2 * T], F32)
-            nc.vector.tensor_tensor(wide[:].indirect(token_list[:]), gated[:, i, :], base_rows[i][:], ADD)
-            nc.sync.dma_start(out=out[c * P : (c + 1) * P, :], in_=wide[:, 0:T])
+
+        def quantise_w(s):
+            codes = sbuf(f"wq{s}", [P, N], U32)
+            scales = sbuf(f"wq_sc{s}", [P, N], U8)
+            nc.vector.quantize_mx(out=codes[:].bitcast(FP8X4), scales=scales[:], in_=w_bf[s][:].rearrange("p n j -> p (n j)"))
+            return codes, scales
+
+        halves = [slice(hf * HALF_SLOTS, (hf + 1) * HALF_SLOTS) for hf in range(HALVES)]
+        second_layer(0)
+        second_layer(1)
+        scatter_first(0, gated_first(0))
+        second_layer(2)
+        scatter_first(1, gated_first(1))
+        second_layer(3)
+        target, source = rounding_views(0, slice(0, SCALAR_W_COLS))
+        nc.scalar.copy(out=target, in_=source)
+        nc.vector.tensor_copy(*rounding_views(0, slice(SCALAR_W_COLS, N)))
+        gated_a = gated_first(2)
+        gated_2 = gated_last(2, slice(0, T), "gated_2")
+        gated_3 = gated_last(3, halves[0], "gated_3")
+        nc.vector.tensor_copy(routed[3][:].indirect(tokens_of(halves[0])), gated_3[:])
+        nc.vector.tensor_copy(*rounding_views(1, slice(0, N)))
+        wq = [quantise_w(s) for s in range(PASSES)]
+        scatter_on_scalar(0, halves[1], gated_a[:, 0, :])
+        scatter_on_scalar(2, halves[0], gated_2[:, halves[0]])
+        scatter_on_scalar(1, halves[1], gated_a[:, 1, :])
+        scatter_on_scalar(2, halves[1], gated_2[:, halves[1]])
+        gated_3 = gated_last(3, halves[1], "w_bf1")
+        nc.vector.tensor_copy(routed[3][:].indirect(tokens_of(halves[1])), gated_3[:])
+
+        for c, number in ((0, 5), (3, 6), (1, 7), (2, 0)):
+            base_ps = bank(number, [P, T])
+            for s in range(PASSES):
+                codes, scales = wq[s]
+                nc.tensor.matmul_mx(
+                    out=base_ps[:],
+                    lhsT=codes[:, c * P : (c + 1) * P].bitcast(FP8X4),
+                    lhsT_scale=scales[:, c * P : (c + 1) * P],
+                    rhs=xw[s][:, 0:T].bitcast(FP8X4),
+                    rhs_scale=xs[4 * s : P, 0:T],
+                    start=(s == 0),
+                    stop=(s == PASSES - 1),
+                )
+            result = sbuf(f"result{c}", [P, T], F32)
+            nc.vector.tensor_tensor(result[:], base_ps[:], routed[c][:], ADD)
+            nc.sync.dma_start(out=out[c * P : (c + 1) * P, :], in_=result[:])

@@ -26,7 +26,6 @@ HALF_BLOCKS = B // HALVES
 HALF_SLOTS = HALF_BLOCKS * SLOTS
 TOKEN_WINDOW = 704
 CHUNKS = N // P
-SCALAR_W_COLS = 256
 B_ROW = 8
 
 
@@ -107,14 +106,14 @@ def tile_moe_dyl_relu_kernel(
         nc.sync.dma_start(out=xw[0][:, 0:T], in_=words_of(x_words[0]))
         nc.sync.dma_start(token_list[:], offs)
         nc.sync.dma_start(out=xw[1][:, 0:T], in_=words_of(x_words[1]))
-        nc.sync.dma_start(a_list[:], offs2)
-        load_all(a_rows)
         load_scales(nc, xs, x_scales, T)
+        nc.sync.dma_start(out=aw[0][:], in_=words_of(wa_words[0]))
+        nc.sync.dma_start(a_list[:], offs2)
+        nc.sync.dma_start(out=gate_rows[0:B, :], in_=gate[0].rearrange("(m j) -> m j", m=B))
+        load_all(a_rows)
+        nc.sync.dma_start(out=aw[1][:], in_=words_of(wa_words[1]))
         nc.sync.dma_start(b_list[:], offs3)
         load_all(b_rows)
-        nc.sync.dma_start(out=aw[0][:], in_=words_of(wa_words[0]))
-        nc.sync.dma_start(out=gate_rows[0:B, :], in_=gate[0].rearrange("(m j) -> m j", m=B))
-        nc.sync.dma_start(out=aw[1][:], in_=words_of(wa_words[1]))
         nc.sync.dma_start(out=bw[:], in_=words_of(wb_words[0]))
         for s in range(PASSES):
             load_w(s)
@@ -126,16 +125,8 @@ def tile_moe_dyl_relu_kernel(
         xg = [sbuf(f"xg{s}", [P, T], U32) for s in range(PASSES)]
         for s in range(PASSES):
             nc.vector.tensor_copy(xg[s][:], xw[s][:].bitcast(U32).indirect(token_list[:]))
-        ag_sc = [sbuf(f"ag_sc{hf}", [P, half_cols], U8) for hf in range(HALVES)]
-        for hf in range(HALVES):
-            nc.vector.tensor_copy(ag_sc[hf][:], a_sc[:].indirect(a_list[:, half_list[hf]]))
         xg_sc = sbuf("xg_sc", [P, T], U8)
         nc.vector.tensor_copy(xg_sc[:], xs[:].indirect(token_list[:]))
-        early_cols = (B - 1) * N
-        bg_sc = sbuf("bg_sc", [P, early_cols], U8)
-        nc.vector.tensor_copy(bg_sc[:], b_sc[:].indirect(b_list[:, 0 : early_cols // 16]))
-        b_scales = [bg_sc[:, m * N : (m + 1) * N] for m in range(B - 1)]
-
         gate_ps = bank(2, [P, P])
         nc.tensor.transpose(gate_ps[:], gate_rows[:], ident[:])
         gate_col = sbuf("gate_col", [P, B], F32)
@@ -149,6 +140,14 @@ def tile_moe_dyl_relu_kernel(
         ag0 = [sbuf(f"ag0_{hf}", [P, half_cols], U32) for hf in range(HALVES)]
         for hf in range(HALVES):
             nc.vector.tensor_copy(ag0[hf][:], aw[0][:].bitcast(U32).indirect(a_list[:, half_list[hf]]))
+        ag_sc = [sbuf(f"ag_sc{hf}", [P, half_cols], U8) for hf in range(HALVES)]
+        for hf in range(HALVES):
+            nc.vector.tensor_copy(ag_sc[hf][:], a_sc[:].indirect(a_list[:, half_list[hf]]))
+
+        def gather_b_scales(hf, name):
+            scales = sbuf(name, [P, half_cols], U8)
+            nc.vector.tensor_copy(scales[:], b_sc[:].indirect(b_list[:, half_list[hf]]))
+            return [scales[:, b * N : (b + 1) * N] for b in range(HALF_BLOCKS)]
 
         def gather_a1(m, name):
             words = sbuf(name, [P, H], U32)
@@ -182,29 +181,23 @@ def tile_moe_dyl_relu_kernel(
             h_words.append(sbuf(f"h_words{m}", [P, SLOTS, 2], F32))
             nc.scalar.copy(out=h_words[m][:], in_=turned[:].rearrange("p u j -> p j u"))
             if m == 0:
-                bg_sc_last = sbuf("ag1_0", [P, N], U8)
-                nc.vector.tensor_copy(bg_sc_last[:], b_sc[:].indirect(b_list[:, block_list[B - 1]]))
-                b_scales.append(bg_sc_last[:])
+                b_scales = gather_b_scales(0, "bg_sc0")
                 ag1.append(gather_a1(B - 1, "h_pairs0"))
 
-        first_chunks, last_chunks = (0, 1), (2, 3)
         groups = ((0,), (1,), (2, 3))
-        y_first = [bank(g, [P, len(first_chunks), len(blocks) * SLOTS]) for g, blocks in enumerate(groups)]
-        y_last = {c: bank(c + 1, [P, T]) for c in last_chunks}
 
-        def second_layer(m):
+        def second_layer(m, name):
             bg = sbuf(f"bg{m % 2}", [P, N], U32)
-            hq = sbuf(f"hq{m % 2}", [P, SLOTS], U32)
+            hq = sbuf(name, [P, SLOTS], U32)
             hq_sc = sbuf(f"hq_sc{m}", [P, SLOTS], U8)
             nc.vector.quantize_mx(
                 out=hq[:].bitcast(FP8X4), scales=hq_sc[:], in_=h_words[m][:].rearrange("p j u -> p (j u)").bitcast(BF16)
             )
             nc.vector.tensor_copy(bg[:], bw[:].bitcast(U32).indirect(b_list[:, block_list[m]]))
-            g = min(m, len(groups) - 1)
-            place = slice((m - groups[g][0]) * SLOTS, (m - groups[g][0] + 1) * SLOTS)
+            y_ps = bank(m, [P, CHUNKS, SLOTS])
             for c in range(CHUNKS):
                 nc.tensor.matmul_mx(
-                    out=y_first[g][:, c, place] if c in first_chunks else y_last[c][:, m * SLOTS : (m + 1) * SLOTS],
+                    out=y_ps[:, c, :],
                     lhsT=bg[:, c * P : (c + 1) * P].bitcast(FP8X4),
                     lhsT_scale=b_scales[m][B_ROW:P, c * P : (c + 1) * P],
                     rhs=hq[:].bitcast(FP8X4),
@@ -212,6 +205,7 @@ def tile_moe_dyl_relu_kernel(
                     start=True,
                     stop=True,
                 )
+            return y_ps
 
         def slots_of(blocks):
             return slice(blocks[0] * SLOTS, (blocks[-1] + 1) * SLOTS)
@@ -219,66 +213,56 @@ def tile_moe_dyl_relu_kernel(
         def tokens_of(slots):
             return token_list[:, slots.start // 16 : slots.stop // 16]
 
-        def gated_first(g):
-            slots = slots_of(groups[g])
-            shape = [P, len(first_chunks), slots.stop - slots.start]
-            gated = sbuf(f"gated_first{g}", shape, F32)
-            nc.vector.tensor_tensor(gated[:], y_first[g][:], gate_all[:, slots].unsqueeze(1).to_broadcast(shape), MULT)
-            return gated
+        gated = [sbuf(f"gated{g}", [P, CHUNKS, len(blocks) * SLOTS], F32) for g, blocks in enumerate(groups)]
 
-        def gated_last(c, slots, name):
-            gated = sbuf(name, [P, slots.stop - slots.start], F32)
-            nc.vector.tensor_tensor(gated[:], y_last[c][:, slots], gate_all[:, slots], MULT)
-            return gated
+        def gate_block(m, y_ps, chunks):
+            g = min(m, len(groups) - 1)
+            gates = gate_all[:, slots_of((m,))].unsqueeze(1).to_broadcast([P, chunks, SLOTS])
+            nc.vector.tensor_tensor(gated[g][:, 0:chunks, slots_of((m - groups[g][0],))], y_ps[:, 0:chunks], gates, MULT)
 
         routed = [sbuf(f"routed{c}", [P, T], F32) for c in range(CHUNKS)]
 
-        def scatter_on_scalar(c, slots, values):
-            nc.scalar.activation(out=routed[c][:].indirect(tokens_of(slots)), in_=values, func=COPY)
+        def scatter(g, chunks):
+            for c in chunks:
+                nc.scalar.activation(out=routed[c][:].indirect(tokens_of(slots_of(groups[g]))), in_=gated[g][:, c, :], func=COPY)
 
-        def scatter_first(g, gated):
-            for c in first_chunks:
-                scatter_on_scalar(c, slots_of(groups[g]), gated[:, c, :])
-
-        w_bf = [sbuf(f"w_bf{s}", [P, N, 4], BF16) for s in range(PASSES)]
-
-        def rounding_views(s, cols):
-            return (
-                w_bf[s][:, cols, :].rearrange("p (c i) j -> p c j i", i=4),
-                w_raw[s][:, :, cols].rearrange("p j (c i) -> p c j i", i=4),
+        def round_w(s):
+            w_bf = sbuf(f"w_bf{s}", [P, N, 4], BF16)
+            nc.vector.tensor_copy(
+                w_bf[:].rearrange("p (c i) j -> p c j i", i=4), w_raw[s][:].rearrange("p j (c i) -> p c j i", i=4)
             )
+            return w_bf
 
-        def quantise_w(s):
+        def quantise_w(s, w_bf):
             codes = sbuf(f"wq{s}", [P, N], U32)
             scales = sbuf(f"wq_sc{s}", [P, N], U8)
-            nc.vector.quantize_mx(out=codes[:].bitcast(FP8X4), scales=scales[:], in_=w_bf[s][:].rearrange("p n j -> p (n j)"))
+            nc.vector.quantize_mx(out=codes[:].bitcast(FP8X4), scales=scales[:], in_=w_bf[:].rearrange("p n j -> p (n j)"))
             return codes, scales
 
-        halves = [slice(hf * HALF_SLOTS, (hf + 1) * HALF_SLOTS) for hf in range(HALVES)]
-        second_layer(0)
-        second_layer(1)
-        scatter_first(0, gated_first(0))
-        second_layer(2)
-        scatter_first(1, gated_first(1))
-        second_layer(3)
-        target, source = rounding_views(0, slice(0, SCALAR_W_COLS))
-        nc.scalar.copy(out=target, in_=source)
-        nc.vector.tensor_copy(*rounding_views(0, slice(SCALAR_W_COLS, N)))
-        gated_a = gated_first(2)
-        gated_2 = gated_last(2, slice(0, T), "gated_2")
-        gated_3 = gated_last(3, halves[0], "gated_3")
-        nc.vector.tensor_copy(routed[3][:].indirect(tokens_of(halves[0])), gated_3[:])
-        nc.vector.tensor_copy(*rounding_views(1, slice(0, N)))
-        wq = [quantise_w(s) for s in range(PASSES)]
-        scatter_on_scalar(0, halves[1], gated_a[:, 0, :])
-        scatter_on_scalar(2, halves[0], gated_2[:, halves[0]])
-        scatter_on_scalar(1, halves[1], gated_a[:, 1, :])
-        scatter_on_scalar(2, halves[1], gated_2[:, halves[1]])
-        gated_3 = gated_last(3, halves[1], "w_bf1")
-        nc.vector.tensor_copy(routed[3][:].indirect(tokens_of(halves[1])), gated_3[:])
+        y0 = second_layer(0, "hq0")
+        y1 = second_layer(1, "hq1")
+        gate_block(0, y0, CHUNKS)
+        scatter(0, range(CHUNKS))
+        b_scales.extend(gather_b_scales(1, "hq0"))
+        gate_block(1, y1, CHUNKS)
+        scatter(1, range(CHUNKS))
+        y2 = second_layer(2, "hq_sc0")
+        y3 = second_layer(3, "hq1")
+        gate_block(2, y2, CHUNKS - 1)
+        w_bf0 = round_w(0)
+        gate_block(3, y3, CHUNKS - 1)
+        scatter(2, range(CHUNKS - 1))
+        w_bf1 = round_w(1)
+        wq = [quantise_w(0, w_bf0), quantise_w(1, w_bf1)]
 
-        for c, number in ((0, 5), (3, 6), (1, 7), (2, 0)):
-            base_ps = bank(number, [P, T])
+        last = CHUNKS - 1
+        gated_last = sbuf("w_bf1", [P, HALF_SLOTS], F32)
+        for b, y_ps in enumerate((y2, y3)):
+            nc.vector.tensor_tensor(gated_last[:, slots_of((b,))], y_ps[:, last, :], gate_all[:, slots_of((2 + b,))], MULT)
+        nc.vector.tensor_copy(routed[last][:].indirect(tokens_of(slots_of(groups[2]))), gated_last[:])
+
+        for c in (0, 1, 3, 2):
+            base_ps = bank(4 + c, [P, T])
             for s in range(PASSES):
                 codes, scales = wq[s]
                 nc.tensor.matmul_mx(

@@ -149,14 +149,12 @@ def tile_moe_dyl_relu_kernel(
             nc.vector.tensor_copy(scales[:], b_sc[:].indirect(b_list[:, half_list[hf]]))
             return [scales[:, b * N : (b + 1) * N] for b in range(HALF_BLOCKS)]
 
-        def gather_a1(m, name):
-            words = sbuf(name, [P, H], U32)
-            nc.vector.tensor_copy(words[:], aw[1][:].bitcast(U32).indirect(a_list[:, block_list[m]]))
-            return words
+        ag1 = [sbuf(f"ag1_{m}", [P, H], U32) for m in range(B)]
+        for m in range(B):
+            nc.vector.tensor_copy(ag1[m][:], aw[1][:].bitcast(U32).indirect(a_list[:, block_list[m]]))
+        b_scales = gather_b_scales(0, "bg_sc0")
 
-        ag1 = [gather_a1(m, f"ag1_{m}") for m in range(B - 1)]
-
-        h_words = []
+        h_pairs = []
         for m in range(B):
             hf, b = divmod(m, HALF_BLOCKS)
             slots = slice(m * SLOTS, (m + 1) * SLOTS)
@@ -172,36 +170,39 @@ def tile_moe_dyl_relu_kernel(
                     start=(s == 0),
                     stop=(s == PASSES - 1),
                 )
-            h_pairs = sbuf(f"h_pairs{m}", [P, 2, P, 2], BF16)
-            nc.scalar.activation(out=h_pairs[:], in_=h_ps[:].rearrange("j (p u e) -> j u p e", u=2, e=2), func=RELU)
+            h_pairs.append(sbuf(f"h_pairs{m}", [P, 2, P, 2], BF16))
+            nc.scalar.activation(out=h_pairs[m][:], in_=h_ps[:].rearrange("j (p u e) -> j u p e", u=2, e=2), func=RELU)
+        h_words = []
+        for m in range(B):
             turned = bank(4 + m, [P, 2, SLOTS])
-            pairs = h_pairs[:].rearrange("j u p e -> j (u p e)").bitcast(F32)
+            pairs = h_pairs[m][:].rearrange("j u p e -> j (u p e)").bitcast(F32)
             for u in range(2):
                 nc.tensor.transpose(turned[:, u, :], pairs[:, u * P : (u + 1) * P], ident[:])
-            h_words.append(sbuf(f"h_words{m}", [P, SLOTS, 2], F32))
+            h_words.append(sbuf("ag1_3" if m == 0 else f"h_words{m}", [P, SLOTS, 2], F32))
             nc.scalar.copy(out=h_words[m][:], in_=turned[:].rearrange("p u j -> p j u"))
-            if m == 0:
-                b_scales = gather_b_scales(0, "bg_sc0")
-                ag1.append(gather_a1(B - 1, "h_pairs0"))
 
         groups = ((0,), (1,), (2, 3))
 
-        def second_layer(m, name):
-            bg = sbuf(f"bg{m % 2}", [P, N], U32)
-            hq = sbuf(name, [P, SLOTS], U32)
-            hq_sc = sbuf(f"hq_sc{m}", [P, SLOTS], U8)
+        def quantise_h(m, name):
+            codes = sbuf(name, [P, SLOTS], U32)
+            scales = sbuf(f"hq_sc{m}", [P, SLOTS], U8)
             nc.vector.quantize_mx(
-                out=hq[:].bitcast(FP8X4), scales=hq_sc[:], in_=h_words[m][:].rearrange("p j u -> p (j u)").bitcast(BF16)
+                out=codes[:].bitcast(FP8X4), scales=scales[:], in_=h_words[m][:].rearrange("p j u -> p (j u)").bitcast(BF16)
             )
-            nc.vector.tensor_copy(bg[:], bw[:].bitcast(U32).indirect(b_list[:, block_list[m]]))
-            y_ps = bank(m, [P, CHUNKS, SLOTS])
-            for c in range(CHUNKS):
+            return codes, scales
+
+        def second_layer(m, hq, first, count, name, number):
+            bg = sbuf(name, [P, count * P], U32)
+            start = (m * N + first * P) // 16
+            nc.vector.tensor_copy(bg[:], bw[:].bitcast(U32).indirect(b_list[:, start : start + count * P // 16]))
+            y_ps = bank(number, [P, count, SLOTS])
+            for i in range(count):
                 nc.tensor.matmul_mx(
-                    out=y_ps[:, c, :],
-                    lhsT=bg[:, c * P : (c + 1) * P].bitcast(FP8X4),
-                    lhsT_scale=b_scales[m][B_ROW:P, c * P : (c + 1) * P],
-                    rhs=hq[:].bitcast(FP8X4),
-                    rhs_scale=hq_sc[:],
+                    out=y_ps[:, i, :],
+                    lhsT=bg[:, i * P : (i + 1) * P].bitcast(FP8X4),
+                    lhsT_scale=b_scales[m][B_ROW:P, (first + i) * P : (first + i + 1) * P],
+                    rhs=hq[0][:].bitcast(FP8X4),
+                    rhs_scale=hq[1][:],
                     start=True,
                     stop=True,
                 )
@@ -215,10 +216,11 @@ def tile_moe_dyl_relu_kernel(
 
         gated = [sbuf(f"gated{g}", [P, CHUNKS, len(blocks) * SLOTS], F32) for g, blocks in enumerate(groups)]
 
-        def gate_block(m, y_ps, chunks):
+        def gate_block(m, y_ps, first, count):
             g = min(m, len(groups) - 1)
-            gates = gate_all[:, slots_of((m,))].unsqueeze(1).to_broadcast([P, chunks, SLOTS])
-            nc.vector.tensor_tensor(gated[g][:, 0:chunks, slots_of((m - groups[g][0],))], y_ps[:, 0:chunks], gates, MULT)
+            gates = gate_all[:, slots_of((m,))].unsqueeze(1).to_broadcast([P, count, SLOTS])
+            target = gated[g][:, first : first + count, slots_of((m - groups[g][0],))]
+            nc.vector.tensor_tensor(target, y_ps[:, 0:count], gates, MULT)
 
         routed = [sbuf(f"routed{c}", [P, T], F32) for c in range(CHUNKS)]
 
@@ -239,29 +241,34 @@ def tile_moe_dyl_relu_kernel(
             nc.vector.quantize_mx(out=codes[:].bitcast(FP8X4), scales=scales[:], in_=w_bf[:].rearrange("p n j -> p (n j)"))
             return codes, scales
 
-        y0 = second_layer(0, "hq0")
-        y1 = second_layer(1, "hq1")
-        gate_block(0, y0, CHUNKS)
-        scatter(0, range(CHUNKS))
+        last = CHUNKS - 1
+        hq0 = quantise_h(0, "hq0")
+        y0_first = second_layer(0, hq0, 0, 2, "bg0_first", 0)
+        y0_second = second_layer(0, hq0, 2, 2, "bg0_second", 1)
+        hq1 = quantise_h(1, "bg0_first")
+        gate_block(0, y0_first, 0, 2)
+        scatter(0, (0, 1))
+        y1 = second_layer(1, hq1, 0, CHUNKS, "bg1", 2)
+        gate_block(0, y0_second, 2, 2)
+        scatter(0, (2, 3))
         b_scales.extend(gather_b_scales(1, "hq0"))
-        gate_block(1, y1, CHUNKS)
+        gate_block(1, y1, 0, CHUNKS)
         scatter(1, range(CHUNKS))
-        y2 = second_layer(2, "hq_sc0")
-        y3 = second_layer(3, "hq1")
-        gate_block(2, y2, CHUNKS - 1)
+        y2 = second_layer(2, quantise_h(2, "bg0_second"), 0, CHUNKS, "hq_sc0", 3)
+        y3 = second_layer(3, quantise_h(3, "bg0_first"), 0, CHUNKS, "bg1", 0)
+        gate_block(2, y2, 0, CHUNKS)
         w_bf0 = round_w(0)
-        gate_block(3, y3, CHUNKS - 1)
-        scatter(2, range(CHUNKS - 1))
+        gate_block(3, y3, 0, last)
+        nc.scalar.activation(out=routed[last][:].indirect(tokens_of(slots_of((2,)))), in_=gated[2][:, last, 0:SLOTS], func=COPY)
+        scatter(2, range(last))
         w_bf1 = round_w(1)
         wq = [quantise_w(0, w_bf0), quantise_w(1, w_bf1)]
 
-        last = CHUNKS - 1
-        gated_last = sbuf("w_bf1", [P, HALF_SLOTS], F32)
-        for b, y_ps in enumerate((y2, y3)):
-            nc.vector.tensor_tensor(gated_last[:, slots_of((b,))], y_ps[:, last, :], gate_all[:, slots_of((2 + b,))], MULT)
-        nc.vector.tensor_copy(routed[last][:].indirect(tokens_of(slots_of(groups[2]))), gated_last[:])
+        gated_last = sbuf("w_bf1", [P, SLOTS], F32)
+        nc.vector.tensor_tensor(gated_last[:], y3[:, last, :], gate_all[:, slots_of((3,))], MULT)
+        nc.vector.tensor_copy(routed[last][:].indirect(tokens_of(slots_of((3,)))), gated_last[:])
 
-        for c in (0, 1, 3, 2):
+        for c in (0, 3, 1, 2):
             base_ps = bank(4 + c, [P, T])
             for s in range(PASSES):
                 codes, scales = wq[s]
@@ -274,6 +281,9 @@ def tile_moe_dyl_relu_kernel(
                     start=(s == 0),
                     stop=(s == PASSES - 1),
                 )
-            result = sbuf(f"result{c}", [P, T], F32)
-            nc.vector.tensor_tensor(result[:], base_ps[:], routed[c][:], ADD)
-            nc.sync.dma_start(out=out[c * P : (c + 1) * P, :], in_=result[:])
+            pieces = 2 if c == 2 else 1
+            for piece in range(pieces):
+                tokens = slice(piece * T // pieces, (piece + 1) * T // pieces)
+                result = sbuf(f"result{c}_{piece}", [P, T // pieces], F32)
+                nc.vector.tensor_tensor(result[:], base_ps[:, tokens], routed[c][:, tokens], ADD)
+                nc.sync.dma_start(out=out[c * P : (c + 1) * P, tokens], in_=result[:])

@@ -57,12 +57,17 @@ def tile_moe_dyl_relu_kernel(
     with ExitStack() as ctx:
         lists = ctx.enter_context(tc.tile_pool(name="lists", bufs=1))
         keep = ctx.enter_context(tc.tile_pool(name="keep", bufs=1))
+        shared = ctx.enter_context(tc.tile_pool(name="shared", bufs=1))
         psum = ctx.enter_context(tc.psum_pool(name="psum", bufs=1))
 
         def bank(number, shape):
             return psum.tile(shape, F32, name=f"bank{number}")
 
+        offsets = {"bg0_first": 0, "hq1": 0, "bg1": 512}
+
         def sbuf(name, shape, dtype):
+            if name in offsets:
+                return shared.tile(shape, dtype, name=name, offset=offsets[name], align_bytes=64)
             return keep.tile(shape, dtype, name=name, align_bytes=64)
 
         token_list = lists.tile([P, T // 16], U16, name="token_list")
@@ -152,7 +157,7 @@ def tile_moe_dyl_relu_kernel(
         ag1 = [sbuf(f"ag1_{m}", [P, H], U32) for m in range(B)]
         for m in range(B):
             nc.vector.tensor_copy(ag1[m][:], aw[1][:].bitcast(U32).indirect(a_list[:, block_list[m]]))
-        b_scales = gather_b_scales(0, "bg_sc0")
+        b_scales = gather_b_scales(0, "bg_sc0") + gather_b_scales(1, "bg_sc1")
 
         h_pairs = []
         for m in range(B):
@@ -242,33 +247,32 @@ def tile_moe_dyl_relu_kernel(
             return codes, scales
 
         last = CHUNKS - 1
-        hq0 = quantise_h(0, "hq0")
+        hq0 = quantise_h(0, "b_sc")
         y0_first = second_layer(0, hq0, 0, 2, "bg0_first", 0)
         y0_second = second_layer(0, hq0, 2, 2, "bg0_second", 1)
-        hq1 = quantise_h(1, "bg0_first")
         gate_block(0, y0_first, 0, 2)
         scatter(0, (0, 1))
+        hq1 = quantise_h(1, "hq1")
         y1 = second_layer(1, hq1, 0, CHUNKS, "bg1", 2)
         gate_block(0, y0_second, 2, 2)
         scatter(0, (2, 3))
-        b_scales.extend(gather_b_scales(1, "hq0"))
         gate_block(1, y1, 0, CHUNKS)
         scatter(1, range(CHUNKS))
         y2 = second_layer(2, quantise_h(2, "bg0_second"), 0, CHUNKS, "hq_sc0", 3)
-        y3 = second_layer(3, quantise_h(3, "bg0_first"), 0, CHUNKS, "bg1", 0)
-        gate_block(2, y2, 0, CHUNKS)
+        y3 = second_layer(3, quantise_h(3, "hq1"), 0, CHUNKS, "bg1", 0)
+        gate_block(2, y2, 0, last)
         w_bf0 = round_w(0)
         gate_block(3, y3, 0, last)
-        nc.scalar.activation(out=routed[last][:].indirect(tokens_of(slots_of((2,)))), in_=gated[2][:, last, 0:SLOTS], func=COPY)
         scatter(2, range(last))
         w_bf1 = round_w(1)
         wq = [quantise_w(0, w_bf0), quantise_w(1, w_bf1)]
 
-        gated_last = sbuf("w_bf1", [P, SLOTS], F32)
-        nc.vector.tensor_tensor(gated_last[:], y3[:, last, :], gate_all[:, slots_of((3,))], MULT)
-        nc.vector.tensor_copy(routed[last][:].indirect(tokens_of(slots_of((3,)))), gated_last[:])
+        gated_last = sbuf("w_bf1", [P, HALF_SLOTS], F32)
+        for b, y_ps in enumerate((y2, y3)):
+            nc.vector.tensor_tensor(gated_last[:, slots_of((b,))], y_ps[:, last, :], gate_all[:, slots_of((2 + b,))], MULT)
+        nc.vector.tensor_copy(routed[last][:].indirect(tokens_of(slots_of(groups[2]))), gated_last[:])
 
-        for c in (0, 3, 1, 2):
+        for c in (0, 1, 3, 2):
             base_ps = bank(4 + c, [P, T])
             for s in range(PASSES):
                 codes, scales = wq[s]
@@ -284,6 +288,6 @@ def tile_moe_dyl_relu_kernel(
             pieces = 2 if c == 2 else 1
             for piece in range(pieces):
                 tokens = slice(piece * T // pieces, (piece + 1) * T // pieces)
-                result = sbuf(f"result{c}_{piece}", [P, T // pieces], F32)
+                result = sbuf("w_bf1" if c == 1 else f"result{c}_{piece}", [P, T // pieces], F32)
                 nc.vector.tensor_tensor(result[:], base_ps[:, tokens], routed[c][:, tokens], ADD)
                 nc.sync.dma_start(out=out[c * P : (c + 1) * P, tokens], in_=result[:])

@@ -57,17 +57,12 @@ def tile_moe_dyl_relu_kernel(
     with ExitStack() as ctx:
         lists = ctx.enter_context(tc.tile_pool(name="lists", bufs=1))
         keep = ctx.enter_context(tc.tile_pool(name="keep", bufs=1))
-        shared = ctx.enter_context(tc.tile_pool(name="shared", bufs=1))
         psum = ctx.enter_context(tc.psum_pool(name="psum", bufs=1))
 
         def bank(number, shape):
             return psum.tile(shape, F32, name=f"bank{number}")
 
-        offsets = {"bg0_first": 0, "hq1": 0, "bg1": 512}
-
         def sbuf(name, shape, dtype):
-            if name in offsets:
-                return shared.tile(shape, dtype, name=name, offset=offsets[name], align_bytes=64)
             return keep.tile(shape, dtype, name=name, align_bytes=64)
 
         token_list = lists.tile([P, T // 16], U16, name="token_list")
@@ -81,7 +76,7 @@ def tile_moe_dyl_relu_kernel(
         bw = sbuf("bw", [P, E * N], I32)
         b_sc = sbuf("b_sc", [P, E * N], U8)
         w_raw = [sbuf(f"w_raw{s}", [P, 4, N], F32) for s in range(PASSES)]
-        gate_rows = sbuf("gate_rows", [P, SLOTS], F32)
+        gate_all = sbuf("gate_all", [P, T], F32)
         ident = sbuf("ident", [P, P], F32)
 
         nc.gpsimd.memset(xs[:].bitcast(I32), 0)
@@ -89,7 +84,6 @@ def tile_moe_dyl_relu_kernel(
         nc.vector.memset(a_sc[:].bitcast(I32), 0)
         for s in range(PASSES):
             nc.vector.memset(xw[s][:, T:TOKEN_WINDOW], 0)
-        nc.gpsimd.memset(gate_rows[:], 0.0)
         make_identity(nc, ident[:])
 
         def load_w(s):
@@ -114,12 +108,12 @@ def tile_moe_dyl_relu_kernel(
         load_scales(nc, xs, x_scales, T)
         nc.sync.dma_start(out=aw[0][:], in_=words_of(wa_words[0]))
         nc.sync.dma_start(a_list[:], offs2)
-        nc.sync.dma_start(out=gate_rows[0:B, :], in_=gate[0].rearrange("(m j) -> m j", m=B))
         load_all(a_rows)
         nc.sync.dma_start(out=aw[1][:], in_=words_of(wa_words[1]))
         nc.sync.dma_start(b_list[:], offs3)
         load_all(b_rows)
         nc.sync.dma_start(out=bw[:], in_=words_of(wb_words[0]))
+        nc.sync.dma_start(out=gate_all[:], in_=gate)
         for s in range(PASSES):
             load_w(s)
 
@@ -132,16 +126,6 @@ def tile_moe_dyl_relu_kernel(
             nc.vector.tensor_copy(xg[s][:], xw[s][:].bitcast(U32).indirect(token_list[:]))
         xg_sc = sbuf("xg_sc", [P, T], U8)
         nc.vector.tensor_copy(xg_sc[:], xs[:].indirect(token_list[:]))
-        gate_ps = bank(2, [P, P])
-        nc.tensor.transpose(gate_ps[:], gate_rows[:], ident[:])
-        gate_col = sbuf("gate_col", [P, B], F32)
-        nc.scalar.copy(out=gate_col[:], in_=gate_ps[:, 0:B])
-        spread_ps = bank(3, [P, B, SLOTS])
-        for m in range(B):
-            nc.tensor.transpose(spread_ps[:, m, :], gate_col[:, m : m + 1].to_broadcast([P, P]), ident[:])
-        gate_all = sbuf("gate_all", [P, T], F32)
-        nc.scalar.copy(out=gate_all[:], in_=spread_ps[:].rearrange("p m j -> p (m j)"))
-
         ag0 = [sbuf(f"ag0_{hf}", [P, half_cols], U32) for hf in range(HALVES)]
         for hf in range(HALVES):
             nc.vector.tensor_copy(ag0[hf][:], aw[0][:].bitcast(U32).indirect(a_list[:, half_list[hf]]))
@@ -177,61 +161,52 @@ def tile_moe_dyl_relu_kernel(
                 )
             h_pairs.append(sbuf(f"h_pairs{m}", [P, 2, P, 2], BF16))
             nc.scalar.activation(out=h_pairs[m][:], in_=h_ps[:].rearrange("j (p u e) -> j u p e", u=2, e=2), func=RELU)
-        h_words = []
+        h_late = sbuf("h_late", [P, HALF_BLOCKS, SLOTS, 2], F32)
+        h_words = [sbuf("ag1_3", [P, SLOTS, 2], F32)[:], sbuf("h_words1", [P, SLOTS, 2], F32)[:], h_late[:, 0], h_late[:, 1]]
         for m in range(B):
             turned = bank(4 + m, [P, 2, SLOTS])
             pairs = h_pairs[m][:].rearrange("j u p e -> j (u p e)").bitcast(F32)
             for u in range(2):
                 nc.tensor.transpose(turned[:, u, :], pairs[:, u * P : (u + 1) * P], ident[:])
-            h_words.append(sbuf("ag1_3" if m == 0 else f"h_words{m}", [P, SLOTS, 2], F32))
-            nc.scalar.copy(out=h_words[m][:], in_=turned[:].rearrange("p u j -> p j u"))
+            nc.scalar.copy(out=h_words[m], in_=turned[:].rearrange("p u j -> p j u"))
 
-        groups = ((0,), (1,), (2, 3))
-
-        def quantise_h(m, name):
-            codes = sbuf(name, [P, SLOTS], U32)
-            scales = sbuf(f"hq_sc{m}", [P, SLOTS], U8)
-            nc.vector.quantize_mx(
-                out=codes[:].bitcast(FP8X4), scales=scales[:], in_=h_words[m][:].rearrange("p j u -> p (j u)").bitcast(BF16)
-            )
+        def quantise_h(words, name):
+            slots = words.shape[1] // 2
+            codes = sbuf(name, [P, slots], U32)
+            scales = sbuf(f"{name}_h_scales", [P, slots], U8)
+            nc.vector.quantize_mx(out=codes[:].bitcast(FP8X4), scales=scales[:], in_=words.bitcast(BF16))
             return codes, scales
 
-        def second_layer(m, hq, first, count, name, number):
-            bg = sbuf(name, [P, count * P], U32)
-            start = (m * N + first * P) // 16
-            nc.vector.tensor_copy(bg[:], bw[:].bitcast(U32).indirect(b_list[:, start : start + count * P // 16]))
-            y_ps = bank(number, [P, count, SLOTS])
-            for i in range(count):
-                nc.tensor.matmul_mx(
-                    out=y_ps[:, i, :],
-                    lhsT=bg[:, i * P : (i + 1) * P].bitcast(FP8X4),
-                    lhsT_scale=b_scales[m][B_ROW:P, (first + i) * P : (first + i + 1) * P],
-                    rhs=hq[0][:].bitcast(FP8X4),
-                    rhs_scale=hq[1][:],
-                    start=True,
-                    stop=True,
-                )
-            return y_ps
+        def gather_b(first_col, cols, name):
+            words = sbuf(name, [P, cols], U32)
+            nc.vector.tensor_copy(words[:], bw[:].bitcast(U32).indirect(b_list[:, first_col // 16 : (first_col + cols) // 16]))
+            return words
 
-        def slots_of(blocks):
+        def second_layer(target, m, c, words, hq, slots):
+            nc.tensor.matmul_mx(
+                out=target,
+                lhsT=words.bitcast(FP8X4),
+                lhsT_scale=b_scales[m][B_ROW:P, c * P : (c + 1) * P],
+                rhs=hq[0][:, slots].bitcast(FP8X4),
+                rhs_scale=hq[1][:, slots],
+                start=True,
+                stop=True,
+            )
+
+        def slots_of(*blocks):
             return slice(blocks[0] * SLOTS, (blocks[-1] + 1) * SLOTS)
 
         def tokens_of(slots):
             return token_list[:, slots.start // 16 : slots.stop // 16]
 
-        gated = [sbuf(f"gated{g}", [P, CHUNKS, len(blocks) * SLOTS], F32) for g, blocks in enumerate(groups)]
-
-        def gate_block(m, y_ps, first, count):
-            g = min(m, len(groups) - 1)
-            gates = gate_all[:, slots_of((m,))].unsqueeze(1).to_broadcast([P, count, SLOTS])
-            target = gated[g][:, first : first + count, slots_of((m - groups[g][0],))]
-            nc.vector.tensor_tensor(target, y_ps[:, 0:count], gates, MULT)
-
         routed = [sbuf(f"routed{c}", [P, T], F32) for c in range(CHUNKS)]
 
-        def scatter(g, chunks):
-            for c in chunks:
-                nc.scalar.activation(out=routed[c][:].indirect(tokens_of(slots_of(groups[g]))), in_=gated[g][:, c, :], func=COPY)
+        def gate_and_scatter(name, y_ps, first_chunk, slots):
+            shape = list(y_ps.shape)
+            gated = sbuf(name, shape, F32)
+            nc.vector.tensor_tensor(gated[:], y_ps, gate_all[:, slots].unsqueeze(1).to_broadcast(shape), MULT)
+            for i in range(shape[1]):
+                nc.scalar.activation(out=routed[first_chunk + i][:].indirect(tokens_of(slots)), in_=gated[:, i, :], func=COPY)
 
         def round_w(s):
             w_bf = sbuf(f"w_bf{s}", [P, N, 4], BF16)
@@ -246,31 +221,39 @@ def tile_moe_dyl_relu_kernel(
             nc.vector.quantize_mx(out=codes[:].bitcast(FP8X4), scales=scales[:], in_=w_bf[:].rearrange("p n j -> p (n j)"))
             return codes, scales
 
+        pair = CHUNKS // 2
         last = CHUNKS - 1
-        hq0 = quantise_h(0, "b_sc")
-        y0_first = second_layer(0, hq0, 0, 2, "bg0_first", 0)
-        y0_second = second_layer(0, hq0, 2, 2, "bg0_second", 1)
-        gate_block(0, y0_first, 0, 2)
-        scatter(0, (0, 1))
-        hq1 = quantise_h(1, "hq1")
-        y1 = second_layer(1, hq1, 0, CHUNKS, "bg1", 2)
-        gate_block(0, y0_second, 2, 2)
-        scatter(0, (2, 3))
-        gate_block(1, y1, 0, CHUNKS)
-        scatter(1, range(CHUNKS))
-        y2 = second_layer(2, quantise_h(2, "bg0_second"), 0, CHUNKS, "hq_sc0", 3)
-        y3 = second_layer(3, quantise_h(3, "hq1"), 0, CHUNKS, "bg1", 0)
-        gate_block(2, y2, 0, last)
+        hq0 = quantise_h(h_words[0].rearrange("p j u -> p (j u)"), "b_sc")
+        y0 = []
+        for hf in range(2):
+            words = gather_b(hf * pair * P, pair * P, f"bg0_{hf}")
+            y0.append(bank(hf, [P, pair, SLOTS]))
+            for i in range(pair):
+                second_layer(y0[hf][:, i, :], 0, hf * pair + i, words[:, i * P : (i + 1) * P], hq0, slots_of(0))
+        bg1 = gather_b(N, N, "bg1")
+        gate_and_scatter("gated0_0", y0[0][:], 0, slots_of(0))
+        hq1 = quantise_h(h_words[1].rearrange("p j u -> p (j u)"), "bg0_0")
+        y1 = bank(2, [P, CHUNKS, SLOTS])
+        for c in range(CHUNKS):
+            second_layer(y1[:, c, :], 1, c, bg1[:, c * P : (c + 1) * P], hq1, slots_of(0))
+        gate_and_scatter("gated0_1", y0[1][:], pair, slots_of(0))
+        hq_late = quantise_h(h_late[:].rearrange("p b j u -> p (b j u)"), "bg0_1")
+        bg_late = gather_b(HALF_BLOCKS * N, HALF_BLOCKS * N, "b_sc")
+        gate_and_scatter("gated1", y1[:], 0, slots_of(1))
+        y_late = [bank(number, [P, pair, HALF_SLOTS]) for number in (3, 0)]
+        for c in range(CHUNKS):
+            for b in range(HALF_BLOCKS):
+                words = bg_late[:, b * N + c * P : b * N + (c + 1) * P]
+                second_layer(y_late[c // pair][:, c % pair, slots_of(b)], HALF_BLOCKS + b, c, words, hq_late, slots_of(b))
         w_bf0 = round_w(0)
-        gate_block(3, y3, 0, last)
-        scatter(2, range(last))
+        gate_and_scatter("gated_late0", y_late[0][:], 0, slots_of(2, 3))
+        gate_and_scatter("gated_late1", y_late[1][:, 0:1, :], pair, slots_of(2, 3))
+        wq = [quantise_w(0, w_bf0)]
         w_bf1 = round_w(1)
-        wq = [quantise_w(0, w_bf0), quantise_w(1, w_bf1)]
-
-        gated_last = sbuf("w_bf1", [P, HALF_SLOTS], F32)
-        for b, y_ps in enumerate((y2, y3)):
-            nc.vector.tensor_tensor(gated_last[:, slots_of((b,))], y_ps[:, last, :], gate_all[:, slots_of((2 + b,))], MULT)
-        nc.vector.tensor_copy(routed[last][:].indirect(tokens_of(slots_of(groups[2]))), gated_last[:])
+        gated_last = sbuf("w_raw1", [P, HALF_SLOTS], F32)
+        nc.vector.tensor_tensor(gated_last[:], y_late[1][:, 1, :], gate_all[:, slots_of(2, 3)], MULT)
+        wq.append(quantise_w(1, w_bf1))
+        nc.vector.tensor_copy(routed[last][:].indirect(tokens_of(slots_of(2, 3))), gated_last[:])
 
         for c in (0, 1, 3, 2):
             base_ps = bank(4 + c, [P, T])
@@ -288,6 +271,6 @@ def tile_moe_dyl_relu_kernel(
             pieces = 2 if c == 2 else 1
             for piece in range(pieces):
                 tokens = slice(piece * T // pieces, (piece + 1) * T // pieces)
-                result = sbuf("w_bf1" if c == 1 else f"result{c}_{piece}", [P, T // pieces], F32)
+                result = sbuf(f"result{c}_{piece}", [P, T // pieces], F32)
                 nc.vector.tensor_tensor(result[:], base_ps[:, tokens], routed[c][:, tokens], ADD)
                 nc.sync.dma_start(out=out[c * P : (c + 1) * P, tokens], in_=result[:])

@@ -133,15 +133,15 @@ def tile_moe_dyl_relu_kernel(
         for hf in range(HALVES):
             nc.vector.tensor_copy(ag_sc[hf][:], a_sc[:].indirect(a_list[:, half_list[hf]]))
 
-        def gather_b_scales(hf, name):
-            scales = sbuf(name, [P, half_cols], U8)
-            nc.vector.tensor_copy(scales[:], b_sc[:].indirect(b_list[:, half_list[hf]]))
-            return [scales[:, b * N : (b + 1) * N] for b in range(HALF_BLOCKS)]
+        def gather_b_scales(first, count, name):
+            scales = sbuf(name, [P, count * N], U8)
+            nc.vector.tensor_copy(scales[:], b_sc[:].indirect(b_list[:, first * N // 16 : (first + count) * N // 16]))
+            return [scales[:, b * N : (b + 1) * N] for b in range(count)]
 
         ag1 = [sbuf(f"ag1_{m}", [P, H], U32) for m in range(B)]
         for m in range(B):
             nc.vector.tensor_copy(ag1[m][:], aw[1][:].bitcast(U32).indirect(a_list[:, block_list[m]]))
-        b_scales = gather_b_scales(0, "bg_sc0") + gather_b_scales(1, "bg_sc1")
+        b_scales = gather_b_scales(0, B - 1, "bg_sc")
 
         h_pairs = []
         for m in range(B):
@@ -170,10 +170,10 @@ def tile_moe_dyl_relu_kernel(
                 nc.tensor.transpose(turned[:, u, :], pairs[:, u * P : (u + 1) * P], ident[:])
             nc.scalar.copy(out=h_words[m], in_=turned[:].rearrange("p u j -> p j u"))
 
-        def quantise_h(words, name):
+        def quantise_h(words, name, scales_name):
             slots = words.shape[1] // 2
             codes = sbuf(name, [P, slots], U32)
-            scales = sbuf(f"{name}_h_scales", [P, slots], U8)
+            scales = sbuf(scales_name, [P, slots], U8)
             nc.vector.quantize_mx(out=codes[:].bitcast(FP8X4), scales=scales[:], in_=words.bitcast(BF16))
             return codes, scales
 
@@ -223,7 +223,7 @@ def tile_moe_dyl_relu_kernel(
 
         pair = CHUNKS // 2
         last = CHUNKS - 1
-        hq0 = quantise_h(h_words[0].rearrange("p j u -> p (j u)"), "b_sc")
+        hq0 = quantise_h(h_words[0].rearrange("p j u -> p (j u)"), "h_pairs2", "hq_sc0")
         y0 = []
         for hf in range(2):
             words = gather_b(hf * pair * P, pair * P, f"bg0_{hf}")
@@ -232,14 +232,15 @@ def tile_moe_dyl_relu_kernel(
                 second_layer(y0[hf][:, i, :], 0, hf * pair + i, words[:, i * P : (i + 1) * P], hq0, slots_of(0))
         bg1 = gather_b(N, N, "bg1")
         gate_and_scatter("gated0_0", y0[0][:], 0, slots_of(0))
-        hq1 = quantise_h(h_words[1].rearrange("p j u -> p (j u)"), "bg0_0")
+        hq1 = quantise_h(h_words[1].rearrange("p j u -> p (j u)"), "bg0_0", "hq_sc1")
         y1 = bank(2, [P, CHUNKS, SLOTS])
         for c in range(CHUNKS):
             second_layer(y1[:, c, :], 1, c, bg1[:, c * P : (c + 1) * P], hq1, slots_of(0))
         gate_and_scatter("gated0_1", y0[1][:], pair, slots_of(0))
-        hq_late = quantise_h(h_late[:].rearrange("p b j u -> p (b j u)"), "bg0_1")
-        bg_late = gather_b(HALF_BLOCKS * N, HALF_BLOCKS * N, "b_sc")
+        b_scales.extend(gather_b_scales(B - 1, 1, "hq_sc0"))
+        hq_late = quantise_h(h_late[:].rearrange("p b j u -> p (b j u)"), "bg0_1", "hq_sc_late")
         gate_and_scatter("gated1", y1[:], 0, slots_of(1))
+        bg_late = gather_b(HALF_BLOCKS * N, HALF_BLOCKS * N, "h_pairs2")
         y_late = [bank(number, [P, pair, HALF_SLOTS]) for number in (3, 0)]
         for c in range(CHUNKS):
             for b in range(HALF_BLOCKS):

@@ -71,7 +71,7 @@ def tile_moe_dyl_relu_kernel(
 
         xw = [sbuf(f"xw{s}", [P, TOKEN_WINDOW], I32) for s in range(PASSES)]
         xs = sbuf("xs", [P, TOKEN_WINDOW], U8)
-        aw = [sbuf(f"aw{s}", [P, E * H], I32) for s in range(PASSES)]
+        aw = [sbuf("aw0", [P, 2 * B * H], I32), sbuf("aw1", [P, E * H], I32)]
         a_sc = sbuf("a_sc", [P, E * H], U8)
         bw = sbuf("bw", [P, E * N], I32)
         b_sc = sbuf("b_sc", [P, E * N], U8)
@@ -82,8 +82,6 @@ def tile_moe_dyl_relu_kernel(
         nc.gpsimd.memset(xs[:].bitcast(I32), 0)
         nc.gpsimd.memset(b_sc[:].bitcast(I32), 0)
         nc.vector.memset(a_sc[:].bitcast(I32), 0)
-        for s in range(PASSES):
-            nc.vector.memset(xw[s][:, T:TOKEN_WINDOW], 0)
         make_identity(nc, ident[:])
 
         def load_w(s):
@@ -106,7 +104,7 @@ def tile_moe_dyl_relu_kernel(
         nc.sync.dma_start(token_list[:], offs)
         nc.sync.dma_start(out=xw[1][:, 0:T], in_=words_of(x_words[1]))
         load_scales(nc, xs, x_scales, T)
-        nc.sync.dma_start(out=aw[0][:], in_=words_of(wa_words[0]))
+        nc.sync.dma_start(out=aw[0][:, 0 : E * H], in_=words_of(wa_words[0]))
         nc.sync.dma_start(a_list[:], offs2)
         load_all(a_rows)
         nc.sync.dma_start(out=aw[1][:], in_=words_of(wa_words[1]))
@@ -126,9 +124,8 @@ def tile_moe_dyl_relu_kernel(
             nc.vector.tensor_copy(xg[s][:], xw[s][:].bitcast(U32).indirect(token_list[:]))
         xg_sc = sbuf("xg_sc", [P, T], U8)
         nc.vector.tensor_copy(xg_sc[:], xs[:].indirect(token_list[:]))
-        ag0 = [sbuf(f"ag0_{hf}", [P, half_cols], U32) for hf in range(HALVES)]
-        for hf in range(HALVES):
-            nc.vector.tensor_copy(ag0[hf][:], aw[0][:].bitcast(U32).indirect(a_list[:, half_list[hf]]))
+        ag0 = sbuf("ag0", [P, B * H], U32)
+        nc.vector.tensor_copy(ag0[:], aw[0][:].bitcast(U32).indirect(a_list[:]))
         ag_sc = [sbuf(f"ag_sc{hf}", [P, half_cols], U8) for hf in range(HALVES)]
         for hf in range(HALVES):
             nc.vector.tensor_copy(ag_sc[hf][:], a_sc[:].indirect(a_list[:, half_list[hf]]))
@@ -149,7 +146,7 @@ def tile_moe_dyl_relu_kernel(
             slots = slice(m * SLOTS, (m + 1) * SLOTS)
             cols = slice(b * H, (b + 1) * H)
             h_ps = bank(4 + m, [P, H])
-            for s, words in enumerate((ag0[hf][:, cols], ag1[m][:])):
+            for s, words in enumerate((ag0[:, m * H : (m + 1) * H], ag1[m][:])):
                 nc.tensor.matmul_mx(
                     out=h_ps[:],
                     lhsT=xg[s][:, slots].bitcast(FP8X4),
@@ -207,6 +204,7 @@ def tile_moe_dyl_relu_kernel(
             nc.vector.tensor_tensor(gated[:], y_ps, gate_all[:, slots].unsqueeze(1).to_broadcast(shape), MULT)
             for i in range(shape[1]):
                 nc.scalar.activation(out=routed[first_chunk + i][:].indirect(tokens_of(slots)), in_=gated[:, i, :], func=COPY)
+            return gated
 
         def round_w(s):
             w_bf = sbuf(f"w_bf{s}", [P, N, 4], BF16)
@@ -224,35 +222,36 @@ def tile_moe_dyl_relu_kernel(
         pair = CHUNKS // 2
         last = CHUNKS - 1
         hq0 = quantise_h(h_words[0].rearrange("p j u -> p (j u)"), "h_pairs2", "hq_sc0")
-        y0 = []
-        for hf in range(2):
+        y_first = bank(0, [P, pair, SLOTS])
+        y_early = bank(1, [P, pair, HALF_SLOTS])
+        y_rest = [bank(2 + c, [P, 1, (B - 1) * SLOTS]) for c in range(pair)]
+        for hf, target in enumerate((y_first[:], y_early[:, :, slots_of(0)])):
             words = gather_b(hf * pair * P, pair * P, f"bg0_{hf}")
-            y0.append(bank(hf, [P, pair, SLOTS]))
             for i in range(pair):
-                second_layer(y0[hf][:, i, :], 0, hf * pair + i, words[:, i * P : (i + 1) * P], hq0, slots_of(0))
+                second_layer(target[:, i, :], 0, hf * pair + i, words[:, i * P : (i + 1) * P], hq0, slots_of(0))
         bg1 = gather_b(N, N, "bg1")
-        gate_and_scatter("gated0_0", y0[0][:], 0, slots_of(0))
+        g0 = gate_and_scatter("gated_first", y_first[:], 0, slots_of(0))
         hq1 = quantise_h(h_words[1].rearrange("p j u -> p (j u)"), "bg0_0", "hq_sc1")
-        y1 = bank(2, [P, CHUNKS, SLOTS])
-        for c in range(CHUNKS):
-            second_layer(y1[:, c, :], 1, c, bg1[:, c * P : (c + 1) * P], hq1, slots_of(0))
-        gate_and_scatter("gated0_1", y0[1][:], pair, slots_of(0))
+        for c in (2, 3, 0, 1):
+            target = y_early[:, c - pair, slots_of(1)] if c >= pair else y_rest[c][:, 0, slots_of(0)]
+            second_layer(target, 1, c, bg1[:, c * P : (c + 1) * P], hq1, slots_of(0))
         b_scales.extend(gather_b_scales(B - 1, 1, "hq_sc0"))
+        g1 = gate_and_scatter("gated_early", y_early[:], pair, slots_of(0, 1))
         hq_late = quantise_h(h_late[:].rearrange("p b j u -> p (b j u)"), "bg0_1", "hq_sc_late")
-        gate_and_scatter("gated1", y1[:], 0, slots_of(1))
-        bg_late = gather_b(HALF_BLOCKS * N, HALF_BLOCKS * N, "h_pairs2")
-        y_late = [bank(number, [P, pair, HALF_SLOTS]) for number in (3, 0)]
+        bg_late = gather_b(HALF_BLOCKS * N, HALF_BLOCKS * N, "bg1")
+        y_late = bank(0, [P, pair, HALF_SLOTS])
         for c in range(CHUNKS):
             for b in range(HALF_BLOCKS):
                 words = bg_late[:, b * N + c * P : b * N + (c + 1) * P]
-                second_layer(y_late[c // pair][:, c % pair, slots_of(b)], HALF_BLOCKS + b, c, words, hq_late, slots_of(b))
+                target = y_late[:, c - pair, slots_of(b)] if c >= pair else y_rest[c][:, 0, slots_of(1 + b)]
+                second_layer(target, HALF_BLOCKS + b, c, words, hq_late, slots_of(b))
         w_bf0 = round_w(0)
-        gate_and_scatter("gated_late0", y_late[0][:], 0, slots_of(2, 3))
-        gate_and_scatter("gated_late1", y_late[1][:, 0:1, :], pair, slots_of(2, 3))
+        g_rest = [gate_and_scatter(f"gated_rest{c}", y_rest[c][:], c, slots_of(1, 3)) for c in range(pair)]
+        gate_and_scatter("gated_late", y_late[:, 0:1, :], pair, slots_of(2, 3))
         wq = [quantise_w(0, w_bf0)]
         w_bf1 = round_w(1)
         gated_last = sbuf("w_raw1", [P, HALF_SLOTS], F32)
-        nc.vector.tensor_tensor(gated_last[:], y_late[1][:, 1, :], gate_all[:, slots_of(2, 3)], MULT)
+        nc.vector.tensor_tensor(gated_last[:], y_late[:, 1, :], gate_all[:, slots_of(2, 3)], MULT)
         wq.append(quantise_w(1, w_bf1))
         nc.vector.tensor_copy(routed[last][:].indirect(tokens_of(slots_of(2, 3))), gated_last[:])
 

@@ -158,14 +158,16 @@ def tile_moe_dyl_relu_kernel(
                 )
             h_pairs.append(sbuf(f"h_pairs{m}", [P, 2, P, 2], BF16))
             nc.scalar.activation(out=h_pairs[m][:], in_=h_ps[:].rearrange("j (p u e) -> j u p e", u=2, e=2), func=RELU)
-        h_late = sbuf("h_late", [P, HALF_BLOCKS, SLOTS, 2], F32)
-        h_words = [sbuf("ag1_3", [P, SLOTS, 2], F32)[:], sbuf("h_words1", [P, SLOTS, 2], F32)[:], h_late[:, 0], h_late[:, 1]]
-        for m in range(B):
-            turned = bank(4 + m, [P, 2, SLOTS])
-            pairs = h_pairs[m][:].rearrange("j u p e -> j (u p e)").bitcast(F32)
-            for u in range(2):
-                nc.tensor.transpose(turned[:, u, :], pairs[:, u * P : (u + 1) * P], ident[:])
-            nc.scalar.copy(out=h_words[m], in_=turned[:].rearrange("p u j -> p j u"))
+        h_first = sbuf("ag1_3", [P, 1, SLOTS, 2], F32)
+        h_rest = sbuf("h_rest", [P, B - 1, SLOTS, 2], F32)
+        for first, target in ((0, h_first[:]), (1, h_rest[:, 0:2]), (3, h_rest[:, 2:3])):
+            count = target.shape[1]
+            turned = bank(4 + first, [P, count, 2, SLOTS])
+            for b in range(count):
+                pairs = h_pairs[first + b][:].rearrange("j u p e -> j (u p e)").bitcast(F32)
+                for u in range(2):
+                    nc.tensor.transpose(turned[:, b, u, :], pairs[:, u * P : (u + 1) * P], ident[:])
+            nc.scalar.copy(out=target, in_=turned[:].rearrange("p b u j -> p b j u"))
 
         def quantise_h(words, name, scales_name):
             slots = words.shape[1] // 2
@@ -221,24 +223,25 @@ def tile_moe_dyl_relu_kernel(
 
         pair = CHUNKS // 2
         last = CHUNKS - 1
-        hq0 = quantise_h(h_words[0].rearrange("p j u -> p (j u)"), "h_pairs2", "hq_sc0")
+        hq0 = quantise_h(h_first[:].rearrange("p b j u -> p (b j u)"), "h_pairs2", "hq_sc0")
         y_first = bank(0, [P, pair, SLOTS])
         y_early = bank(1, [P, pair, HALF_SLOTS])
         y_rest = [bank(2 + c, [P, 1, (B - 1) * SLOTS]) for c in range(pair)]
-        for hf, target in enumerate((y_first[:], y_early[:, :, slots_of(0)])):
-            words = gather_b(hf * pair * P, pair * P, f"bg0_{hf}")
-            for i in range(pair):
-                second_layer(target[:, i, :], 0, hf * pair + i, words[:, i * P : (i + 1) * P], hq0, slots_of(0))
-        bg1 = gather_b(N, N, "bg1")
+        bg_first = gather_b(0, pair * P, "bg0_0")
+        bg_early = gather_b(pair * P, N + pair * P, "bg0_1")
+        for c in range(CHUNKS):
+            words = bg_first[:, c * P : (c + 1) * P] if c < pair else bg_early[:, (c - pair) * P : (c - pair + 1) * P]
+            second_layer(y_first[:, c, :] if c < pair else y_early[:, c - pair, slots_of(0)], 0, c, words, hq0, slots_of(0))
+        bg1 = bg_early[:, pair * P :]
         g0 = gate_and_scatter("gated_first", y_first[:], 0, slots_of(0))
-        hq1 = quantise_h(h_words[1].rearrange("p j u -> p (j u)"), "bg0_0", "hq_sc1")
+        hq1 = quantise_h(h_rest[:, 0].rearrange("p j u -> p (j u)"), "bg0_0", "hq_sc1")
         for c in (2, 3, 0, 1):
             target = y_early[:, c - pair, slots_of(1)] if c >= pair else y_rest[c][:, 0, slots_of(0)]
             second_layer(target, 1, c, bg1[:, c * P : (c + 1) * P], hq1, slots_of(0))
         b_scales.extend(gather_b_scales(B - 1, 1, "hq_sc0"))
         g1 = gate_and_scatter("gated_early", y_early[:], pair, slots_of(0, 1))
-        hq_late = quantise_h(h_late[:].rearrange("p b j u -> p (b j u)"), "bg0_1", "hq_sc_late")
-        bg_late = gather_b(HALF_BLOCKS * N, HALF_BLOCKS * N, "bg1")
+        hq_late = quantise_h(h_rest[:, 1:].rearrange("p b j u -> p (b j u)"), "bg0_1", "hq_sc_late")
+        bg_late = gather_b(HALF_BLOCKS * N, HALF_BLOCKS * N, "bg0_0")
         y_late = bank(0, [P, pair, HALF_SLOTS])
         for c in range(CHUNKS):
             for b in range(HALF_BLOCKS):

from contextlib import ExitStack

import concourse.mybir as mybir
from concourse.masks import make_identity

K, T, E, B, H, N = 1024, 512, 6, 4, 512, 512
FLOPS = 2 * K * N * T + 2 * K * H * T + 2 * H * N * T

F32 = mybir.dt.float32
BF16 = mybir.dt.bfloat16
I32 = mybir.dt.int32
U32 = mybir.dt.uint32
U16 = mybir.dt.uint16
U8 = mybir.dt.uint8
FP8X4 = mybir.dt.float8_e4m3fn_x4
RELU = mybir.ActivationFunctionType.Relu
COPY = mybir.ActivationFunctionType.Copy
ADD = mybir.AluOpType.add
MULT = mybir.AluOpType.mult

P = 128
PASSES = K // 512
SLOTS = 128
HALVES = 2
HALF_BLOCKS = B // HALVES
HALF_SLOTS = HALF_BLOCKS * SLOTS
TOKEN_WINDOW = 704
CHUNKS = N // P
B_ROW = 8


def words_of(dram_pass):
    return dram_pass.rearrange("p c d -> p (c d)").bitcast(I32)


def load_scale_rows(nc, tile, first_row, dram_scales):
    for r in range(4):
        for s in range(dram_scales.shape[0]):
            nc.sync.dma_start(
                out=tile[first_row + 4 * s + r : P : 32, :].bitcast(I32), in_=dram_scales[s, r:16:4, :].bitcast(I32)
            )


def load_scales(nc, tile, dram_scales, width):
    passes = dram_scales.shape[0]
    for q in range(4):
        nc.sync.dma_start(
            out=tile[32 * q : 32 * q + 4 * passes, 0:width].bitcast(I32),
            in_=dram_scales[:, 4 * q : 4 * q + 4, :].bitcast(I32),
        )


def tile_moe_dyl_relu_kernel(
    tc, x_words, x_scales, w, wa_words, wa_scales, wb_words, wb_scales, gate, offs, offs2, offs3, out
):
    nc = tc.nc
    with ExitStack() as ctx:
        lists = ctx.enter_context(tc.tile_pool(name="lists", bufs=1))
        keep = ctx.enter_context(tc.tile_pool(name="keep", bufs=1))
        psum = ctx.enter_context(tc.psum_pool(name="psum", bufs=1))

        def bank(number, shape):
            return psum.tile(shape, F32, name=f"bank{number}")

        def sbuf(name, shape, dtype):
            return keep.tile(shape, dtype, name=name, align_bytes=64)

        token_list = lists.tile([P, T // 16], U16, name="token_list")
        a_list = lists.tile([P, B * H // 16], U16, name="a_list")
        b_list = lists.tile([P, B * N // 16], U16, name="b_list")

        xw = [sbuf(f"xw{s}", [P, TOKEN_WINDOW], I32) for s in range(PASSES)]
        xs = sbuf("xs", [P, TOKEN_WINDOW], U8)
        aw = [sbuf("aw0", [P, 2 * B * H], I32), sbuf("aw1", [P, E * H], I32)]
        a_sc = sbuf("a_sc", [P, E * H], U8)
        bw = sbuf("bw", [P, E * N], I32)
        b_sc = sbuf("b_sc", [P, E * N], U8)
        w_raw = [sbuf(f"w_raw{s}", [P, 4, N], F32) for s in range(PASSES)]
        gate_all = sbuf("gate_all", [P, T], F32)
        ident = sbuf("ident", [P, P], F32)

        nc.gpsimd.memset(xs[:].bitcast(I32), 0)
        nc.gpsimd.memset(b_sc[:].bitcast(I32), 0)
        nc.vector.memset(a_sc[:].bitcast(I32), 0)
        make_identity(nc, ident[:])

        def load_w(s):
            nc.sync.dma_start(out=w_raw[s][:], in_=w[512 * s : 512 * (s + 1), :].rearrange("(p j) n -> p j n", j=4))

        def scale_row_loads(tile, first_row, dram_scales):
            return [
                (tile[first_row + 4 * s + r : P : 32, :].bitcast(I32), dram_scales[s, r:16:4, :].bitcast(I32))
                for r in range(4)
                for s in range(dram_scales.shape[0])
            ]

        def load_all(loads):
            for target, source in loads:
                nc.sync.dma_start(out=target, in_=source)

        a_rows = scale_row_loads(a_sc, 0, wa_scales)
        b_rows = scale_row_loads(b_sc, B_ROW, wb_scales)
        nc.sync.dma_start(out=xw[0][:, 0:T], in_=words_of(x_words[0]))
        nc.sync.dma_start(token_list[:], offs)
        nc.sync.dma_start(out=xw[1][:, 0:T], in_=words_of(x_words[1]))
        load_scales(nc, xs, x_scales, T)
        nc.sync.dma_start(out=aw[0][:, 0 : E * H], in_=words_of(wa_words[0]))
        nc.sync.dma_start(a_list[:], offs2)
        load_all(a_rows)
        nc.sync.dma_start(out=aw[1][:], in_=words_of(wa_words[1]))
        nc.sync.dma_start(b_list[:], offs3)
        load_all(b_rows)
        nc.sync.dma_start(out=bw[:], in_=words_of(wb_words[0]))
        nc.sync.dma_start(out=gate_all[:], in_=gate)
        for s in range(PASSES):
            load_w(s)

        half_cols = HALF_BLOCKS * H
        half_list = [slice(hf * half_cols // 16, (hf + 1) * half_cols // 16) for hf in range(HALVES)]
        block_list = [slice(m * H // 16, (m + 1) * H // 16) for m in range(B)]

        xg = [sbuf(f"xg{s}", [P, T], U32) for s in range(PASSES)]
        for s in range(PASSES):
            nc.vector.tensor_copy(xg[s][:], xw[s][:].bitcast(U32).indirect(token_list[:]))
        xg_sc = sbuf("xg_sc", [P, T], U8)
        nc.vector.tensor_copy(xg_sc[:], xs[:].indirect(token_list[:]))
        ag0 = sbuf("ag0", [P, B * H], U32)
        nc.vector.tensor_copy(ag0[:], aw[0][:].bitcast(U32).indirect(a_list[:]))
        ag_sc = [sbuf(f"ag_sc{hf}", [P, half_cols], U8) for hf in range(HALVES)]
        for hf in range(HALVES):
            nc.vector.tensor_copy(ag_sc[hf][:], a_sc[:].indirect(a_list[:, half_list[hf]]))

        def gather_b_scales(first, count, name):
            scales = sbuf(name, [P, count * N], U8)
            nc.vector.tensor_copy(scales[:], b_sc[:].indirect(b_list[:, first * N // 16 : (first + count) * N // 16]))
            return [scales[:, b * N : (b + 1) * N] for b in range(count)]

        ag1 = [sbuf(f"ag1_{m}", [P, H], U32) for m in range(B)]
        for m in range(B):
            nc.vector.tensor_copy(ag1[m][:], aw[1][:].bitcast(U32).indirect(a_list[:, block_list[m]]))
        b_scales = gather_b_scales(0, B - 1, "bg_sc")

        h_pairs = []
        for m in range(B):
            hf, b = divmod(m, HALF_BLOCKS)
            slots = slice(m * SLOTS, (m + 1) * SLOTS)
            cols = slice(b * H, (b + 1) * H)
            h_ps = bank(4 + m, [P, H])
            for s, words in enumerate((ag0[:, m * H : (m + 1) * H], ag1[m][:])):
                nc.tensor.matmul_mx(
                    out=h_ps[:],
                    lhsT=xg[s][:, slots].bitcast(FP8X4),
                    lhsT_scale=xg_sc[4 * s : P, slots],
                    rhs=words.bitcast(FP8X4),
                    rhs_scale=ag_sc[hf][4 * s : P, cols],
                    start=(s == 0),
                    stop=(s == PASSES - 1),
                )
            h_pairs.append(sbuf(f"h_pairs{m}", [P, 2, P, 2], BF16))
            nc.scalar.activation(out=h_pairs[m][:], in_=h_ps[:].rearrange("j (p u e) -> j u p e", u=2, e=2), func=RELU)
        h_first = sbuf("ag1_3", [P, 1, SLOTS, 2], F32)
        h_rest = sbuf("h_rest", [P, B - 1, SLOTS, 2], F32)
        for first, target in ((0, h_first[:]), (1, h_rest[:, 0:2]), (3, h_rest[:, 2:3])):
            count = target.shape[1]
            turned = bank(4 + first, [P, count, 2, SLOTS])
            for b in range(count):
                pairs = h_pairs[first + b][:].rearrange("j u p e -> j (u p e)").bitcast(F32)
                for u in range(2):
                    nc.tensor.transpose(turned[:, b, u, :], pairs[:, u * P : (u + 1) * P], ident[:])
            nc.scalar.copy(out=target, in_=turned[:].rearrange("p b u j -> p b j u"))

        def quantise_h(words, name, scales_name):
            slots = words.shape[1] // 2
            codes = sbuf(name, [P, slots], U32)
            scales = sbuf(scales_name, [P, slots], U8)
            nc.vector.quantize_mx(out=codes[:].bitcast(FP8X4), scales=scales[:], in_=words.bitcast(BF16))
            return codes, scales

        def gather_b(first_col, cols, name):
            words = sbuf(name, [P, cols], U32)
            nc.vector.tensor_copy(words[:], bw[:].bitcast(U32).indirect(b_list[:, first_col // 16 : (first_col + cols) // 16]))
            return words

        def second_layer(target, m, c, words, hq, slots):
            nc.tensor.matmul_mx(
                out=target,
                lhsT=words.bitcast(FP8X4),
                lhsT_scale=b_scales[m][B_ROW:P, c * P : (c + 1) * P],
                rhs=hq[0][:, slots].bitcast(FP8X4),
                rhs_scale=hq[1][:, slots],
                start=True,
                stop=True,
            )

        def slots_of(*blocks):
            return slice(blocks[0] * SLOTS, (blocks[-1] + 1) * SLOTS)

        def tokens_of(slots):
            return token_list[:, slots.start // 16 : slots.stop // 16]

        routed = [sbuf(f"routed{c}", [P, T], F32) for c in range(CHUNKS)]

        def gate_and_scatter(name, y_ps, first_chunk, slots):
            shape = list(y_ps.shape)
            gated = sbuf(name, shape, F32)
            nc.vector.tensor_tensor(gated[:], y_ps, gate_all[:, slots].unsqueeze(1).to_broadcast(shape), MULT)
            for i in range(shape[1]):
                nc.scalar.activation(out=routed[first_chunk + i][:].indirect(tokens_of(slots)), in_=gated[:, i, :], func=COPY)
            return gated

        def round_w(s):
            w_bf = sbuf(f"w_bf{s}", [P, N, 4], BF16)
            nc.vector.tensor_copy(
                w_bf[:].rearrange("p (c i) j -> p c j i", i=4), w_raw[s][:].rearrange("p j (c i) -> p c j i", i=4)
            )
            return w_bf

        def quantise_w(s, w_bf):
            codes = sbuf(f"wq{s}", [P, N], U32)
            scales = sbuf(f"wq_sc{s}", [P, N], U8)
            nc.vector.quantize_mx(out=codes[:].bitcast(FP8X4), scales=scales[:], in_=w_bf[:].rearrange("p n j -> p (n j)"))
            return codes, scales

        pair = CHUNKS // 2
        last = CHUNKS - 1
        hq0 = quantise_h(h_first[:].rearrange("p b j u -> p (b j u)"), "h_pairs2", "hq_sc0")
        y_first = bank(0, [P, pair, SLOTS])
        y_early = bank(1, [P, pair, HALF_SLOTS])
        y_rest = [bank(2 + c, [P, 1, (B - 1) * SLOTS]) for c in range(pair)]
        bg_first = gather_b(0, pair * P, "bg0_0")
        bg_early = gather_b(pair * P, N + pair * P, "bg0_1")
        for c in range(CHUNKS):
            words = bg_first[:, c * P : (c + 1) * P] if c < pair else bg_early[:, (c - pair) * P : (c - pair + 1) * P]
            second_layer(y_first[:, c, :] if c < pair else y_early[:, c - pair, slots_of(0)], 0, c, words, hq0, slots_of(0))
        bg1 = bg_early[:, pair * P :]
        g0 = gate_and_scatter("gated_first", y_first[:], 0, slots_of(0))
        hq1 = quantise_h(h_rest[:, 0].rearrange("p j u -> p (j u)"), "bg0_0", "hq_sc1")
        for c in (2, 3, 0, 1):
            target = y_early[:, c - pair, slots_of(1)] if c >= pair else y_rest[c][:, 0, slots_of(0)]
            second_layer(target, 1, c, bg1[:, c * P : (c + 1) * P], hq1, slots_of(0))
        b_scales.extend(gather_b_scales(B - 1, 1, "hq_sc0"))
        g1 = gate_and_scatter("gated_early", y_early[:], pair, slots_of(0, 1))
        hq_late = quantise_h(h_rest[:, 1:].rearrange("p b j u -> p (b j u)"), "bg0_1", "hq_sc_late")
        bg_late = gather_b(HALF_BLOCKS * N, HALF_BLOCKS * N, "bg0_0")
        y_late = bank(0, [P, pair, HALF_SLOTS])
        for c in range(CHUNKS):
            for b in range(HALF_BLOCKS):
                words = bg_late[:, b * N + c * P : b * N + (c + 1) * P]
                target = y_late[:, c - pair, slots_of(b)] if c >= pair else y_rest[c][:, 0, slots_of(1 + b)]
                second_layer(target, HALF_BLOCKS + b, c, words, hq_late, slots_of(b))
        w_bf0 = round_w(0)
        g_rest = [gate_and_scatter(f"gated_rest{c}", y_rest[c][:], c, slots_of(1, 3)) for c in range(pair)]
        gate_and_scatter("gated_late", y_late[:, 0:1, :], pair, slots_of(2, 3))
        wq = [quantise_w(0, w_bf0)]
        w_bf1 = round_w(1)
        gated_last = sbuf("w_raw1", [P, HALF_SLOTS], F32)
        nc.vector.tensor_tensor(gated_last[:], y_late[:, 1, :], gate_all[:, slots_of(2, 3)], MULT)
        wq.append(quantise_w(1, w_bf1))
        nc.vector.tensor_copy(routed[last][:].indirect(tokens_of(slots_of(2, 3))), gated_last[:])

        for c in (0, 1, 3, 2):
            base_ps = bank(4 + c, [P, T])
            for s in range(PASSES):
                codes, scales = wq[s]
                nc.tensor.matmul_mx(
                    out=base_ps[:],
                    lhsT=codes[:, c * P : (c + 1) * P].bitcast(FP8X4),
                    lhsT_scale=scales[:, c * P : (c + 1) * P],
                    rhs=xw[s][:, 0:T].bitcast(FP8X4),
                    rhs_scale=xs[4 * s : P, 0:T],
                    start=(s == 0),
                    stop=(s == PASSES - 1),
                )
            pieces = 2 if c == 2 else 1
            for piece in range(pieces):
                tokens = slice(piece * T // pieces, (piece + 1) * T // pieces)
                result = sbuf(f"result{c}_{piece}", [P, T // pieces], F32)
                nc.vector.tensor_tensor(result[:], base_ps[:, tokens], routed[c][:, tokens], ADD)
                nc.sync.dma_start(out=out[c * P : (c + 1) * P, tokens], in_=result[:])
